import numpy as np
import ml_dtypes


def mxq(x, axis, fmt="e4m3"):
    dtype, down = {"e4m3": (ml_dtypes.float8_e4m3fn, 7), "e5m2": (ml_dtypes.float8_e5m2, 14)}[fmt]
    v = np.moveaxis(np.asarray(x, np.float32).astype(ml_dtypes.bfloat16).astype(np.float64), axis, -1)
    blocks = v.reshape(v.shape[:-1] + (-1, 32))
    amax = np.abs(blocks).max(-1, keepdims=True)
    byte = np.maximum(np.where(amax > 0, np.frexp(amax)[1] - 1 + 127, 0) - down, 1)
    scale = np.exp2(byte - 127.0)
    codes = (blocks / scale).astype(np.float32).astype(dtype).astype(np.float64)
    return np.moveaxis((codes * scale).reshape(v.shape), -1, axis)


WIDE = False


def mx_kscale(k):
    if not WIDE:
        return np.ones(k)
    levels = np.array([10, -10, 5, -5, 0])
    if k % 512:
        return np.exp2(np.random.permutation(np.resize(levels, k // 32))).repeat(32)
    a = np.empty((k // 512, 16))
    for p in range(k // 512):
        a[p, :8] = np.random.permutation(np.resize(levels, 8))
        for g in range(8):
            far = levels[np.abs(levels - a[p, g]) >= 10]
            a[p, g + 8] = far[np.random.randint(len(far))]
    return np.exp2(a.ravel()).repeat(32)


def f64(x):
    return np.asarray(x).astype(np.float64)


def striped8(idx):
    return np.concatenate([v.reshape(-1, 16).T for v in idx]).astype(np.uint16)


def unstriped8(offs):
    return np.stack([offs[16 * g:16 * g + 16].T.reshape(-1) for g in range(8)]).astype(np.int64)


E2M1 = np.array([0.0, 0.5, 1.0, 1.5, 2.0, 3.0, 4.0, 6.0, -0.0, -0.5, -1.0, -1.5, -2.0, -3.0, -4.0, -6.0])


def pack_weight(w, fmt):
    k, n = w.shape
    w = f64(np.asarray(w, np.float32).astype(ml_dtypes.bfloat16)).reshape(k // 32, 32, n)
    amax = np.abs(w).max(1)
    if fmt == "e4m3":
        byte = np.frexp(amax)[1] - 1 + 127 - 7
    else:
        mant, ex = np.frexp(amax / 6.0)
        byte = np.where(mant > 0.5, ex, ex - 1) + 127
    byte = np.clip(np.where(amax > 0, byte, 1), 1, 254)
    scaled = (w * np.exp2(127.0 - byte)[:, None, :]).reshape(k, n).astype(np.float32)
    by_word = np.ascontiguousarray(scaled.reshape(k // 512, 128, 4, n).transpose(0, 1, 3, 2))
    if fmt == "e4m3":
        words = by_word.astype(ml_dtypes.float8_e4m3fn).view(np.uint8)
    else:
        c = by_word.astype(ml_dtypes.float4_e2m1fn).view(np.uint8) & 0xF
        words = (c[..., 0::2] | (c[..., 1::2] << 4)).reshape(k // 512, 128, 2 * n)
    return np.ascontiguousarray(words), np.ascontiguousarray(byte.astype(np.uint8).reshape(k // 512, 16, n))


def unpack_weight(words, scales, fmt):
    g, _, n = scales.shape
    words = np.ascontiguousarray(words).reshape(g, 128, n, -1)
    if fmt == "e4m3":
        vals = words.view(ml_dtypes.float8_e4m3fn).astype(np.float64)
    else:
        nib = np.empty((g, 128, n, 4), np.uint8)
        nib[..., 0::2] = words & 0xF
        nib[..., 1::2] = words >> 4
        vals = E2M1[nib]
    vals = vals * np.repeat(np.exp2(scales.astype(np.float64) - 127.0), 8, axis=1)[..., None]
    return vals.transpose(0, 1, 3, 2).reshape(g * 512, n)


def gelu(v):
    return 0.5 * v * (1.0 + np.tanh(np.sqrt(2.0 / np.pi) * (v + 0.044715 * v**3)))


K, M, T, S = 1024, 1024, 1024, 512


def setup_inputs():
    n = np.random.standard_normal
    s = mx_kscale(K)[:, None]
    u = mx_kscale(512)[:, None]
    p_w4 = pack_weight(n((K, M)) / np.sqrt(K) / s, "e2m1")
    return {
        "xT": (n((K, T)) * s).astype(np.float32),
        "w4_words": p_w4[0],
        "w4_scales": p_w4[1],
        "down": (n((K, 512)) / np.sqrt(K) / s * u.T).astype(np.float32),
        "up": (0.5 * n((512, M)) / np.sqrt(512) / u).astype(np.float32),
        "wgt": np.repeat(np.random.uniform(0.5, 2.0, (8, S)), 16, axis=0).astype(np.float32),
        "b": (0.3 * n(1024)).astype(np.float32),
        "wgo": np.repeat(np.random.uniform(0.5, 2.0, (8, S)), 16, axis=0).astype(np.float32),
        "offs": striped8(np.stack([np.random.permutation(T)[:S] for _ in range(8)])),
        "offs2": striped8(np.stack([np.random.permutation(T)[:S] for _ in range(8)])),
    }


def reference(xT, w4_words, w4_scales, down, up, wgt, b, wgo, offs, offs2):
    idx = unstriped8(offs)
    group = np.arange(K) % 512 // 64
    xg = f64(wgt)[np.arange(K) // 4 % 128] * f64(xT)[np.arange(K)[:, None], idx[group]]
    xT_ = mxq(xg, 0, "e4m3")
    w4_ = unpack_weight(w4_words, w4_scales, "e2m1")
    down_ = mxq(f64(down), 0, "e4m3")
    up_ = mxq(f64(up), 0, "e4m3")
    h_ = mxq(down_.T @ xT_, 0, "e4m3")
    y = w4_.T @ xT_ + up_.T @ h_
    place = unstriped8(offs2)[np.arange(M) % 128 // 16]
    out = np.zeros((M, T))
    out[np.arange(M)[:, None], place] = f64(wgo)[np.arange(M) % 128] * (gelu(y + f64(b)[:, None]))
    return out

@@ -1,0 +1,279 @@
+from contextlib import ExitStack
+
+import concourse.mybir as mybir
+from concourse.masks import make_identity
+
+K, M, T, S, R = 1024, 1024, 1024, 512, 512
+FLOPS = 2 * S * (K * R + K * M + R * M)
+
+F32 = mybir.dt.float32
+BF16 = mybir.dt.bfloat16
+I32 = mybir.dt.int32
+U32 = mybir.dt.uint32
+U16 = mybir.dt.uint16
+U8 = mybir.dt.uint8
+FP8X4 = mybir.dt.float8_e4m3fn_x4
+FP4X4 = mybir.dt.float4_e2m1fn_x4
+MULT = mybir.AluOpType.mult
+GELU = mybir.ActivationFunctionType.Gelu_apprx_tanh
+
+P = 128
+PACK = 4
+K_PASS = P * PACK
+PASSES = K // K_PASS
+HALF = S // 2
+QUARTER = S // 4
+ROW_TILES = M // P
+OUT_TILES = 3
+UP_CHUNKS = [(0, 128), (128, 128), (256, 256), (512, 256), (768, 256)]
+W4_CHUNKS = [(0, 256), (256, 768)]
+
+
+def tile_list_hboth_l_gelu_kernel(
+    tc, xT, w4_words, w4_scales, down, up, wgt, b, wgo, offs, offs2, out
+):
+    nc = tc.nc
+    with ExitStack() as ctx:
+        keep = ctx.enter_context(tc.tile_pool(name="keep", bufs=1))
+        psum = ctx.enter_context(tc.psum_pool(name="psum", bufs=8))
+
+        def sb(name, shape, dtype):
+            return keep.tile(shape, dtype, name=name, align_bytes=64)
+
+        def bank():
+            return psum.tile([P, S], F32, name="bank")
+
+        pick = keep.tile([P, S // 16], U16, name="pick")
+        place = keep.tile([P, S // 16], U16, name="place")
+        wgt_sb = sb("wgt_sb", [P, S], F32)
+        wgo_sb = sb("wgo_sb", [P, S], F32)
+        planes = [[sb(f"plane{a}{i}", [P, T], F32) for i in range(PACK)] for a in range(PASSES)]
+        down_raw0 = sb("down_raw0", [P, PACK, R], F32)
+        down_raw1 = [sb(f"down_raw1{u}", [P, PACK, R // 2], F32) for u in range(2)]
+        up_raw = [sb(f"up_raw{c}", [P, PACK, w], F32) for c, (n0, w) in enumerate(UP_CHUNKS)]
+        w4_codes = [sb(f"w4_codes{c}", [P, PASSES, 2 * w], U8) for c, (n0, w) in enumerate(W4_CHUNKS)]
+        w4_sc = sb("w4_sc", [P, PASSES, M], U8)
+        b_rows = sb("b_rows", [P, P], F32)
+        bias = sb("bias", [P, ROW_TILES], F32)
+        ident = sb("ident", [P, P], F32)
+        warm = sb("warm", [P, 8], F32)
+        outs = [sb(f"out{o}", [P, T], F32) for o in range(OUT_TILES)]
+
+        nc.vector.memset(b_rows[:], 0.0)
+        nc.scalar.activation(warm[:, 0:1], b_rows[:, 0:1], GELU)
+        nc.vector.memset(w4_sc[:].rearrange("p a n -> p (a n)").bitcast(U32), 0)
+        nc.vector.memset(outs[0][:], 0.0)
+        make_identity(nc, ident[:])
+        for o in range(1, OUT_TILES):
+            nc.gpsimd.memset(outs[o][:], 0.0)
+
+        def load_plane(a, i):
+            rows = xT[a * K_PASS : (a + 1) * K_PASS, :].rearrange("(p i) t -> p i t", i=PACK)
+            nc.sync.dma_start(planes[a][i][:], rows[:, i, :])
+
+        def down_rows(a):
+            return down[a * K_PASS : (a + 1) * K_PASS, :].rearrange("(p j) r -> p j r", j=PACK)
+
+        def load_up(c):
+            n0, w = UP_CHUNKS[c]
+            nc.sync.dma_start(up_raw[c][:], up.rearrange("(p j) n -> p j n", j=PACK)[:, :, n0 : n0 + w])
+
+        def load_w4(c):
+            n0, w = W4_CHUNKS[c]
+            src = w4_words[:, :, 2 * n0 : 2 * (n0 + w)].rearrange("a p n -> p a n")
+            nc.sync.dma_start(w4_codes[c][:].bitcast(I32), src.bitcast(I32))
+
+        nc.sync.dma_start(pick[:], offs)
+        nc.sync.dma_start(wgt_sb[:], wgt)
+        for i in range(PACK):
+            load_plane(0, i)
+        nc.sync.dma_start(b_rows[0:ROW_TILES, :], b.rearrange("(c p) -> c p", p=P))
+        nc.sync.dma_start(down_raw0[:], down_rows(0))
+        nc.sync.dma_start(place[:], offs2)
+        for i in range(PACK):
+            load_plane(1, i)
+        for u in range(2):
+            nc.sync.dma_start(down_raw1[u][:], down_rows(1)[:, :, u * (R // 2) : (u + 1) * (R // 2)])
+        load_up(0)
+        for q in range(4):
+            src = w4_scales[:, 4 * q : 4 * q + 4, :].rearrange("a r n -> r a n")
+            nc.sync.dma_start(w4_sc[32 * q : 32 * q + 4, :, :].bitcast(I32), src.bitcast(I32))
+        load_w4(0)
+        nc.sync.dma_start(wgo_sb[:], wgo)
+        load_up(1)
+        load_w4(1)
+        for c in range(2, len(UP_CHUNKS)):
+            load_up(c)
+
+        b_bank = bank()
+        nc.tensor.transpose(b_bank[:, 0:P], b_rows[:], ident[:])
+        nc.scalar.copy(bias[:], b_bank[:, 0:ROW_TILES])
+
+        def interleave(copy, dst, src):
+            copy(
+                dst.rearrange("p (c i) t -> p c t i", i=4),
+                src.rearrange("p t (c i) -> p c t i", i=4),
+            )
+
+        def quantize(codes, scales, grouped):
+            nc.vector.quantize_mx(out=codes.bitcast(FP8X4), scales=scales, in_=grouped)
+
+        x_codes = sb("x_codes", [P, PASSES, S], U32)
+        x_sc = sb("x_sc", [P, PASSES, S], U8)
+        picked = [[sb(f"picked{a}{h}", [P, PACK, HALF], F32) for h in range(2)] for a in range(PASSES)]
+        x_bf = [[sb(f"x_bf{a}{h}", [P, HALF, PACK], BF16) for h in range(2)] for a in range(PASSES)]
+
+        def gather(a):
+            for i in range(PACK):
+                for h in range(2):
+                    window = planes[a][i][:].indirect(pick[:, 16 * h : 16 * (h + 1)])
+                    nc.vector.tensor_tensor(
+                        picked[a][h][:, i, :], window, wgt_sb[:, h * HALF : (h + 1) * HALF], MULT
+                    )
+
+        def x_round(a, h):
+            interleave(nc.scalar.copy, x_bf[a][h][:], picked[a][h][:])
+
+        def x_quantize(a, h):
+            cols = slice(h * HALF, (h + 1) * HALF)
+            quantize(x_codes[:, a, cols], x_sc[:, a, cols], x_bf[a][h][:].rearrange("p c t -> p (c t)"))
+
+        d_codes = sb("d_codes", [P, PASSES, R], U32)
+        d_sc = sb("d_sc", [P, PASSES, R], U8)
+        d_bf = [sb(f"d_bf{a}", [P, PACK, P, PACK], BF16) for a in range(PASSES)]
+
+        def down_round(copy, a, raw, m0, m1):
+            copy(
+                d_bf[a][:, :, m0:m1, :].rearrange("p t m j -> p m j t"),
+                raw.rearrange("p j (m t) -> p m j t", t=PACK),
+            )
+
+        u_codes = sb("u_codes", [P, M], U32)
+        u_sc = sb("u_sc", [P, M], U8)
+        u_bf = [sb(f"u_bf{c}", [P, w, PACK], BF16) for c, (n0, w) in enumerate(UP_CHUNKS)]
+
+        def up_prepare(c, copy):
+            n0, w = UP_CHUNKS[c]
+            interleave(copy, u_bf[c][:], up_raw[c][:])
+            quantize(u_codes[:, n0 : n0 + w], u_sc[:, n0 : n0 + w], u_bf[c][:].rearrange("p n t -> p (n t)"))
+
+        h_codes = sb("h_codes", [P, S], U32)
+        h_sc = sb("h_sc", [P, S], U8)
+        h_bf = [sb(f"h_bf{q}", [P, QUARTER, PACK], BF16) for q in range(4)]
+
+        def h_quarter(q):
+            acc = bank()
+            cols = slice(q * QUARTER, (q + 1) * QUARTER)
+            for t in range(PACK):
+                m = slice(t * P, (t + 1) * P)
+                for a in range(PASSES):
+                    nc.tensor.matmul_mx(
+                        out=acc[:, m],
+                        lhsT=d_codes[:, a, m].bitcast(FP8X4),
+                        lhsT_scale=d_sc[:, a, m],
+                        rhs=x_codes[:, a, cols].bitcast(FP8X4),
+                        rhs_scale=x_sc[:, a, cols],
+                        start=(a == 0),
+                        stop=(a == PASSES - 1),
+                    )
+            nc.scalar.copy(h_bf[q][:], acc[:].rearrange("p (t n) -> p n t", t=PACK))
+
+        def h_quantize(q):
+            cols = slice(q * QUARTER, (q + 1) * QUARTER)
+            quantize(h_codes[:, cols], h_sc[:, cols], h_bf[q][:].rearrange("p n t -> p (n t)"))
+
+        act = [sb(f"act{n}", [P, S], F32) for n in range(ROW_TILES)]
+
+        def y_sum(acc, n, cols):
+            c = 0 if n * P < W4_CHUNKS[1][0] else 1
+            off = n * P - W4_CHUNKS[c][0]
+            rows = slice(n * P, (n + 1) * P)
+            for a in range(PASSES):
+                nc.tensor.matmul_mx(
+                    out=acc,
+                    lhsT=w4_codes[c][:, a, 2 * off : 2 * (off + P)].bitcast(FP4X4),
+                    lhsT_scale=w4_sc[:, a, rows],
+                    rhs=x_codes[:, a, cols].bitcast(FP8X4),
+                    rhs_scale=x_sc[:, a, cols],
+                    start=(a == 0),
+                    stop=False,
+                )
+            nc.tensor.matmul_mx(
+                out=acc,
+                lhsT=u_codes[:, rows].bitcast(FP8X4),
+                lhsT_scale=u_sc[:, rows],
+                rhs=h_codes[:, cols].bitcast(FP8X4),
+                rhs_scale=h_sc[:, cols],
+                start=False,
+                stop=True,
+            )
+
+        def y_piece(n, j0, width):
+            acc = bank()
+            cols = slice(j0, j0 + width)
+            y_sum(acc[:, 0:width], n, cols)
+            nc.scalar.activation(act[n][:, cols], acc[:, 0:width], GELU, bias=bias[:, n : n + 1])
+
+        def y_half(n, h):
+            acc = bank()
+            for v in range(2):
+                j0 = h * HALF + v * QUARTER
+                y_sum(acc[:, v * QUARTER : (v + 1) * QUARTER], n, slice(j0, j0 + QUARTER))
+            cols = slice(h * HALF, (h + 1) * HALF)
+            nc.scalar.activation(act[n][:, cols], acc[:, 0:HALF], GELU, bias=bias[:, n : n + 1])
+
+        def scatter(n, h):
+            cols = slice(h * HALF, (h + 1) * HALF)
+            window = outs[n % OUT_TILES][:].indirect(place[:, 16 * h : 16 * (h + 1)])
+            nc.vector.tensor_tensor(window, act[n][:, cols], wgo_sb[:, cols], MULT)
+
+        def store(n):
+            nc.sync.dma_start(out[n * P : (n + 1) * P, :], outs[n % OUT_TILES][:])
+
+        gather(0)
+        x_round(0, 0)
+        x_round(0, 1)
+        down_round(nc.scalar.copy, 0, down_raw0[:], 0, P)
+        x_quantize(0, 0)
+        x_quantize(0, 1)
+        quantize(d_codes[:, 0, :], d_sc[:, 0, :], d_bf[0][:].rearrange("p t m j -> p (t m j)"))
+        gather(1)
+        x_round(1, 0)
+        down_round(nc.vector.tensor_copy, 1, down_raw1[0][:], 0, P // 2)
+        x_quantize(1, 0)
+        down_round(nc.vector.tensor_copy, 1, down_raw1[1][:, :, 0:160], 64, 104)
+        down_round(nc.scalar.copy, 1, down_raw1[1][:, :, 160:256], 104, P)
+        x_round(1, 1)
+        for t in range(PACK):
+            m = slice(t * P, (t + 1) * P)
+            quantize(d_codes[:, 1, m], d_sc[:, 1, m], d_bf[1][:, t, :, :].rearrange("p m j -> p (m j)"))
+        x_quantize(1, 1)
+        h_quarter(0)
+        h_quarter(1)
+        up_prepare(0, nc.vector.tensor_copy)
+        h_quantize(0)
+        h_quantize(1)
+        y_piece(0, 0, QUARTER)
+        y_piece(0, QUARTER, QUARTER)
+        up_prepare(1, nc.vector.tensor_copy)
+        h_quarter(2)
+        h_quarter(3)
+        scatter(0, 0)
+        y_half(1, 0)
+        h_quantize(2)
+        h_quantize(3)
+        scatter(1, 0)
+        y_half(0, 1)
+        y_half(1, 1)
+        up_prepare(2, nc.scalar.copy)
+        scatter(0, 1)
+        store(0)
+        scatter(1, 1)
+        store(1)
+        for n in range(2, ROW_TILES):
+            if n in (2, 4):
+                up_prepare(n // 2 + 2, nc.scalar.copy)
+            y_piece(n, 0, S)
+            scatter(n, 0)
+            scatter(n, 1)
+            store(n)

@@ -24,9 +24,10 @@ PASSES = K // K_PASS
 HALF = S // 2
 QUARTER = S // 4
 ROW_TILES = M // P
-OUT_TILES = 3
-UP_CHUNKS = [(0, 128), (128, 128), (256, 256), (512, 256), (768, 256)]
-W4_CHUNKS = [(0, 256), (256, 768)]
+OUT_TILES = 8
+EARLY_TILES = 4
+UP_CHUNKS = [(0, 128), (128, 256), (384, 128), (512, 256), (768, 256)]
+W4_CHUNKS = [(0, 512), (512, 512)]
 
 
 def tile_list_hboth_l_gelu_kernel(
@@ -35,21 +36,20 @@ def tile_list_hboth_l_gelu_kernel(
     nc = tc.nc
     with ExitStack() as ctx:
         keep = ctx.enter_context(tc.tile_pool(name="keep", bufs=1))
-        psum = ctx.enter_context(tc.psum_pool(name="psum", bufs=8))
+        psum = ctx.enter_context(tc.psum_pool(name="psum", bufs=1))
 
-        def sb(name, shape, dtype):
-            return keep.tile(shape, dtype, name=name, align_bytes=64)
+        def sb(name, shape, dtype, tag=None):
+            return keep.tile(shape, dtype, name=name, tag=tag or name, align_bytes=64)
 
-        def bank():
-            return psum.tile([P, S], F32, name="bank")
+        def bank(tag):
+            return psum.tile([P, S], F32, name=tag, tag=tag, bufs=4 if tag == "ring" else 1)
 
         pick = keep.tile([P, S // 16], U16, name="pick")
         place = keep.tile([P, S // 16], U16, name="place")
         wgt_sb = sb("wgt_sb", [P, S], F32)
         wgo_sb = sb("wgo_sb", [P, S], F32)
         planes = [[sb(f"plane{a}{i}", [P, T], F32) for i in range(PACK)] for a in range(PASSES)]
-        down_raw0 = sb("down_raw0", [P, PACK, R], F32)
-        down_raw1 = [sb(f"down_raw1{u}", [P, PACK, R // 2], F32) for u in range(2)]
+        down_raw = [[sb(f"down_raw{a}{u}", [P, PACK, R // 2], F32) for u in range(2)] for a in range(PASSES)]
         up_raw = [sb(f"up_raw{c}", [P, PACK, w], F32) for c, (n0, w) in enumerate(UP_CHUNKS)]
         w4_codes = [sb(f"w4_codes{c}", [P, PASSES, 2 * w], U8) for c, (n0, w) in enumerate(W4_CHUNKS)]
         w4_sc = sb("w4_sc", [P, PASSES, M], U8)
@@ -59,20 +59,20 @@ def tile_list_hboth_l_gelu_kernel(
         warm = sb("warm", [P, 8], F32)
         outs = [sb(f"out{o}", [P, T], F32) for o in range(OUT_TILES)]
 
-        nc.vector.memset(b_rows[:], 0.0)
+        nc.gpsimd.memset(b_rows[:], 0.0)
         nc.scalar.activation(warm[:, 0:1], b_rows[:, 0:1], GELU)
-        nc.vector.memset(w4_sc[:].rearrange("p a n -> p (a n)").bitcast(U32), 0)
-        nc.vector.memset(outs[0][:], 0.0)
         make_identity(nc, ident[:])
-        for o in range(1, OUT_TILES):
+        nc.gpsimd.memset(w4_sc[:].rearrange("p a n -> p (a n)").bitcast(U32), 0)
+        for o in range(OUT_TILES):
             nc.gpsimd.memset(outs[o][:], 0.0)
 
         def load_plane(a, i):
             rows = xT[a * K_PASS : (a + 1) * K_PASS, :].rearrange("(p i) t -> p i t", i=PACK)
             nc.sync.dma_start(planes[a][i][:], rows[:, i, :])
 
-        def down_rows(a):
-            return down[a * K_PASS : (a + 1) * K_PASS, :].rearrange("(p j) r -> p j r", j=PACK)
+        def load_down(a, u):
+            rows = down[a * K_PASS : (a + 1) * K_PASS, :].rearrange("(p j) r -> p j r", j=PACK)
+            nc.sync.dma_start(down_raw[a][u][:], rows[:, :, u * (R // 2) : (u + 1) * (R // 2)])
 
         def load_up(c):
             n0, w = UP_CHUNKS[c]
@@ -83,31 +83,43 @@ def tile_list_hboth_l_gelu_kernel(
             src = w4_words[:, :, 2 * n0 : 2 * (n0 + w)].rearrange("a p n -> p a n")
             nc.sync.dma_start(w4_codes[c][:].bitcast(I32), src.bitcast(I32))
 
+        def load_scales():
+            for q in range(4):
+                src = w4_scales[:, 4 * q : 4 * q + 4, :].rearrange("a r n -> r a n")
+                nc.sync.dma_start(w4_sc[32 * q : 32 * q + 4, :, :].bitcast(I32), src.bitcast(I32))
+
         nc.sync.dma_start(pick[:], offs)
-        nc.sync.dma_start(wgt_sb[:], wgt)
-        for i in range(PACK):
+        nc.sync.dma_start(wgt_sb[:, 0:HALF], wgt[:, 0:HALF])
+        load_plane(0, 0)
+        nc.sync.dma_start(wgt_sb[:, HALF:S], wgt[:, HALF:S])
+        for i in range(1, PACK):
             load_plane(0, i)
         nc.sync.dma_start(b_rows[0:ROW_TILES, :], b.rearrange("(c p) -> c p", p=P))
-        nc.sync.dma_start(down_raw0[:], down_rows(0))
+        load_plane(1, 0)
+        load_plane(1, 1)
+        load_plane(1, 2)
+        load_down(0, 0)
         nc.sync.dma_start(place[:], offs2)
-        for i in range(PACK):
-            load_plane(1, i)
-        for u in range(2):
-            nc.sync.dma_start(down_raw1[u][:], down_rows(1)[:, :, u * (R // 2) : (u + 1) * (R // 2)])
+        load_plane(1, 3)
+        load_down(0, 1)
+        load_down(1, 0)
+        load_down(1, 1)
         load_up(0)
-        for q in range(4):
-            src = w4_scales[:, 4 * q : 4 * q + 4, :].rearrange("a r n -> r a n")
-            nc.sync.dma_start(w4_sc[32 * q : 32 * q + 4, :, :].bitcast(I32), src.bitcast(I32))
+        load_up(1)
+        load_scales()
         load_w4(0)
         nc.sync.dma_start(wgo_sb[:], wgo)
-        load_up(1)
+        load_up(2)
         load_w4(1)
-        for c in range(2, len(UP_CHUNKS)):
-            load_up(c)
+        load_up(3)
+        load_up(4)
 
-        b_bank = bank()
+        b_bank = bank("c")
         nc.tensor.transpose(b_bank[:, 0:P], b_rows[:], ident[:])
         nc.scalar.copy(bias[:], b_bank[:, 0:ROW_TILES])
+        own_bias = {n: sb(f"bias{n}", [P, 1], F32) for n in (0, 1, 2, 3)}
+        for n in own_bias:
+            nc.scalar.copy(own_bias[n][:], b_bank[:, n : n + 1])
 
         def interleave(copy, dst, src):
             copy(
@@ -120,27 +132,30 @@ def tile_list_hboth_l_gelu_kernel(
 
         x_codes = sb("x_codes", [P, PASSES, S], U32)
         x_sc = sb("x_sc", [P, PASSES, S], U8)
-        picked = [[sb(f"picked{a}{h}", [P, PACK, HALF], F32) for h in range(2)] for a in range(PASSES)]
-        x_bf = [[sb(f"x_bf{a}{h}", [P, HALF, PACK], BF16) for h in range(2)] for a in range(PASSES)]
+        shared = sb("shared", [P, 6, HALF], F32)
+        picked = {(1, 1): shared[:, 0:4, :]}
+        x_bf = {}
 
-        def gather(a):
-            for i in range(PACK):
-                for h in range(2):
-                    window = planes[a][i][:].indirect(pick[:, 16 * h : 16 * (h + 1)])
-                    nc.vector.tensor_tensor(
-                        picked[a][h][:, i, :], window, wgt_sb[:, h * HALF : (h + 1) * HALF], MULT
-                    )
+        def gather(a, i, h):
+            if (a, h) not in picked:
+                picked[a, h] = sb(f"picked{a}{h}", [P, PACK, HALF], F32, tag={}.get((a, h)))[:]
+            window = planes[a][i][:].indirect(pick[:, 16 * h : 16 * (h + 1)])
+            nc.vector.tensor_tensor(picked[a, h][:, i, :], window, wgt_sb[:, h * HALF : (h + 1) * HALF], MULT)
 
-        def x_round(a, h):
-            interleave(nc.scalar.copy, x_bf[a][h][:], picked[a][h][:])
+        def x_round(copy, a, h):
+            x_bf[a, h] = sb(f"x_bf{a}{h}", [P, HALF, PACK], BF16, tag={(1, 1): "bias1"}.get((a, h)))
+            interleave(copy, x_bf[a, h][:], picked[a, h])
 
         def x_quantize(a, h):
             cols = slice(h * HALF, (h + 1) * HALF)
-            quantize(x_codes[:, a, cols], x_sc[:, a, cols], x_bf[a][h][:].rearrange("p c t -> p (c t)"))
+            quantize(x_codes[:, a, cols], x_sc[:, a, cols], x_bf[a, h][:].rearrange("p c t -> p (c t)"))
 
         d_codes = sb("d_codes", [P, PASSES, R], U32)
         d_sc = sb("d_sc", [P, PASSES, R], U8)
-        d_bf = [sb(f"d_bf{a}", [P, PACK, P, PACK], BF16) for a in range(PASSES)]
+        d_bf = [
+            sb("d_bf0", [P, PACK, P, PACK], BF16),
+            shared[:, 2:6, :].rearrange("p u c -> p (u c)").bitcast(BF16).rearrange("p (t m j) -> p t m j", t=PACK, j=PACK),
+        ]
 
         def down_round(copy, a, raw, m0, m1):
             copy(
@@ -150,19 +165,37 @@ def tile_list_hboth_l_gelu_kernel(
 
         u_codes = sb("u_codes", [P, M], U32)
         u_sc = sb("u_sc", [P, M], U8)
-        u_bf = [sb(f"u_bf{c}", [P, w, PACK], BF16) for c, (n0, w) in enumerate(UP_CHUNKS)]
+        UP_TAG = {2: "bias0", 3: "bias2", 4: "bias3"}
 
-        def up_prepare(c, copy):
+        def up_prepare(copy, c):
             n0, w = UP_CHUNKS[c]
-            interleave(copy, u_bf[c][:], up_raw[c][:])
-            quantize(u_codes[:, n0 : n0 + w], u_sc[:, n0 : n0 + w], u_bf[c][:].rearrange("p n t -> p (n t)"))
+            grouped = sb(f"u_bf{c}", [P, w, PACK], BF16, tag=UP_TAG.get(c))
+            interleave(copy, grouped[:], up_raw[c][:])
+            quantize(u_codes[:, n0 : n0 + w], u_sc[:, n0 : n0 + w], grouped[:].rearrange("p n t -> p (n t)"))
+
+        def d_quantize(a, t0, t1):
+            m = slice(t0 * P, t1 * P)
+            quantize(d_codes[:, a, m], d_sc[:, a, m], d_bf[a][:, t0:t1, :, :].rearrange("p t m j -> p (t m j)"))
+
+        def warm_up():
+            spare = bank("d")
+            for w in range(6):
+                nc.tensor.matmul_mx(
+                    out=spare[:, (w % 2) * HALF : (w % 2 + 1) * HALF],
+                    lhsT=d_codes[:, 0, 0:P].bitcast(FP8X4),
+                    lhsT_scale=d_sc[:, 0, 0:P],
+                    rhs=x_codes[:, 0, 0:HALF].bitcast(FP8X4),
+                    rhs_scale=x_sc[:, 0, 0:HALF],
+                    start=True,
+                    stop=True,
+                )
 
         h_codes = sb("h_codes", [P, S], U32)
         h_sc = sb("h_sc", [P, S], U8)
-        h_bf = [sb(f"h_bf{q}", [P, QUARTER, PACK], BF16) for q in range(4)]
+        h_bf = [sb(f"h_bf{h}", [P, HALF, PACK], BF16) for h in range(2)]
 
-        def h_quarter(q):
-            acc = bank()
+        def h_quarter(q, tag):
+            acc = bank(tag)
             cols = slice(q * QUARTER, (q + 1) * QUARTER)
             for t in range(PACK):
                 m = slice(t * P, (t + 1) * P)
@@ -176,15 +209,23 @@ def tile_list_hboth_l_gelu_kernel(
                         start=(a == 0),
                         stop=(a == PASSES - 1),
                     )
-            nc.scalar.copy(h_bf[q][:], acc[:].rearrange("p (t n) -> p n t", t=PACK))
+            v = q % 2
+            dst = h_bf[q // 2][:, v * QUARTER : (v + 1) * QUARTER, :]
+            nc.scalar.copy(dst, acc[:].rearrange("p (t n) -> p n t", t=PACK))
 
-        def h_quantize(q):
-            cols = slice(q * QUARTER, (q + 1) * QUARTER)
-            quantize(h_codes[:, cols], h_sc[:, cols], h_bf[q][:].rearrange("p n t -> p (n t)"))
+        def h_quantize(j0, j1):
+            grouped = h_bf[j0 // HALF][:, j0 % HALF : j0 % HALF + j1 - j0, :]
+            quantize(h_codes[:, j0:j1], h_sc[:, j0:j1], grouped.rearrange("p n t -> p (n t)"))
 
-        act = [sb(f"act{n}", [P, S], F32) for n in range(ROW_TILES)]
+        act = {}
+        AFTER = {(1, 0): "up_raw2", (2, 0): "shared", (3, 0): "up_raw3", (5, 0): "up_raw4"}
 
-        def y_sum(acc, n, cols):
+        def act_half(n, h):
+            if (n, h) not in act:
+                act[n, h] = sb(f"act{n}{h}", [P, HALF], F32, tag=AFTER.get((n, h)))
+            return act[n, h]
+
+        def y_base(acc, n, cols):
             c = 0 if n * P < W4_CHUNKS[1][0] else 1
             off = n * P - W4_CHUNKS[c][0]
             rows = slice(n * P, (n + 1) * P)
@@ -198,6 +239,9 @@ def tile_list_hboth_l_gelu_kernel(
                     start=(a == 0),
                     stop=False,
                 )
+
+        def y_branch(acc, n, cols):
+            rows = slice(n * P, (n + 1) * P)
             nc.tensor.matmul_mx(
                 out=acc,
                 lhsT=u_codes[:, rows].bitcast(FP8X4),
@@ -208,72 +252,82 @@ def tile_list_hboth_l_gelu_kernel(
                 stop=True,
             )
 
-        def y_piece(n, j0, width):
-            acc = bank()
-            cols = slice(j0, j0 + width)
-            y_sum(acc[:, 0:width], n, cols)
-            nc.scalar.activation(act[n][:, cols], acc[:, 0:width], GELU, bias=bias[:, n : n + 1])
+        def y_sum(acc, n, cols):
+            y_base(acc, n, cols)
+            y_branch(acc, n, cols)
 
-        def y_half(n, h):
-            acc = bank()
+        def gelu(n, h, dst_cols, acc):
+            nc.scalar.activation(act_half(n, h)[:, dst_cols], acc, GELU, bias=own_bias[n][:] if h == 0 and n in own_bias else bias[:, n : n + 1])
+
+        def y_quarter(n, v, tag):
+            acc = bank(tag)
+            cols = slice(v * QUARTER, (v + 1) * QUARTER)
+            y_sum(acc[:, 0:QUARTER], n, cols)
+            gelu(n, 0, cols, acc[:, 0:QUARTER])
+
+        def y_half(n, h, tag="ring"):
+            acc = bank(tag)
             for v in range(2):
                 j0 = h * HALF + v * QUARTER
                 y_sum(acc[:, v * QUARTER : (v + 1) * QUARTER], n, slice(j0, j0 + QUARTER))
-            cols = slice(h * HALF, (h + 1) * HALF)
-            nc.scalar.activation(act[n][:, cols], acc[:, 0:HALF], GELU, bias=bias[:, n : n + 1])
+            gelu(n, h, slice(0, HALF), acc[:, 0:HALF])
 
         def scatter(n, h):
             cols = slice(h * HALF, (h + 1) * HALF)
             window = outs[n % OUT_TILES][:].indirect(place[:, 16 * h : 16 * (h + 1)])
-            nc.vector.tensor_tensor(window, act[n][:, cols], wgo_sb[:, cols], MULT)
+            nc.vector.tensor_tensor(window, act[n, h][:], wgo_sb[:, cols], MULT)
 
         def store(n):
             nc.sync.dma_start(out[n * P : (n + 1) * P, :], outs[n % OUT_TILES][:])
 
-        gather(0)
-        x_round(0, 0)
-        x_round(0, 1)
-        down_round(nc.scalar.copy, 0, down_raw0[:], 0, P)
+        on_scalar, on_vector = nc.scalar.copy, nc.vector.tensor_copy
+        for i in range(PACK):
+            gather(0, i, 0)
+            gather(0, i, 1)
+        x_round(on_scalar, 0, 0)
+        for i in range(PACK):
+            gather(1, i, 0)
+        down_round(on_scalar, 0, down_raw[0][0][:], 0, 64)
+        x_round(on_scalar, 1, 0)
         x_quantize(0, 0)
-        x_quantize(0, 1)
-        quantize(d_codes[:, 0, :], d_sc[:, 0, :], d_bf[0][:].rearrange("p t m j -> p (t m j)"))
-        gather(1)
-        x_round(1, 0)
-        down_round(nc.vector.tensor_copy, 1, down_raw1[0][:], 0, P // 2)
+        down_round(on_vector, 0, down_raw[0][1][:], 64, P)
         x_quantize(1, 0)
-        down_round(nc.vector.tensor_copy, 1, down_raw1[1][:, :, 0:160], 64, 104)
-        down_round(nc.scalar.copy, 1, down_raw1[1][:, :, 160:256], 104, P)
-        x_round(1, 1)
-        for t in range(PACK):
-            m = slice(t * P, (t + 1) * P)
-            quantize(d_codes[:, 1, m], d_sc[:, 1, m], d_bf[1][:, t, :, :].rearrange("p m j -> p (m j)"))
-        x_quantize(1, 1)
-        h_quarter(0)
-        h_quarter(1)
-        up_prepare(0, nc.vector.tensor_copy)
-        h_quantize(0)
-        h_quantize(1)
-        y_piece(0, 0, QUARTER)
-        y_piece(0, QUARTER, QUARTER)
-        up_prepare(1, nc.vector.tensor_copy)
-        h_quarter(2)
-        h_quarter(3)
+        d_quantize(0, 0, 4)
+        warm_up()
+        down_round(on_scalar, 1, down_raw[1][0][:], 0, 64)
+        down_round(on_vector, 1, down_raw[1][1][:], 64, P)
+        d_quantize(1, 0, 4)
+        h_quarter(0, "a")
+        h_quarter(1, "b")
+        h_quantize(0, QUARTER)
+        h_quantize(QUARTER, HALF)
+        up_prepare(on_scalar, 0)
+        y_quarter(0, 0, "c")
+        y_quarter(0, 1, "d")
+        x_round(on_scalar, 0, 1)
+        x_quantize(0, 1)
+        up_prepare(on_scalar, 1)
+        for i in range(PACK):
+            gather(1, i, 1)
         scatter(0, 0)
+        up_prepare(on_scalar, 2)
         y_half(1, 0)
-        h_quantize(2)
-        h_quantize(3)
-        scatter(1, 0)
-        y_half(0, 1)
-        y_half(1, 1)
-        up_prepare(2, nc.scalar.copy)
-        scatter(0, 1)
-        store(0)
-        scatter(1, 1)
-        store(1)
-        for n in range(2, ROW_TILES):
-            if n in (2, 4):
-                up_prepare(n // 2 + 2, nc.scalar.copy)
-            y_piece(n, 0, S)
+        x_round(on_scalar, 1, 1)
+        x_quantize(1, 1)
+        y_half(2, 0)
+        up_prepare(on_scalar, 3)
+        y_half(3, 0)
+        up_prepare(on_scalar, 4)
+        y_half(4, 0)
+        h_quarter(2, "a")
+        h_quarter(3, "b")
+        h_quantize(HALF, S)
+        y_half(5, 0)
+        y_half(6, 0)
+        y_half(7, 0, "b")
+        for n in range(1, ROW_TILES):
             scatter(n, 0)
+        for n in range(ROW_TILES):
+            y_half(n, 1)
             scatter(n, 1)
             store(n)

@@ -26,7 +26,7 @@ QUARTER = S // 4
 ROW_TILES = M // P
 OUT_TILES = 8
 EARLY_TILES = 4
-UP_CHUNKS = [(0, 128), (128, 256), (384, 128), (512, 256), (768, 256)]
+UP_CHUNKS = [(0, 256), (256, 256), (512, 256), (768, 256)]
 W4_CHUNKS = [(0, 512), (512, 512)]
 
 
@@ -49,7 +49,7 @@ def tile_list_hboth_l_gelu_kernel(
         wgt_sb = sb("wgt_sb", [P, S], F32)
         wgo_sb = sb("wgo_sb", [P, S], F32)
         planes = [[sb(f"plane{a}{i}", [P, T], F32) for i in range(PACK)] for a in range(PASSES)]
-        down_raw = [[sb(f"down_raw{a}{u}", [P, PACK, R // 2], F32) for u in range(2)] for a in range(PASSES)]
+        down_raw = [sb(f"down_raw{a}", [P, PACK, R], F32) for a in range(PASSES)]
         up_raw = [sb(f"up_raw{c}", [P, PACK, w], F32) for c, (n0, w) in enumerate(UP_CHUNKS)]
         w4_codes = [sb(f"w4_codes{c}", [P, PASSES, 2 * w], U8) for c, (n0, w) in enumerate(W4_CHUNKS)]
         w4_sc = sb("w4_sc", [P, PASSES, M], U8)
@@ -62,17 +62,20 @@ def tile_list_hboth_l_gelu_kernel(
         nc.gpsimd.memset(b_rows[:], 0.0)
         nc.scalar.activation(warm[:, 0:1], b_rows[:, 0:1], GELU)
         make_identity(nc, ident[:])
-        nc.gpsimd.memset(w4_sc[:].rearrange("p a n -> p (a n)").bitcast(U32), 0)
-        for o in range(OUT_TILES):
-            nc.gpsimd.memset(outs[o][:], 0.0)
+        nc.vector.memset(w4_sc[:].rearrange("p a n -> p (a n)").bitcast(U32), 0)
+        for o in range(4):
+            nc.vector.memset(outs[o][:].bitcast(I32), 0)
+        for o in range(4, OUT_TILES):
+            nc.vector.memset(outs[o][:, 0:8].bitcast(I32), 0)
+            nc.gpsimd.memset(outs[o][:].bitcast(I32), 0)
 
         def load_plane(a, i):
             rows = xT[a * K_PASS : (a + 1) * K_PASS, :].rearrange("(p i) t -> p i t", i=PACK)
             nc.sync.dma_start(planes[a][i][:], rows[:, i, :])
 
-        def load_down(a, u):
+        def load_down(a):
             rows = down[a * K_PASS : (a + 1) * K_PASS, :].rearrange("(p j) r -> p j r", j=PACK)
-            nc.sync.dma_start(down_raw[a][u][:], rows[:, :, u * (R // 2) : (u + 1) * (R // 2)])
+            nc.sync.dma_start(down_raw[a][:], rows)
 
         def load_up(c):
             n0, w = UP_CHUNKS[c]
@@ -89,30 +92,26 @@ def tile_list_hboth_l_gelu_kernel(
                 nc.sync.dma_start(w4_sc[32 * q : 32 * q + 4, :, :].bitcast(I32), src.bitcast(I32))
 
         nc.sync.dma_start(pick[:], offs)
-        nc.sync.dma_start(wgt_sb[:, 0:HALF], wgt[:, 0:HALF])
+        nc.sync.dma_start(wgt_sb[:], wgt)
         load_plane(0, 0)
-        nc.sync.dma_start(wgt_sb[:, HALF:S], wgt[:, HALF:S])
         for i in range(1, PACK):
             load_plane(0, i)
         nc.sync.dma_start(b_rows[0:ROW_TILES, :], b.rearrange("(c p) -> c p", p=P))
         load_plane(1, 0)
         load_plane(1, 1)
         load_plane(1, 2)
-        load_down(0, 0)
-        nc.sync.dma_start(place[:], offs2)
         load_plane(1, 3)
-        load_down(0, 1)
-        load_down(1, 0)
-        load_down(1, 1)
+        nc.sync.dma_start(place[:], offs2)
+        load_down(0)
+        load_down(1)
         load_up(0)
-        load_up(1)
         load_scales()
         load_w4(0)
         nc.sync.dma_start(wgo_sb[:], wgo)
-        load_up(2)
+        load_up(1)
         load_w4(1)
+        load_up(2)
         load_up(3)
-        load_up(4)
 
         b_bank = bank("c")
         nc.tensor.transpose(b_bank[:, 0:P], b_rows[:], ident[:])
@@ -157,15 +156,15 @@ def tile_list_hboth_l_gelu_kernel(
             shared[:, 2:6, :].rearrange("p u c -> p (u c)").bitcast(BF16).rearrange("p (t m j) -> p t m j", t=PACK, j=PACK),
         ]
 
-        def down_round(copy, a, raw, m0, m1):
+        def down_round(copy, a, m0, m1):
             copy(
                 d_bf[a][:, :, m0:m1, :].rearrange("p t m j -> p m j t"),
-                raw.rearrange("p j (m t) -> p m j t", t=PACK),
+                down_raw[a][:, :, PACK * m0 : PACK * m1].rearrange("p j (m t) -> p m j t", t=PACK),
             )
 
         u_codes = sb("u_codes", [P, M], U32)
         u_sc = sb("u_sc", [P, M], U8)
-        UP_TAG = {2: "bias0", 3: "bias2", 4: "bias3"}
+        UP_TAG = {1: "bias0", 2: "bias2", 3: "bias3"}
 
         def up_prepare(copy, c):
             n0, w = UP_CHUNKS[c]
@@ -218,7 +217,7 @@ def tile_list_hboth_l_gelu_kernel(
             quantize(h_codes[:, j0:j1], h_sc[:, j0:j1], grouped.rearrange("p n t -> p (n t)"))
 
         act = {}
-        AFTER = {(1, 0): "up_raw2", (2, 0): "shared", (3, 0): "up_raw3", (5, 0): "up_raw4"}
+        AFTER = {(1, 0): "up_raw1", (2, 0): "shared", (3, 0): "up_raw2", (5, 0): "up_raw3"}
 
         def act_half(n, h):
             if (n, h) not in act:
@@ -287,15 +286,15 @@ def tile_list_hboth_l_gelu_kernel(
         x_round(on_scalar, 0, 0)
         for i in range(PACK):
             gather(1, i, 0)
-        down_round(on_scalar, 0, down_raw[0][0][:], 0, 64)
         x_round(on_scalar, 1, 0)
         x_quantize(0, 0)
-        down_round(on_vector, 0, down_raw[0][1][:], 64, P)
+        down_round(on_scalar, 0, 64, P)
+        down_round(on_vector, 0, 0, 64)
         x_quantize(1, 0)
         d_quantize(0, 0, 4)
         warm_up()
-        down_round(on_scalar, 1, down_raw[1][0][:], 0, 64)
-        down_round(on_vector, 1, down_raw[1][1][:], 64, P)
+        down_round(on_scalar, 1, 84, P)
+        down_round(on_vector, 1, 0, 84)
         d_quantize(1, 0, 4)
         h_quarter(0, "a")
         h_quarter(1, "b")
@@ -306,18 +305,17 @@ def tile_list_hboth_l_gelu_kernel(
         y_quarter(0, 1, "d")
         x_round(on_scalar, 0, 1)
         x_quantize(0, 1)
-        up_prepare(on_scalar, 1)
         for i in range(PACK):
             gather(1, i, 1)
         scatter(0, 0)
-        up_prepare(on_scalar, 2)
+        up_prepare(on_scalar, 1)
         y_half(1, 0)
         x_round(on_scalar, 1, 1)
         x_quantize(1, 1)
         y_half(2, 0)
-        up_prepare(on_scalar, 3)
+        up_prepare(on_scalar, 2)
         y_half(3, 0)
-        up_prepare(on_scalar, 4)
+        up_prepare(on_scalar, 3)
         y_half(4, 0)
         h_quarter(2, "a")
         h_quarter(3, "b")

@@ -24,10 +24,12 @@ PASSES = K // K_PASS
 HALF = S // 2
 QUARTER = S // 4
 ROW_TILES = M // P
-OUT_TILES = 8
-EARLY_TILES = 4
+OUT_TILES = 6
+EARLY = 1
+DOWN_ON_VECTOR = (64, 64)
+LOADS = "x00 x01 x02 x03 d0 x10 d1 x11 x12 x13"
 UP_CHUNKS = [(0, 256), (256, 256), (512, 256), (768, 256)]
-W4_CHUNKS = [(0, 512), (512, 512)]
+W4_CHUNKS = [(0, 640), (640, 384)]
 
 
 def tile_list_hboth_l_gelu_kernel(
@@ -60,14 +62,12 @@ def tile_list_hboth_l_gelu_kernel(
         outs = [sb(f"out{o}", [P, T], F32) for o in range(OUT_TILES)]
 
         nc.gpsimd.memset(b_rows[:], 0.0)
-        nc.scalar.activation(warm[:, 0:1], b_rows[:, 0:1], GELU)
+        nc.scalar.dma_start(b_rows[0:ROW_TILES, :], b.rearrange("(c p) -> c p", p=P))
         make_identity(nc, ident[:])
+        nc.scalar.activation(warm[:, 0:1], ident[:, 0:1], GELU)
         nc.vector.memset(w4_sc[:].rearrange("p a n -> p (a n)").bitcast(U32), 0)
-        for o in range(4):
+        for o in range(OUT_TILES):
             nc.vector.memset(outs[o][:].bitcast(I32), 0)
-        for o in range(4, OUT_TILES):
-            nc.vector.memset(outs[o][:, 0:8].bitcast(I32), 0)
-            nc.gpsimd.memset(outs[o][:].bitcast(I32), 0)
 
         def load_plane(a, i):
             rows = xT[a * K_PASS : (a + 1) * K_PASS, :].rearrange("(p i) t -> p i t", i=PACK)
@@ -93,30 +93,25 @@ def tile_list_hboth_l_gelu_kernel(
 
         nc.sync.dma_start(pick[:], offs)
         nc.sync.dma_start(wgt_sb[:], wgt)
-        load_plane(0, 0)
-        for i in range(1, PACK):
-            load_plane(0, i)
-        nc.sync.dma_start(b_rows[0:ROW_TILES, :], b.rearrange("(c p) -> c p", p=P))
-        load_plane(1, 0)
-        load_plane(1, 1)
-        load_plane(1, 2)
-        load_plane(1, 3)
-        nc.sync.dma_start(place[:], offs2)
-        load_down(0)
-        load_down(1)
+        for step in LOADS.split():
+            if step.startswith("x"):
+                load_plane(int(step[1]), int(step[2]))
+            else:
+                load_down(int(step[1]))
         load_up(0)
         load_scales()
         load_w4(0)
+        nc.sync.dma_start(place[:], offs2)
         nc.sync.dma_start(wgo_sb[:], wgo)
         load_up(1)
-        load_w4(1)
         load_up(2)
+        load_w4(1)
         load_up(3)
 
-        b_bank = bank("c")
+        b_bank = bank("d")
         nc.tensor.transpose(b_bank[:, 0:P], b_rows[:], ident[:])
         nc.scalar.copy(bias[:], b_bank[:, 0:ROW_TILES])
-        own_bias = {n: sb(f"bias{n}", [P, 1], F32) for n in (0, 1, 2, 3)}
+        own_bias = {n: sb(f"bias{n}", [P, 1], F32) for n in (0, 1, 2, 3, 5)}
         for n in own_bias:
             nc.scalar.copy(own_bias[n][:], b_bank[:, n : n + 1])
 
@@ -131,8 +126,8 @@ def tile_list_hboth_l_gelu_kernel(
 
         x_codes = sb("x_codes", [P, PASSES, S], U32)
         x_sc = sb("x_sc", [P, PASSES, S], U8)
-        shared = sb("shared", [P, 6, HALF], F32)
-        picked = {(1, 1): shared[:, 0:4, :]}
+        shared = sb("shared", [P, PACK + 1, HALF], F32)
+        picked = {(1, 1): shared[:, 0:PACK, :]}
         x_bf = {}
 
         def gather(a, i, h):
@@ -149,11 +144,29 @@ def tile_list_hboth_l_gelu_kernel(
             cols = slice(h * HALF, (h + 1) * HALF)
             quantize(x_codes[:, a, cols], x_sc[:, a, cols], x_bf[a, h][:].rearrange("p c t -> p (c t)"))
 
+        as_bf = shared[:].rearrange("p u c -> p (u c)").bitcast(BF16)
+        late_bf = [
+            sb("late_bf0", [P, QUARTER, PACK], BF16)[:],
+            as_bf[:, 1280:1792].rearrange("p (c t) -> p c t", t=PACK),
+        ]
+
+        def gather_quarter(v):
+            cols = slice(v * QUARTER, (v + 1) * QUARTER)
+            window = planes[1][3][:].indirect(pick[:, 8 * v : 8 * (v + 1)])
+            nc.vector.tensor_tensor(picked[1, 0][:, 3, cols], window, wgt_sb[:, cols], MULT)
+
+        def round_quarter(copy, v):
+            interleave(copy, late_bf[v], picked[1, 0][:, :, v * QUARTER : (v + 1) * QUARTER])
+
+        def quantize_quarter(v):
+            cols = slice(v * QUARTER, (v + 1) * QUARTER)
+            quantize(x_codes[:, 1, cols], x_sc[:, 1, cols], late_bf[v].rearrange("p c t -> p (c t)"))
+
         d_codes = sb("d_codes", [P, PASSES, R], U32)
         d_sc = sb("d_sc", [P, PASSES, R], U8)
         d_bf = [
-            sb("d_bf0", [P, PACK, P, PACK], BF16),
-            shared[:, 2:6, :].rearrange("p u c -> p (u c)").bitcast(BF16).rearrange("p (t m j) -> p t m j", t=PACK, j=PACK),
+            sb("d_bf0", [P, PACK, P, PACK], BF16)[:],
+            as_bf[:, 512:2560].rearrange("p (t m j) -> p t m j", t=PACK, j=PACK),
         ]
 
         def down_round(copy, a, m0, m1):
@@ -164,25 +177,26 @@ def tile_list_hboth_l_gelu_kernel(
 
         u_codes = sb("u_codes", [P, M], U32)
         u_sc = sb("u_sc", [P, M], U8)
-        UP_TAG = {1: "bias0", 2: "bias2", 3: "bias3"}
 
-        def up_prepare(copy, c):
-            n0, w = UP_CHUNKS[c]
-            grouped = sb(f"u_bf{c}", [P, w, PACK], BF16, tag=UP_TAG.get(c))
-            interleave(copy, grouped[:], up_raw[c][:])
-            quantize(u_codes[:, n0 : n0 + w], u_sc[:, n0 : n0 + w], grouped[:].rearrange("p n t -> p (n t)"))
+        def up_tile(n0, n1, tag):
+            return sb(f"u_bf{n0}", [P, n1 - n0, PACK], BF16, tag=tag)[:]
+
+        def up_prepare(copy, c, n0, n1, grouped):
+            base = UP_CHUNKS[c][0]
+            interleave(copy, grouped, up_raw[c][:, :, n0 - base : n1 - base])
+            quantize(u_codes[:, n0:n1], u_sc[:, n0:n1], grouped.rearrange("p n t -> p (n t)"))
 
         def d_quantize(a, t0, t1):
             m = slice(t0 * P, t1 * P)
             quantize(d_codes[:, a, m], d_sc[:, a, m], d_bf[a][:, t0:t1, :, :].rearrange("p t m j -> p (t m j)"))
 
         def warm_up():
-            spare = bank("d")
+            spare = bank("c")
             for w in range(6):
                 nc.tensor.matmul_mx(
                     out=spare[:, (w % 2) * HALF : (w % 2 + 1) * HALF],
-                    lhsT=d_codes[:, 0, 0:P].bitcast(FP8X4),
-                    lhsT_scale=d_sc[:, 0, 0:P],
+                    lhsT=d_codes[:, 1, 0:P].bitcast(FP8X4),
+                    lhsT_scale=d_sc[:, 1, 0:P],
                     rhs=x_codes[:, 0, 0:HALF].bitcast(FP8X4),
                     rhs_scale=x_sc[:, 0, 0:HALF],
                     start=True,
@@ -191,9 +205,13 @@ def tile_list_hboth_l_gelu_kernel(
 
         h_codes = sb("h_codes", [P, S], U32)
         h_sc = sb("h_sc", [P, S], U8)
-        h_bf = [sb(f"h_bf{h}", [P, HALF, PACK], BF16) for h in range(2)]
+        h_early = [
+            sb("h_bf0", [P, QUARTER, PACK], BF16)[:],
+            sb("h_bf1", [P, QUARTER, PACK], BF16)[:],
+        ]
 
-        def h_quarter(q, tag):
+
+        def h_quarter(q, tag, dst):
             acc = bank(tag)
             cols = slice(q * QUARTER, (q + 1) * QUARTER)
             for t in range(PACK):
@@ -208,16 +226,13 @@ def tile_list_hboth_l_gelu_kernel(
                         start=(a == 0),
                         stop=(a == PASSES - 1),
                     )
-            v = q % 2
-            dst = h_bf[q // 2][:, v * QUARTER : (v + 1) * QUARTER, :]
             nc.scalar.copy(dst, acc[:].rearrange("p (t n) -> p n t", t=PACK))
 
-        def h_quantize(j0, j1):
-            grouped = h_bf[j0 // HALF][:, j0 % HALF : j0 % HALF + j1 - j0, :]
+        def h_quantize(j0, j1, grouped):
             quantize(h_codes[:, j0:j1], h_sc[:, j0:j1], grouped.rearrange("p n t -> p (n t)"))
 
         act = {}
-        AFTER = {(1, 0): "up_raw1", (2, 0): "shared", (3, 0): "up_raw2", (5, 0): "up_raw3"}
+        AFTER = {(1, 0): "up_raw1", (2, 0): "shared", (3, 0): "up_raw2"}
 
         def act_half(n, h):
             if (n, h) not in act:
@@ -228,14 +243,14 @@ def tile_list_hboth_l_gelu_kernel(
             c = 0 if n * P < W4_CHUNKS[1][0] else 1
             off = n * P - W4_CHUNKS[c][0]
             rows = slice(n * P, (n + 1) * P)
-            for a in range(PASSES):
+            for a in (1, 0):
                 nc.tensor.matmul_mx(
                     out=acc,
                     lhsT=w4_codes[c][:, a, 2 * off : 2 * (off + P)].bitcast(FP4X4),
                     lhsT_scale=w4_sc[:, a, rows],
                     rhs=x_codes[:, a, cols].bitcast(FP8X4),
                     rhs_scale=x_sc[:, a, cols],
-                    start=(a == 0),
+                    start=(a == 1),
                     stop=False,
                 )
 
@@ -266,7 +281,7 @@ def tile_list_hboth_l_gelu_kernel(
 
         def y_half(n, h, tag="ring"):
             acc = bank(tag)
-            for v in range(2):
+            for v in (1, 0):
                 j0 = h * HALF + v * QUARTER
                 y_sum(acc[:, v * QUARTER : (v + 1) * QUARTER], n, slice(j0, j0 + QUARTER))
             gelu(n, h, slice(0, HALF), acc[:, 0:HALF])
@@ -284,48 +299,57 @@ def tile_list_hboth_l_gelu_kernel(
             gather(0, i, 0)
             gather(0, i, 1)
         x_round(on_scalar, 0, 0)
-        for i in range(PACK):
-            gather(1, i, 0)
-        x_round(on_scalar, 1, 0)
-        x_quantize(0, 0)
-        down_round(on_scalar, 0, 64, P)
-        down_round(on_vector, 0, 0, 64)
-        x_quantize(1, 0)
-        d_quantize(0, 0, 4)
-        warm_up()
-        down_round(on_scalar, 1, 84, P)
-        down_round(on_vector, 1, 0, 84)
-        d_quantize(1, 0, 4)
-        h_quarter(0, "a")
-        h_quarter(1, "b")
-        h_quantize(0, QUARTER)
-        h_quantize(QUARTER, HALF)
-        up_prepare(on_scalar, 0)
-        y_quarter(0, 0, "c")
-        y_quarter(0, 1, "d")
         x_round(on_scalar, 0, 1)
+        for i in range(PACK - 1):
+            gather(1, i, 0)
+            if i < EARLY:
+                gather(1, i, 1)
+        for a, m in enumerate(DOWN_ON_VECTOR):
+            if m < P:
+                down_round(on_scalar, a, m, P)
+            if m > 0:
+                down_round(on_vector, a, 0, m)
+            d_quantize(a, 0, PACK)
+        gather_quarter(0)
+        gather_quarter(1)
+        round_quarter(on_vector, 0)
+        round_quarter(on_scalar, 1)
+        quantize_quarter(0)
+        quantize_quarter(1)
+        x_quantize(0, 0)
         x_quantize(0, 1)
-        for i in range(PACK):
+        for i in range(EARLY, 2):
             gather(1, i, 1)
+        warm_up()
+        h_quarter(0, "a", h_early[0])
+        h_quarter(1, "b", h_early[1])
+        h_quantize(0, QUARTER, h_early[0])
+        h_quantize(QUARTER, HALF, h_early[1])
+        up_prepare(on_scalar, 0, 0, 128, up_tile(0, 128, "picked10"))
+        y_quarter(0, 0, "a")
+        y_quarter(0, 1, "b")
+        up_prepare(on_vector, 0, 128, 256, up_tile(128, 256, "h_bf1"))
+        gather(1, 3, 1)
+        gather(1, 2, 1)
         scatter(0, 0)
-        up_prepare(on_scalar, 1)
+        up_prepare(on_scalar, 1, 256, 512, up_tile(256, 512, "bias0"))
         y_half(1, 0)
         x_round(on_scalar, 1, 1)
         x_quantize(1, 1)
         y_half(2, 0)
-        up_prepare(on_scalar, 2)
+        up_prepare(on_scalar, 2, 512, 768, up_tile(512, 768, "bias2"))
         y_half(3, 0)
-        up_prepare(on_scalar, 3)
+        h_late = sb("h_late", [P, HALF, PACK], BF16, tag="bias3")
+        h_quarter(2, "c", h_late[:, 0:QUARTER, :])
+        h_quarter(3, "d", h_late[:, QUARTER:HALF, :])
+        h_quantize(HALF, S, h_late[:])
         y_half(4, 0)
-        h_quarter(2, "a")
-        h_quarter(3, "b")
-        h_quantize(HALF, S)
         y_half(5, 0)
-        y_half(6, 0)
-        y_half(7, 0, "b")
-        for n in range(1, ROW_TILES):
+        up_prepare(on_scalar, 3, 768, 1024, up_tile(768, 1024, "bias5"))
+        for n in range(1, OUT_TILES):
             scatter(n, 0)
-        for n in range(ROW_TILES):
-            y_half(n, 1)
-            scatter(n, 1)
-            store(n)
+        for n, h in [(0, 1), (1, 1), (2, 1), (3, 1), (6, 0), (7, 0), (4, 1), (5, 1), (6, 1), (7, 1)]:
+            y_half(n, h)
+            scatter(n, h)
+            if h == 1:
+                store(n)

@@ -15,6 +15,7 @@ U8 = mybir.dt.uint8
 FP8X4 = mybir.dt.float8_e4m3fn_x4
 FP4X4 = mybir.dt.float4_e2m1fn_x4
 MULT = mybir.AluOpType.mult
+IDENTITY = mybir.ActivationFunctionType.Identity
 GELU = mybir.ActivationFunctionType.Gelu_apprx_tanh
 
 P = 128
@@ -23,13 +24,17 @@ K_PASS = P * PACK
 PASSES = K // K_PASS
 HALF = S // 2
 QUARTER = S // 4
+GROUP = 16
 ROW_TILES = M // P
-OUT_TILES = 6
-EARLY = 1
-DOWN_ON_VECTOR = (64, 64)
-LOADS = "x00 x01 x02 x03 d0 x10 d1 x11 x12 x13"
-UP_CHUNKS = [(0, 256), (256, 256), (512, 256), (768, 256)]
-W4_CHUNKS = [(0, 640), (640, 384)]
+RING_BANKS = 4
+UP_CHUNK = 2 * P
+W4_SPLIT = (1 + RING_BANKS) * P
+W4_CHUNKS = [(0, W4_SPLIT), (W4_SPLIT, M - W4_SPLIT)]
+DOWN_ON_VECTOR = (64, 56)
+ZEROED_ON_VECTOR = 4
+WARM_PASSES = 6
+OWN_BIAS = (0, 1, 3, 4, 5)
+GELU_AFTER = {1: "up_raw1", 3: "up_raw2", 4: "picked11", 5: "up_raw3"}
 
 
 def tile_list_hboth_l_gelu_kernel(
@@ -44,30 +49,33 @@ def tile_list_hboth_l_gelu_kernel(
             return keep.tile(shape, dtype, name=name, tag=tag or name, align_bytes=64)
 
         def bank(tag):
-            return psum.tile([P, S], F32, name=tag, tag=tag, bufs=4 if tag == "ring" else 1)
+            return psum.tile([P, S], F32, name=tag, tag=tag, bufs=RING_BANKS if tag == "ring" else 1)
 
-        pick = keep.tile([P, S // 16], U16, name="pick")
-        place = keep.tile([P, S // 16], U16, name="place")
+        pick = keep.tile([P, S // GROUP], U16, name="pick")
+        place = keep.tile([P, S // GROUP], U16, name="place")
         wgt_sb = sb("wgt_sb", [P, S], F32)
         wgo_sb = sb("wgo_sb", [P, S], F32)
         planes = [[sb(f"plane{a}{i}", [P, T], F32) for i in range(PACK)] for a in range(PASSES)]
         down_raw = [sb(f"down_raw{a}", [P, PACK, R], F32) for a in range(PASSES)]
-        up_raw = [sb(f"up_raw{c}", [P, PACK, w], F32) for c, (n0, w) in enumerate(UP_CHUNKS)]
-        w4_codes = [sb(f"w4_codes{c}", [P, PASSES, 2 * w], U8) for c, (n0, w) in enumerate(W4_CHUNKS)]
+        up_raw = [sb(f"up_raw{c}", [P, PACK, UP_CHUNK], F32) for c in range(M // UP_CHUNK)]
+        w4_codes = [sb(f"w4_codes{c}", [P, PASSES, 2 * width], U8) for c, (n0, width) in enumerate(W4_CHUNKS)]
         w4_sc = sb("w4_sc", [P, PASSES, M], U8)
         b_rows = sb("b_rows", [P, P], F32)
         bias = sb("bias", [P, ROW_TILES], F32)
         ident = sb("ident", [P, P], F32)
-        warm = sb("warm", [P, 8], F32)
-        outs = [sb(f"out{o}", [P, T], F32) for o in range(OUT_TILES)]
+        table_load = sb("table_load", [P, 8], F32)
+        outs = [sb(f"out{n}", [P, T], F32) for n in range(ROW_TILES)]
 
         nc.gpsimd.memset(b_rows[:], 0.0)
         nc.scalar.dma_start(b_rows[0:ROW_TILES, :], b.rearrange("(c p) -> c p", p=P))
         make_identity(nc, ident[:])
-        nc.scalar.activation(warm[:, 0:1], ident[:, 0:1], GELU)
+        nc.scalar.activation(table_load[:, 0:1], ident[:, 0:1], GELU)
         nc.vector.memset(w4_sc[:].rearrange("p a n -> p (a n)").bitcast(U32), 0)
-        for o in range(OUT_TILES):
-            nc.vector.memset(outs[o][:].bitcast(I32), 0)
+        for n in range(ZEROED_ON_VECTOR):
+            nc.vector.memset(outs[n][:].bitcast(I32), 0)
+        for n in range(ZEROED_ON_VECTOR, ROW_TILES):
+            nc.vector.memset(outs[n][:, 0:8].bitcast(I32), 0)
+            nc.gpsimd.memset(outs[n][:].bitcast(I32), 0)
 
         def load_plane(a, i):
             rows = xT[a * K_PASS : (a + 1) * K_PASS, :].rearrange("(p i) t -> p i t", i=PACK)
@@ -78,126 +86,132 @@ def tile_list_hboth_l_gelu_kernel(
             nc.sync.dma_start(down_raw[a][:], rows)
 
         def load_up(c):
-            n0, w = UP_CHUNKS[c]
-            nc.sync.dma_start(up_raw[c][:], up.rearrange("(p j) n -> p j n", j=PACK)[:, :, n0 : n0 + w])
+            rows = up.rearrange("(p j) n -> p j n", j=PACK)
+            nc.sync.dma_start(up_raw[c][:], rows[:, :, c * UP_CHUNK : (c + 1) * UP_CHUNK])
 
         def load_w4(c):
-            n0, w = W4_CHUNKS[c]
-            src = w4_words[:, :, 2 * n0 : 2 * (n0 + w)].rearrange("a p n -> p a n")
+            n0, width = W4_CHUNKS[c]
+            src = w4_words[:, :, 2 * n0 : 2 * (n0 + width)].rearrange("a p n -> p a n")
             nc.sync.dma_start(w4_codes[c][:].bitcast(I32), src.bitcast(I32))
 
-        def load_scales():
+        def load_w4_scales():
             for q in range(4):
                 src = w4_scales[:, 4 * q : 4 * q + 4, :].rearrange("a r n -> r a n")
                 nc.sync.dma_start(w4_sc[32 * q : 32 * q + 4, :, :].bitcast(I32), src.bitcast(I32))
 
         nc.sync.dma_start(pick[:], offs)
         nc.sync.dma_start(wgt_sb[:], wgt)
-        for step in LOADS.split():
-            if step.startswith("x"):
-                load_plane(int(step[1]), int(step[2]))
-            else:
-                load_down(int(step[1]))
+        for i in range(PACK):
+            load_plane(0, i)
+        load_down(0)
+        load_plane(1, 0)
+        load_down(1)
+        for i in range(1, PACK):
+            load_plane(1, i)
         load_up(0)
-        load_scales()
+        load_w4_scales()
         load_w4(0)
+        load_up(1)
         nc.sync.dma_start(place[:], offs2)
         nc.sync.dma_start(wgo_sb[:], wgo)
-        load_up(1)
         load_up(2)
         load_w4(1)
         load_up(3)
 
-        b_bank = bank("d")
-        nc.tensor.transpose(b_bank[:, 0:P], b_rows[:], ident[:])
-        nc.scalar.copy(bias[:], b_bank[:, 0:ROW_TILES])
-        own_bias = {n: sb(f"bias{n}", [P, 1], F32) for n in (0, 1, 2, 3, 5)}
-        for n in own_bias:
-            nc.scalar.copy(own_bias[n][:], b_bank[:, n : n + 1])
+        held = [bank(tag) for tag in "cabd"]
+        for tenant in held:
+            nc.tensor.transpose(tenant[:, 0:P], b_rows[:], ident[:])
+        nc.scalar.copy(bias[:], held[0][:, 0:ROW_TILES])
+        own_bias = {n: sb(f"bias{n}", [P, 1], F32) for n in OWN_BIAS}
+        for n in OWN_BIAS:
+            nc.scalar.copy(own_bias[n][:], held[0][:, n : n + 1])
 
         def interleave(copy, dst, src):
             copy(
-                dst.rearrange("p (c i) t -> p c t i", i=4),
-                src.rearrange("p t (c i) -> p c t i", i=4),
+                dst.rearrange("p (c e) t -> p c t e", e=4),
+                src.rearrange("p t (c e) -> p c t e", e=4),
             )
 
-        def quantize(codes, scales, grouped):
-            nc.vector.quantize_mx(out=codes.bitcast(FP8X4), scales=scales, in_=grouped)
+        def quantize(codes, scales, rounded):
+            nc.vector.quantize_mx(out=codes.bitcast(FP8X4), scales=scales, in_=rounded)
 
-        x_codes = sb("x_codes", [P, PASSES, S], U32)
+        x_codes = {(a, h): sb(f"x_codes{a}{h}", [P, HALF], U32)[:] for a, h in [(0, 0), (1, 0), (1, 1)]}
         x_sc = sb("x_sc", [P, PASSES, S], U8)
-        shared = sb("shared", [P, PACK + 1, HALF], F32)
-        picked = {(1, 1): shared[:, 0:PACK, :]}
+        picked11 = sb("picked11", [P, PACK, HALF], F32)
+        picked = {(1, 1): picked11[:]}
         x_bf = {}
 
-        def gather(a, i, h):
-            if (a, h) not in picked:
-                picked[a, h] = sb(f"picked{a}{h}", [P, PACK, HALF], F32, tag={}.get((a, h)))[:]
-            window = planes[a][i][:].indirect(pick[:, 16 * h : 16 * (h + 1)])
-            nc.vector.tensor_tensor(picked[a, h][:, i, :], window, wgt_sb[:, h * HALF : (h + 1) * HALF], MULT)
+        def x_words(a, cols):
+            h = cols.start // HALF
+            return x_codes[a, h][:, cols.start - h * HALF : cols.stop - h * HALF]
 
-        def x_round(copy, a, h):
-            x_bf[a, h] = sb(f"x_bf{a}{h}", [P, HALF, PACK], BF16, tag={(1, 1): "bias1"}.get((a, h)))
-            interleave(copy, x_bf[a, h][:], picked[a, h])
+        def gather_columns(a, i, h, j0, j1):
+            if (a, h) not in picked:
+                picked[a, h] = sb(f"picked{a}{h}", [P, PACK, HALF], F32)[:]
+            window = planes[a][i][:].indirect(pick[:, j0 // GROUP : j1 // GROUP])
+            dst = picked[a, h][:, i, j0 - h * HALF : j1 - h * HALF]
+            nc.vector.tensor_tensor(dst, window, wgt_sb[:, j0:j1], MULT)
+
+        def gather(a, i, h):
+            gather_columns(a, i, h, h * HALF, (h + 1) * HALF)
+
+        def x_round(a, h, tag=None):
+            x_bf[a, h] = sb(f"x_bf{a}{h}", [P, HALF, PACK], BF16, tag=tag)
+            interleave(nc.scalar.copy, x_bf[a, h][:], picked[a, h])
 
         def x_quantize(a, h):
             cols = slice(h * HALF, (h + 1) * HALF)
-            quantize(x_codes[:, a, cols], x_sc[:, a, cols], x_bf[a, h][:].rearrange("p c t -> p (c t)"))
+            quantize(x_words(a, cols), x_sc[:, a, cols], x_bf[a, h][:].rearrange("p c t -> p (c t)"))
 
-        as_bf = shared[:].rearrange("p u c -> p (u c)").bitcast(BF16)
-        late_bf = [
-            sb("late_bf0", [P, QUARTER, PACK], BF16)[:],
-            as_bf[:, 1280:1792].rearrange("p (c t) -> p c t", t=PACK),
+        border = 3 * 2 * HALF
+        across = picked11[:].rearrange("p i c -> p (i c)").bitcast(BF16)[:, border - HALF : border + HALF]
+        quarter_bf = [
+            sb("quarter_bf0", [P, QUARTER, PACK], BF16)[:],
+            across.rearrange("p (c t) -> p c t", t=PACK),
         ]
 
-        def gather_quarter(v):
+        def quarter_round(copy, v):
+            interleave(copy, quarter_bf[v], picked[1, 0][:, :, v * QUARTER : (v + 1) * QUARTER])
+
+        def quarter_quantize(v):
             cols = slice(v * QUARTER, (v + 1) * QUARTER)
-            window = planes[1][3][:].indirect(pick[:, 8 * v : 8 * (v + 1)])
-            nc.vector.tensor_tensor(picked[1, 0][:, 3, cols], window, wgt_sb[:, cols], MULT)
+            quantize(x_words(1, cols), x_sc[:, 1, cols], quarter_bf[v].rearrange("p c t -> p (c t)"))
 
-        def round_quarter(copy, v):
-            interleave(copy, late_bf[v], picked[1, 0][:, :, v * QUARTER : (v + 1) * QUARTER])
-
-        def quantize_quarter(v):
-            cols = slice(v * QUARTER, (v + 1) * QUARTER)
-            quantize(x_codes[:, 1, cols], x_sc[:, 1, cols], late_bf[v].rearrange("p c t -> p (c t)"))
-
-        d_codes = sb("d_codes", [P, PASSES, R], U32)
+        d_codes = {}
         d_sc = sb("d_sc", [P, PASSES, R], U8)
-        d_bf = [
-            sb("d_bf0", [P, PACK, P, PACK], BF16)[:],
-            as_bf[:, 512:2560].rearrange("p (t m j) -> p t m j", t=PACK, j=PACK),
-        ]
+        d_bf = [sb(f"d_bf{a}", [P, PACK, P, PACK], BF16) for a in range(PASSES)]
 
-        def down_round(copy, a, m0, m1):
-            copy(
-                d_bf[a][:, :, m0:m1, :].rearrange("p t m j -> p m j t"),
-                down_raw[a][:, :, PACK * m0 : PACK * m1].rearrange("p j (m t) -> p m j t", t=PACK),
-            )
+        def down_round(a):
+            split = DOWN_ON_VECTOR[a]
+            for copy, m0, m1 in [(nc.scalar.copy, split, P), (nc.vector.tensor_copy, 0, split)]:
+                copy(
+                    d_bf[a][:, :, m0:m1, :].rearrange("p t m j -> p m j t"),
+                    down_raw[a][:, :, PACK * m0 : PACK * m1].rearrange("p j (m t) -> p m j t", t=PACK),
+                )
+
+        def down_quantize(a):
+            quantize(d_codes[a], d_sc[:, a, :], d_bf[a][:].rearrange("p t m j -> p (t m j)"))
 
         u_codes = sb("u_codes", [P, M], U32)
         u_sc = sb("u_sc", [P, M], U8)
 
-        def up_tile(n0, n1, tag):
-            return sb(f"u_bf{n0}", [P, n1 - n0, PACK], BF16, tag=tag)[:]
+        def up_prepare(copy, n0, n1, after):
+            c = n0 // UP_CHUNK
+            rounded = sb(f"u_bf{n0}", [P, n1 - n0, PACK], BF16, tag=after)
+            interleave(copy, rounded[:], up_raw[c][:, :, n0 - c * UP_CHUNK : n1 - c * UP_CHUNK])
+            quantize(u_codes[:, n0:n1], u_sc[:, n0:n1], rounded[:].rearrange("p n t -> p (n t)"))
 
-        def up_prepare(copy, c, n0, n1, grouped):
-            base = UP_CHUNKS[c][0]
-            interleave(copy, grouped, up_raw[c][:, :, n0 - base : n1 - base])
-            quantize(u_codes[:, n0:n1], u_sc[:, n0:n1], grouped.rearrange("p n t -> p (n t)"))
-
-        def d_quantize(a, t0, t1):
-            m = slice(t0 * P, t1 * P)
-            quantize(d_codes[:, a, m], d_sc[:, a, m], d_bf[a][:, t0:t1, :, :].rearrange("p t m j -> p (t m j)"))
+        def up_chunk(c, after):
+            up_prepare(nc.scalar.copy, c * UP_CHUNK, (c + 1) * UP_CHUNK, after)
 
         def warm_up():
             spare = bank("c")
-            for w in range(6):
+            for w in range(WARM_PASSES):
                 nc.tensor.matmul_mx(
                     out=spare[:, (w % 2) * HALF : (w % 2 + 1) * HALF],
-                    lhsT=d_codes[:, 1, 0:P].bitcast(FP8X4),
-                    lhsT_scale=d_sc[:, 1, 0:P],
-                    rhs=x_codes[:, 0, 0:HALF].bitcast(FP8X4),
+                    lhsT=d_codes[0][:, 0:P].bitcast(FP8X4),
+                    lhsT_scale=d_sc[:, 0, 0:P],
+                    rhs=x_codes[0, 0].bitcast(FP8X4),
                     rhs_scale=x_sc[:, 0, 0:HALF],
                     start=True,
                     stop=True,
@@ -205,11 +219,6 @@ def tile_list_hboth_l_gelu_kernel(
 
         h_codes = sb("h_codes", [P, S], U32)
         h_sc = sb("h_sc", [P, S], U8)
-        h_early = [
-            sb("h_bf0", [P, QUARTER, PACK], BF16)[:],
-            sb("h_bf1", [P, QUARTER, PACK], BF16)[:],
-        ]
-
 
         def h_quarter(q, tag, dst):
             acc = bank(tag)
@@ -219,43 +228,32 @@ def tile_list_hboth_l_gelu_kernel(
                 for a in range(PASSES):
                     nc.tensor.matmul_mx(
                         out=acc[:, m],
-                        lhsT=d_codes[:, a, m].bitcast(FP8X4),
+                        lhsT=d_codes[a][:, m].bitcast(FP8X4),
                         lhsT_scale=d_sc[:, a, m],
-                        rhs=x_codes[:, a, cols].bitcast(FP8X4),
+                        rhs=x_words(a, cols).bitcast(FP8X4),
                         rhs_scale=x_sc[:, a, cols],
                         start=(a == 0),
                         stop=(a == PASSES - 1),
                     )
             nc.scalar.copy(dst, acc[:].rearrange("p (t n) -> p n t", t=PACK))
 
-        def h_quantize(j0, j1, grouped):
-            quantize(h_codes[:, j0:j1], h_sc[:, j0:j1], grouped.rearrange("p n t -> p (n t)"))
+        def h_quantize(j0, j1, rounded):
+            quantize(h_codes[:, j0:j1], h_sc[:, j0:j1], rounded.rearrange("p n t -> p (n t)"))
 
-        act = {}
-        AFTER = {(1, 0): "up_raw1", (2, 0): "shared", (3, 0): "up_raw2"}
-
-        def act_half(n, h):
-            if (n, h) not in act:
-                act[n, h] = sb(f"act{n}{h}", [P, HALF], F32, tag=AFTER.get((n, h)))
-            return act[n, h]
-
-        def y_base(acc, n, cols):
-            c = 0 if n * P < W4_CHUNKS[1][0] else 1
-            off = n * P - W4_CHUNKS[c][0]
+        def y_sum(acc, n, cols):
+            c = 0 if n * P < W4_SPLIT else 1
+            first = n * P - W4_CHUNKS[c][0]
             rows = slice(n * P, (n + 1) * P)
             for a in (1, 0):
                 nc.tensor.matmul_mx(
                     out=acc,
-                    lhsT=w4_codes[c][:, a, 2 * off : 2 * (off + P)].bitcast(FP4X4),
+                    lhsT=w4_codes[c][:, a, 2 * first : 2 * (first + P)].bitcast(FP4X4),
                     lhsT_scale=w4_sc[:, a, rows],
-                    rhs=x_codes[:, a, cols].bitcast(FP8X4),
+                    rhs=x_words(a, cols).bitcast(FP8X4),
                     rhs_scale=x_sc[:, a, cols],
                     start=(a == 1),
                     stop=False,
                 )
-
-        def y_branch(acc, n, cols):
-            rows = slice(n * P, (n + 1) * P)
             nc.tensor.matmul_mx(
                 out=acc,
                 lhsT=u_codes[:, rows].bitcast(FP8X4),
@@ -266,21 +264,22 @@ def tile_list_hboth_l_gelu_kernel(
                 stop=True,
             )
 
-        def y_sum(acc, n, cols):
-            y_base(acc, n, cols)
-            y_branch(acc, n, cols)
+        act = {}
 
         def gelu(n, h, dst_cols, acc):
-            nc.scalar.activation(act_half(n, h)[:, dst_cols], acc, GELU, bias=own_bias[n][:] if h == 0 and n in own_bias else bias[:, n : n + 1])
+            if (n, h) not in act:
+                act[n, h] = sb(f"act{n}{h}", [P, HALF], F32, tag=GELU_AFTER.get(n) if h == 0 else None)
+            row_bias = own_bias[n][:] if h == 0 and n in OWN_BIAS else bias[:, n : n + 1]
+            nc.scalar.activation(act[n, h][:, dst_cols], acc, GELU, bias=row_bias)
 
-        def y_quarter(n, v, tag):
+        def y_first_tile(v, tag):
             acc = bank(tag)
             cols = slice(v * QUARTER, (v + 1) * QUARTER)
-            y_sum(acc[:, 0:QUARTER], n, cols)
-            gelu(n, 0, cols, acc[:, 0:QUARTER])
+            y_sum(acc[:, 0:QUARTER], 0, cols)
+            gelu(0, 0, cols, acc[:, 0:QUARTER])
 
-        def y_half(n, h, tag="ring"):
-            acc = bank(tag)
+        def y_half(n, h):
+            acc = bank("ring")
             for v in (1, 0):
                 j0 = h * HALF + v * QUARTER
                 y_sum(acc[:, v * QUARTER : (v + 1) * QUARTER], n, slice(j0, j0 + QUARTER))
@@ -288,68 +287,75 @@ def tile_list_hboth_l_gelu_kernel(
 
         def scatter(n, h):
             cols = slice(h * HALF, (h + 1) * HALF)
-            window = outs[n % OUT_TILES][:].indirect(place[:, 16 * h : 16 * (h + 1)])
+            window = outs[n][:].indirect(place[:, cols.start // GROUP : cols.stop // GROUP])
             nc.vector.tensor_tensor(window, act[n, h][:], wgo_sb[:, cols], MULT)
 
-        def store(n):
-            nc.sync.dma_start(out[n * P : (n + 1) * P, :], outs[n % OUT_TILES][:])
-
-        on_scalar, on_vector = nc.scalar.copy, nc.vector.tensor_copy
         for i in range(PACK):
             gather(0, i, 0)
             gather(0, i, 1)
-        x_round(on_scalar, 0, 0)
-        x_round(on_scalar, 0, 1)
-        for i in range(PACK - 1):
-            gather(1, i, 0)
-            if i < EARLY:
-                gather(1, i, 1)
-        for a, m in enumerate(DOWN_ON_VECTOR):
-            if m < P:
-                down_round(on_scalar, a, m, P)
-            if m > 0:
-                down_round(on_vector, a, 0, m)
-            d_quantize(a, 0, PACK)
-        gather_quarter(0)
-        gather_quarter(1)
-        round_quarter(on_vector, 0)
-        round_quarter(on_scalar, 1)
-        quantize_quarter(0)
-        quantize_quarter(1)
+        x_round(0, 0)
+        x_round(0, 1)
+        down_round(0)
         x_quantize(0, 0)
+        gather(1, 0, 0)
+        gather(1, 0, 1)
+        codes0 = sb("codes0", [P, HALF + R], U32, tag="plane10")
+        x_codes[0, 1], d_codes[0] = codes0[:, 0:HALF], codes0[:, HALF : HALF + R]
         x_quantize(0, 1)
-        for i in range(EARLY, 2):
-            gather(1, i, 1)
+        down_quantize(0)
+
+        down_round(1)
+        gather(1, 1, 0)
+        marks = [sb(f"mark{w}", [P, 1], F32) for w in range(len(held))]
+        for mark, tenant in zip(marks, held):
+            nc.scalar.activation(
+                mark[:], tenant[:, ROW_TILES : ROW_TILES + 1], IDENTITY, bias=picked[1, 0][:, 1, 0:1]
+            )
+        gather(1, 1, 1)
+        d_codes[1] = sb("d_codes1", [P, R], U32, tag="mark0")[:]
+        down_quantize(1)
+        gather(1, 2, 0)
+
+        gather_columns(1, 3, 0, 0, QUARTER)
+        gather_columns(1, 3, 0, QUARTER, HALF)
+        quarter_round(nc.vector.tensor_copy, 0)
+        quarter_round(nc.scalar.copy, 1)
+        quarter_quantize(0)
+        quarter_quantize(1)
         warm_up()
-        h_quarter(0, "a", h_early[0])
-        h_quarter(1, "b", h_early[1])
-        h_quantize(0, QUARTER, h_early[0])
-        h_quantize(QUARTER, HALF, h_early[1])
-        up_prepare(on_scalar, 0, 0, 128, up_tile(0, 128, "picked10"))
-        y_quarter(0, 0, "a")
-        y_quarter(0, 1, "b")
-        up_prepare(on_vector, 0, 128, 256, up_tile(128, 256, "h_bf1"))
+        h_first = [sb(f"h_bf{v}", [P, QUARTER, PACK], BF16)[:] for v in range(2)]
+        h_quarter(0, "a", h_first[0])
+        h_quarter(1, "b", h_first[1])
+        h_quantize(0, QUARTER, h_first[0])
+        h_quantize(QUARTER, HALF, h_first[1])
+        up_prepare(nc.scalar.copy, 0, P, after="picked10")
+        y_first_tile(0, "a")
+        y_first_tile(1, "b")
+        up_prepare(nc.vector.tensor_copy, P, UP_CHUNK, after="h_bf1")
         gather(1, 3, 1)
         gather(1, 2, 1)
         scatter(0, 0)
-        up_prepare(on_scalar, 1, 256, 512, up_tile(256, 512, "bias0"))
+
+        up_chunk(1, after="bias0")
         y_half(1, 0)
-        x_round(on_scalar, 1, 1)
-        x_quantize(1, 1)
         y_half(2, 0)
-        up_prepare(on_scalar, 2, 512, 768, up_tile(512, 768, "bias2"))
+        up_chunk(2, after="bias1")
         y_half(3, 0)
-        h_late = sb("h_late", [P, HALF, PACK], BF16, tag="bias3")
-        h_quarter(2, "c", h_late[:, 0:QUARTER, :])
-        h_quarter(3, "d", h_late[:, QUARTER:HALF, :])
-        h_quantize(HALF, S, h_late[:])
+        x_round(1, 1, tag="bias3")
+        x_quantize(1, 1)
         y_half(4, 0)
+        up_chunk(3, after="bias4")
         y_half(5, 0)
-        up_prepare(on_scalar, 3, 768, 1024, up_tile(768, 1024, "bias5"))
-        for n in range(1, OUT_TILES):
+        h_second = sb("h_second", [P, HALF, PACK], BF16, tag="bias5")
+        h_quarter(2, "c", h_second[:, 0:QUARTER, :])
+        h_quarter(3, "d", h_second[:, QUARTER:HALF, :])
+        h_quantize(HALF, S, h_second[:])
+        y_half(6, 0)
+        y_half(7, 0)
+        for n in range(1, ROW_TILES):
             scatter(n, 0)
-        for n, h in [(0, 1), (1, 1), (2, 1), (3, 1), (6, 0), (7, 0), (4, 1), (5, 1), (6, 1), (7, 1)]:
-            y_half(n, h)
-            scatter(n, h)
-            if h == 1:
-                store(n)
+
+        for n in range(ROW_TILES):
+            y_half(n, 1)
+            scatter(n, 1)
+            nc.sync.dma_start(out[n * P : (n + 1) * P, :], outs[n][:])

@@ -15,7 +15,6 @@ U8 = mybir.dt.uint8
 FP8X4 = mybir.dt.float8_e4m3fn_x4
 FP4X4 = mybir.dt.float4_e2m1fn_x4
 MULT = mybir.AluOpType.mult
-IDENTITY = mybir.ActivationFunctionType.Identity
 GELU = mybir.ActivationFunctionType.Gelu_apprx_tanh
 
 P = 128
@@ -26,15 +25,10 @@ HALF = S // 2
 QUARTER = S // 4
 GROUP = 16
 ROW_TILES = M // P
-RING_BANKS = 4
+RING_BANKS = 6
 UP_CHUNK = 2 * P
-W4_SPLIT = (1 + RING_BANKS) * P
-W4_CHUNKS = [(0, W4_SPLIT), (W4_SPLIT, M - W4_SPLIT)]
-DOWN_ON_VECTOR = (64, 56)
-ZEROED_ON_VECTOR = 4
-WARM_PASSES = 6
-OWN_BIAS = (0, 1, 3, 4, 5)
-GELU_AFTER = {1: "up_raw1", 3: "up_raw2", 4: "picked11", 5: "up_raw3"}
+W4_CHUNKS = [(0, UP_CHUNK), (UP_CHUNK, M - UP_CHUNK)]
+DOWN_ON_VECTOR = (72, 80)
 
 
 def tile_list_hboth_l_gelu_kernel(
@@ -54,7 +48,7 @@ def tile_list_hboth_l_gelu_kernel(
         pick = keep.tile([P, S // GROUP], U16, name="pick")
         place = keep.tile([P, S // GROUP], U16, name="place")
         wgt_sb = sb("wgt_sb", [P, S], F32)
-        wgo_sb = sb("wgo_sb", [P, S], F32)
+        wgo_sb = [sb(f"wgo_sb{h}", [P, HALF], F32) for h in range(2)]
         planes = [[sb(f"plane{a}{i}", [P, T], F32) for i in range(PACK)] for a in range(PASSES)]
         down_raw = [sb(f"down_raw{a}", [P, PACK, R], F32) for a in range(PASSES)]
         up_raw = [sb(f"up_raw{c}", [P, PACK, UP_CHUNK], F32) for c in range(M // UP_CHUNK)]
@@ -70,11 +64,8 @@ def tile_list_hboth_l_gelu_kernel(
         nc.scalar.dma_start(b_rows[0:ROW_TILES, :], b.rearrange("(c p) -> c p", p=P))
         make_identity(nc, ident[:])
         nc.scalar.activation(table_load[:, 0:1], ident[:, 0:1], GELU)
-        nc.vector.memset(w4_sc[:].rearrange("p a n -> p (a n)").bitcast(U32), 0)
-        for n in range(ZEROED_ON_VECTOR):
-            nc.vector.memset(outs[n][:].bitcast(I32), 0)
-        for n in range(ZEROED_ON_VECTOR, ROW_TILES):
-            nc.vector.memset(outs[n][:, 0:8].bitcast(I32), 0)
+        nc.gpsimd.memset(w4_sc[:].rearrange("p a n -> p (a n)").bitcast(U32), 0)
+        for n in range(ROW_TILES):
             nc.gpsimd.memset(outs[n][:].bitcast(I32), 0)
 
         def load_plane(a, i):
@@ -99,32 +90,30 @@ def tile_list_hboth_l_gelu_kernel(
                 src = w4_scales[:, 4 * q : 4 * q + 4, :].rearrange("a r n -> r a n")
                 nc.sync.dma_start(w4_sc[32 * q : 32 * q + 4, :, :].bitcast(I32), src.bitcast(I32))
 
+        def load_wgo(h):
+            nc.sync.dma_start(wgo_sb[h][:], wgo[:, h * HALF : (h + 1) * HALF])
+
         nc.sync.dma_start(pick[:], offs)
         nc.sync.dma_start(wgt_sb[:], wgt)
-        for i in range(PACK):
-            load_plane(0, i)
+        for a in range(PASSES):
+            for i in range(PACK):
+                load_plane(a, i)
         load_down(0)
-        load_plane(1, 0)
         load_down(1)
-        for i in range(1, PACK):
-            load_plane(1, i)
         load_up(0)
         load_w4_scales()
         load_w4(0)
-        load_up(1)
         nc.sync.dma_start(place[:], offs2)
-        nc.sync.dma_start(wgo_sb[:], wgo)
-        load_up(2)
+        load_wgo(0)
+        load_up(1)
         load_w4(1)
+        load_up(2)
         load_up(3)
+        load_wgo(1)
 
-        held = [bank(tag) for tag in "cabd"]
-        for tenant in held:
-            nc.tensor.transpose(tenant[:, 0:P], b_rows[:], ident[:])
-        nc.scalar.copy(bias[:], held[0][:, 0:ROW_TILES])
-        own_bias = {n: sb(f"bias{n}", [P, 1], F32) for n in OWN_BIAS}
-        for n in OWN_BIAS:
-            nc.scalar.copy(own_bias[n][:], held[0][:, n : n + 1])
+        turned = bank("a")
+        nc.tensor.transpose(turned[:, 0:P], b_rows[:], ident[:])
+        nc.scalar.copy(bias[:], turned[:, 0:ROW_TILES])
 
         def interleave(copy, dst, src):
             copy(
@@ -135,49 +124,29 @@ def tile_list_hboth_l_gelu_kernel(
         def quantize(codes, scales, rounded):
             nc.vector.quantize_mx(out=codes.bitcast(FP8X4), scales=scales, in_=rounded)
 
-        x_codes = {(a, h): sb(f"x_codes{a}{h}", [P, HALF], U32)[:] for a, h in [(0, 0), (1, 0), (1, 1)]}
+        picked = [sb(f"picked{a}", [P, PACK, S], F32) for a in range(PASSES)]
         x_sc = sb("x_sc", [P, PASSES, S], U8)
-        picked11 = sb("picked11", [P, PACK, HALF], F32)
-        picked = {(1, 1): picked11[:]}
+        x_codes = {}
+
         x_bf = {}
 
-        def x_words(a, cols):
-            h = cols.start // HALF
-            return x_codes[a, h][:, cols.start - h * HALF : cols.stop - h * HALF]
-
-        def gather_columns(a, i, h, j0, j1):
-            if (a, h) not in picked:
-                picked[a, h] = sb(f"picked{a}{h}", [P, PACK, HALF], F32)[:]
+        def gather(a, i, j0=0, j1=S):
             window = planes[a][i][:].indirect(pick[:, j0 // GROUP : j1 // GROUP])
-            dst = picked[a, h][:, i, j0 - h * HALF : j1 - h * HALF]
-            nc.vector.tensor_tensor(dst, window, wgt_sb[:, j0:j1], MULT)
-
-        def gather(a, i, h):
-            gather_columns(a, i, h, h * HALF, (h + 1) * HALF)
+            nc.vector.tensor_tensor(picked[a][:, i, j0:j1], window, wgt_sb[:, j0:j1], MULT)
 
         def x_round(a, h, tag=None):
             x_bf[a, h] = sb(f"x_bf{a}{h}", [P, HALF, PACK], BF16, tag=tag)
-            interleave(nc.scalar.copy, x_bf[a, h][:], picked[a, h])
+            interleave(nc.scalar.copy, x_bf[a, h][:], picked[a][:, :, h * HALF : (h + 1) * HALF])
 
-        def x_quantize(a, h):
+        def x_quantize(a, h, tag=None):
+            x_codes[a, h] = sb(f"x_codes{a}{h}", [P, HALF], U32, tag=tag)
             cols = slice(h * HALF, (h + 1) * HALF)
-            quantize(x_words(a, cols), x_sc[:, a, cols], x_bf[a, h][:].rearrange("p c t -> p (c t)"))
+            quantize(x_codes[a, h][:], x_sc[:, a, cols], x_bf[a, h][:].rearrange("p c t -> p (c t)"))
 
-        border = 3 * 2 * HALF
-        across = picked11[:].rearrange("p i c -> p (i c)").bitcast(BF16)[:, border - HALF : border + HALF]
-        quarter_bf = [
-            sb("quarter_bf0", [P, QUARTER, PACK], BF16)[:],
-            across.rearrange("p (c t) -> p c t", t=PACK),
-        ]
+        def x_words(a, j):
+            return x_codes[a, j // HALF][:, j % HALF : j % HALF + QUARTER].bitcast(FP8X4)
 
-        def quarter_round(copy, v):
-            interleave(copy, quarter_bf[v], picked[1, 0][:, :, v * QUARTER : (v + 1) * QUARTER])
-
-        def quarter_quantize(v):
-            cols = slice(v * QUARTER, (v + 1) * QUARTER)
-            quantize(x_words(1, cols), x_sc[:, 1, cols], quarter_bf[v].rearrange("p c t -> p (c t)"))
-
-        d_codes = {}
+        d_codes = [sb(f"d_codes{a}", [P, R], U32) for a in range(PASSES)]
         d_sc = sb("d_sc", [P, PASSES, R], U8)
         d_bf = [sb(f"d_bf{a}", [P, PACK, P, PACK], BF16) for a in range(PASSES)]
 
@@ -189,173 +158,124 @@ def tile_list_hboth_l_gelu_kernel(
                     down_raw[a][:, :, PACK * m0 : PACK * m1].rearrange("p j (m t) -> p m j t", t=PACK),
                 )
 
-        def down_quantize(a):
-            quantize(d_codes[a], d_sc[:, a, :], d_bf[a][:].rearrange("p t m j -> p (t m j)"))
+        def down_quantize(a, t0, t1):
+            m = slice(t0 * P, t1 * P)
+            quantize(d_codes[a][:, m], d_sc[:, a, m], d_bf[a][:, t0:t1].rearrange("p t m j -> p (t m j)"))
 
         u_codes = sb("u_codes", [P, M], U32)
         u_sc = sb("u_sc", [P, M], U8)
 
-        def up_prepare(copy, n0, n1, after):
-            c = n0 // UP_CHUNK
-            rounded = sb(f"u_bf{n0}", [P, n1 - n0, PACK], BF16, tag=after)
-            interleave(copy, rounded[:], up_raw[c][:, :, n0 - c * UP_CHUNK : n1 - c * UP_CHUNK])
-            quantize(u_codes[:, n0:n1], u_sc[:, n0:n1], rounded[:].rearrange("p n t -> p (n t)"))
-
-        def up_chunk(c, after):
-            up_prepare(nc.scalar.copy, c * UP_CHUNK, (c + 1) * UP_CHUNK, after)
-
-        def warm_up():
-            spare = bank("c")
-            for w in range(WARM_PASSES):
-                nc.tensor.matmul_mx(
-                    out=spare[:, (w % 2) * HALF : (w % 2 + 1) * HALF],
-                    lhsT=d_codes[0][:, 0:P].bitcast(FP8X4),
-                    lhsT_scale=d_sc[:, 0, 0:P],
-                    rhs=x_codes[0, 0].bitcast(FP8X4),
-                    rhs_scale=x_sc[:, 0, 0:HALF],
-                    start=True,
-                    stop=True,
-                )
+        def up_chunk(copy, c):
+            cols = slice(c * UP_CHUNK, (c + 1) * UP_CHUNK)
+            rounded = sb(f"u_bf{c}", [P, UP_CHUNK, PACK], BF16)
+            interleave(copy, rounded[:], up_raw[c][:])
+            quantize(u_codes[:, cols], u_sc[:, cols], rounded[:].rearrange("p n t -> p (n t)"))
 
         h_codes = sb("h_codes", [P, S], U32)
         h_sc = sb("h_sc", [P, S], U8)
 
-        def h_quarter(q, tag, dst):
-            acc = bank(tag)
+        def h_pass(acc, q, a):
             cols = slice(q * QUARTER, (q + 1) * QUARTER)
             for t in range(PACK):
                 m = slice(t * P, (t + 1) * P)
-                for a in range(PASSES):
-                    nc.tensor.matmul_mx(
-                        out=acc[:, m],
-                        lhsT=d_codes[a][:, m].bitcast(FP8X4),
-                        lhsT_scale=d_sc[:, a, m],
-                        rhs=x_words(a, cols).bitcast(FP8X4),
-                        rhs_scale=x_sc[:, a, cols],
-                        start=(a == 0),
-                        stop=(a == PASSES - 1),
-                    )
+                nc.tensor.matmul_mx(
+                    out=acc[:, m],
+                    lhsT=d_codes[a][:, m].bitcast(FP8X4),
+                    lhsT_scale=d_sc[:, a, m],
+                    rhs=x_words(a, cols.start),
+                    rhs_scale=x_sc[:, a, cols],
+                    start=(a == 0 and t == 0),
+                    stop=(a == PASSES - 1 and t == PACK - 1),
+                )
+
+        def h_round(dst, acc):
             nc.scalar.copy(dst, acc[:].rearrange("p (t n) -> p n t", t=PACK))
 
         def h_quantize(j0, j1, rounded):
             quantize(h_codes[:, j0:j1], h_sc[:, j0:j1], rounded.rearrange("p n t -> p (n t)"))
 
-        def y_sum(acc, n, cols):
-            c = 0 if n * P < W4_SPLIT else 1
+        def y_tile(n, j0, j1, bank_tag, act_tag=None):
+            acc = bank(bank_tag)
+            c = 0 if n * P < UP_CHUNK else 1
             first = n * P - W4_CHUNKS[c][0]
             rows = slice(n * P, (n + 1) * P)
-            for a in (1, 0):
-                nc.tensor.matmul_mx(
-                    out=acc,
-                    lhsT=w4_codes[c][:, a, 2 * first : 2 * (first + P)].bitcast(FP4X4),
-                    lhsT_scale=w4_sc[:, a, rows],
-                    rhs=x_words(a, cols).bitcast(FP8X4),
-                    rhs_scale=x_sc[:, a, cols],
-                    start=(a == 1),
-                    stop=False,
-                )
+            for a in range(PASSES):
+                for j in range(j0, j1, QUARTER):
+                    nc.tensor.matmul_mx(
+                        out=acc[:, j - j0 : j - j0 + QUARTER],
+                        lhsT=w4_codes[c][:, a, 2 * first : 2 * (first + P)].bitcast(FP4X4),
+                        lhsT_scale=w4_sc[:, a, rows],
+                        rhs=x_words(a, j),
+                        rhs_scale=x_sc[:, a, j : j + QUARTER],
+                        start=(a == 0 and j == j0),
+                        stop=False,
+                    )
             nc.tensor.matmul_mx(
-                out=acc,
+                out=acc[:, 0 : j1 - j0],
                 lhsT=u_codes[:, rows].bitcast(FP8X4),
                 lhsT_scale=u_sc[:, rows],
-                rhs=h_codes[:, cols].bitcast(FP8X4),
-                rhs_scale=h_sc[:, cols],
+                rhs=h_codes[:, j0:j1].bitcast(FP8X4),
+                rhs_scale=h_sc[:, j0:j1],
                 start=False,
                 stop=True,
             )
-
-        act = {}
-
-        def gelu(n, h, dst_cols, acc):
-            if (n, h) not in act:
-                act[n, h] = sb(f"act{n}{h}", [P, HALF], F32, tag=GELU_AFTER.get(n) if h == 0 else None)
-            row_bias = own_bias[n][:] if h == 0 and n in OWN_BIAS else bias[:, n : n + 1]
-            nc.scalar.activation(act[n, h][:, dst_cols], acc, GELU, bias=row_bias)
-
-        def y_first_tile(v, tag):
-            acc = bank(tag)
-            cols = slice(v * QUARTER, (v + 1) * QUARTER)
-            y_sum(acc[:, 0:QUARTER], 0, cols)
-            gelu(0, 0, cols, acc[:, 0:QUARTER])
-
-        def y_half(n, h):
-            acc = bank("ring")
-            for v in (1, 0):
-                j0 = h * HALF + v * QUARTER
-                y_sum(acc[:, v * QUARTER : (v + 1) * QUARTER], n, slice(j0, j0 + QUARTER))
-            gelu(n, h, slice(0, HALF), acc[:, 0:HALF])
-
-        def scatter(n, h):
-            cols = slice(h * HALF, (h + 1) * HALF)
-            window = outs[n][:].indirect(place[:, cols.start // GROUP : cols.stop // GROUP])
-            nc.vector.tensor_tensor(window, act[n, h][:], wgo_sb[:, cols], MULT)
+            act = sb(f"act{n}_{j0}", [P, j1 - j0], F32, tag=act_tag)
+            nc.scalar.activation(act[:], acc[:, 0 : j1 - j0], GELU, bias=bias[:, n : n + 1])
+            h = j0 // HALF
+            window = outs[n][:].indirect(place[:, j0 // GROUP : j1 // GROUP])
+            nc.vector.tensor_tensor(window, act[:], wgo_sb[h][:, j0 - h * HALF : j1 - h * HALF], MULT)
+            return act
 
         for i in range(PACK):
-            gather(0, i, 0)
-            gather(0, i, 1)
+            gather(0, i)
         x_round(0, 0)
         x_round(0, 1)
+        for i in range(PACK - 1):
+            gather(1, i)
+        gather(1, PACK - 1, 0, HALF)
+        gather(1, PACK - 1, HALF, S)
+        x_round(1, 0)
+        x_quantize(0, 0, tag="plane13")
+        x_quantize(1, 0)
         down_round(0)
-        x_quantize(0, 0)
-        gather(1, 0, 0)
-        gather(1, 0, 1)
-        codes0 = sb("codes0", [P, HALF + R], U32, tag="plane10")
-        x_codes[0, 1], d_codes[0] = codes0[:, 0:HALF], codes0[:, HALF : HALF + R]
-        x_quantize(0, 1)
-        down_quantize(0)
-
+        down_quantize(0, 0, PACK)
+        h_acc = [bank("a"), bank("b")]
+        h_pass(h_acc[0], 0, 0)
+        h_pass(h_acc[1], 1, 0)
         down_round(1)
-        gather(1, 1, 0)
-        marks = [sb(f"mark{w}", [P, 1], F32) for w in range(len(held))]
-        for mark, tenant in zip(marks, held):
-            nc.scalar.activation(
-                mark[:], tenant[:, ROW_TILES : ROW_TILES + 1], IDENTITY, bias=picked[1, 0][:, 1, 0:1]
-            )
-        gather(1, 1, 1)
-        d_codes[1] = sb("d_codes1", [P, R], U32, tag="mark0")[:]
-        down_quantize(1)
-        gather(1, 2, 0)
-
-        gather_columns(1, 3, 0, 0, QUARTER)
-        gather_columns(1, 3, 0, QUARTER, HALF)
-        quarter_round(nc.vector.tensor_copy, 0)
-        quarter_round(nc.scalar.copy, 1)
-        quarter_quantize(0)
-        quarter_quantize(1)
-        warm_up()
+        for t in range(PACK):
+            down_quantize(1, t, t + 1)
+        h_pass(h_acc[0], 0, 1)
+        h_pass(h_acc[1], 1, 1)
+        up_chunk(nc.vector.tensor_copy, 0)
+        x_round(1, 1, tag="down_raw1")
+        x_quantize(0, 1, tag="d_bf1")
         h_first = [sb(f"h_bf{v}", [P, QUARTER, PACK], BF16)[:] for v in range(2)]
-        h_quarter(0, "a", h_first[0])
-        h_quarter(1, "b", h_first[1])
+        h_round(h_first[0], h_acc[0])
+        h_round(h_first[1], h_acc[1])
         h_quantize(0, QUARTER, h_first[0])
         h_quantize(QUARTER, HALF, h_first[1])
-        up_prepare(nc.scalar.copy, 0, P, after="picked10")
-        y_first_tile(0, "a")
-        y_first_tile(1, "b")
-        up_prepare(nc.vector.tensor_copy, P, UP_CHUNK, after="h_bf1")
-        gather(1, 3, 1)
-        gather(1, 2, 1)
-        scatter(0, 0)
-
-        up_chunk(1, after="bias0")
-        y_half(1, 0)
-        y_half(2, 0)
-        up_chunk(2, after="bias1")
-        y_half(3, 0)
-        x_round(1, 1, tag="bias3")
         x_quantize(1, 1)
-        y_half(4, 0)
-        up_chunk(3, after="bias4")
-        y_half(5, 0)
-        h_second = sb("h_second", [P, HALF, PACK], BF16, tag="bias5")
-        h_quarter(2, "c", h_second[:, 0:QUARTER, :])
-        h_quarter(3, "d", h_second[:, QUARTER:HALF, :])
+        first_act = y_tile(0, 0, QUARTER, "ring")
+        y_tile(1, 0, QUARTER, "ring")
+        y_tile(0, QUARTER, HALF, "a")
+        up_chunk(nc.scalar.copy, 1)
+        y_tile(1, QUARTER, HALF, "b", act_tag="up_raw1")
+        y_tile(2, 0, HALF, "ring")
+        up_chunk(nc.scalar.copy, 2)
+        y_tile(3, 0, HALF, "ring", act_tag="up_raw2")
+        h_second = sb("h_second", [P, HALF, PACK], BF16, tag="up_raw2")
+        for q, tag in [(2, "a"), (3, "b")]:
+            acc = bank(tag)
+            h_pass(acc, q, 0)
+            h_pass(acc, q, 1)
+            h_round(h_second[:, (q - 2) * QUARTER : (q - 1) * QUARTER, :], acc)
+        y_tile(4, 0, HALF, "ring")
         h_quantize(HALF, S, h_second[:])
-        y_half(6, 0)
-        y_half(7, 0)
-        for n in range(1, ROW_TILES):
-            scatter(n, 0)
-
+        up_chunk(nc.scalar.copy, 3)
+        y_tile(5, 0, HALF, "ring", act_tag="up_raw3")
+        y_tile(6, 0, HALF, "ring")
+        y_tile(7, 0, HALF, "ring")
         for n in range(ROW_TILES):
-            y_half(n, 1)
-            scatter(n, 1)
+            y_tile(n, HALF, S, "ring")
             nc.sync.dma_start(out[n * P : (n + 1) * P, :], outs[n][:])

@@ -26,9 +26,13 @@ QUARTER = S // 4
 GROUP = 16
 ROW_TILES = M // P
 RING_BANKS = 6
-UP_CHUNK = 2 * P
-W4_CHUNKS = [(0, UP_CHUNK), (UP_CHUNK, M - UP_CHUNK)]
-DOWN_ON_VECTOR = (72, 80)
+UP_CHUNKS = [(0, 2 * P), (2 * P, 2 * P), (4 * P, 2 * P), (6 * P, 2 * P)]
+W4_SPLIT = 2 * P
+W4_CHUNKS = [(0, W4_SPLIT), (W4_SPLIT, M - W4_SPLIT)]
+FIRST_ON_VECTOR = 64
+DOWN_PIECES = [(0, 0, P), (1, 0, P // 2), (1, P // 2, P)]
+SECOND_ON_VECTOR = 24
+LAST_ON_VECTOR = 24
 
 
 def tile_list_hboth_l_gelu_kernel(
@@ -48,12 +52,12 @@ def tile_list_hboth_l_gelu_kernel(
         pick = keep.tile([P, S // GROUP], U16, name="pick")
         place = keep.tile([P, S // GROUP], U16, name="place")
         wgt_sb = sb("wgt_sb", [P, S], F32)
-        wgo_sb = [sb(f"wgo_sb{h}", [P, HALF], F32) for h in range(2)]
+        wgo_sb = sb("wgo_sb", [P, S], F32)
         planes = [[sb(f"plane{a}{i}", [P, T], F32) for i in range(PACK)] for a in range(PASSES)]
-        down_raw = [sb(f"down_raw{a}", [P, PACK, R], F32) for a in range(PASSES)]
-        up_raw = [sb(f"up_raw{c}", [P, PACK, UP_CHUNK], F32) for c in range(M // UP_CHUNK)]
+        down_raw = [sb(f"down_raw{c}", [P, PACK, PACK * (m1 - m0)], F32) for c, (a, m0, m1) in enumerate(DOWN_PIECES)]
+        up_raw = [sb(f"up_raw{c}", [P, PACK, width], F32) for c, (n0, width) in enumerate(UP_CHUNKS)]
         w4_codes = [sb(f"w4_codes{c}", [P, PASSES, 2 * width], U8) for c, (n0, width) in enumerate(W4_CHUNKS)]
-        w4_sc = sb("w4_sc", [P, PASSES, M], U8)
+        w4_sc = [sb(f"w4_sc{c}", [P, PASSES, width], U8) for c, (n0, width) in enumerate(W4_CHUNKS)]
         b_rows = sb("b_rows", [P, P], F32)
         bias = sb("bias", [P, ROW_TILES], F32)
         ident = sb("ident", [P, P], F32)
@@ -64,7 +68,8 @@ def tile_list_hboth_l_gelu_kernel(
         nc.scalar.dma_start(b_rows[0:ROW_TILES, :], b.rearrange("(c p) -> c p", p=P))
         make_identity(nc, ident[:])
         nc.scalar.activation(table_load[:, 0:1], ident[:, 0:1], GELU)
-        nc.gpsimd.memset(w4_sc[:].rearrange("p a n -> p (a n)").bitcast(U32), 0)
+        for scales in w4_sc:
+            nc.gpsimd.memset(scales[:].rearrange("p a n -> p (a n)").bitcast(U32), 0)
         for n in range(ROW_TILES):
             nc.gpsimd.memset(outs[n][:].bitcast(I32), 0)
 
@@ -72,44 +77,47 @@ def tile_list_hboth_l_gelu_kernel(
             rows = xT[a * K_PASS : (a + 1) * K_PASS, :].rearrange("(p i) t -> p i t", i=PACK)
             nc.sync.dma_start(planes[a][i][:], rows[:, i, :])
 
-        def load_down(a):
+        def load_down(c):
+            a, m0, m1 = DOWN_PIECES[c]
             rows = down[a * K_PASS : (a + 1) * K_PASS, :].rearrange("(p j) r -> p j r", j=PACK)
-            nc.sync.dma_start(down_raw[a][:], rows)
+            nc.sync.dma_start(down_raw[c][:], rows[:, :, PACK * m0 : PACK * m1])
 
         def load_up(c):
             rows = up.rearrange("(p j) n -> p j n", j=PACK)
-            nc.sync.dma_start(up_raw[c][:], rows[:, :, c * UP_CHUNK : (c + 1) * UP_CHUNK])
+            n0, width = UP_CHUNKS[c]
+            nc.sync.dma_start(up_raw[c][:], rows[:, :, n0 : n0 + width])
 
         def load_w4(c):
             n0, width = W4_CHUNKS[c]
+            for r in range(4):
+                rows = w4_scales.rearrange("a (q r) n -> r q a n", r=4)[r][:, :, n0 : n0 + width]
+                nc.sync.dma_start(w4_sc[c][r:P:32, :, :].bitcast(I32), rows.bitcast(I32))
             src = w4_words[:, :, 2 * n0 : 2 * (n0 + width)].rearrange("a p n -> p a n")
             nc.sync.dma_start(w4_codes[c][:].bitcast(I32), src.bitcast(I32))
 
-        def load_w4_scales():
-            for q in range(4):
-                src = w4_scales[:, 4 * q : 4 * q + 4, :].rearrange("a r n -> r a n")
-                nc.sync.dma_start(w4_sc[32 * q : 32 * q + 4, :, :].bitcast(I32), src.bitcast(I32))
-
         def load_wgo(h):
-            nc.sync.dma_start(wgo_sb[h][:], wgo[:, h * HALF : (h + 1) * HALF])
+            nc.sync.dma_start(wgo_sb[:, h * HALF : (h + 1) * HALF], wgo[:, h * HALF : (h + 1) * HALF])
 
         nc.sync.dma_start(pick[:], offs)
         nc.sync.dma_start(wgt_sb[:], wgt)
-        for a in range(PASSES):
-            for i in range(PACK):
-                load_plane(a, i)
+        for i in range(PACK):
+            load_plane(0, i)
+        load_plane(1, 0)
+        load_plane(1, 1)
+        load_plane(1, 2)
+        load_plane(1, 3)
         load_down(0)
         load_down(1)
+        load_down(2)
         load_up(0)
-        load_w4_scales()
+        load_up(1)
         load_w4(0)
         nc.sync.dma_start(place[:], offs2)
         load_wgo(0)
-        load_up(1)
         load_w4(1)
+        load_wgo(1)
         load_up(2)
         load_up(3)
-        load_wgo(1)
 
         turned = bank("a")
         nc.tensor.transpose(turned[:, 0:P], b_rows[:], ident[:])
@@ -130,33 +138,29 @@ def tile_list_hboth_l_gelu_kernel(
 
         x_bf = {}
 
-        def gather(a, i, j0=0, j1=S):
+        def gather(a, i, j0=0, j1=S, weights=None):
             window = planes[a][i][:].indirect(pick[:, j0 // GROUP : j1 // GROUP])
-            nc.vector.tensor_tensor(picked[a][:, i, j0:j1], window, wgt_sb[:, j0:j1], MULT)
+            nc.vector.tensor_tensor(picked[a][:, i, j0:j1], window, wgt_sb[:, j0:j1] if weights is None else weights, MULT)
 
-        def x_round(a, h, tag=None):
-            x_bf[a, h] = sb(f"x_bf{a}{h}", [P, HALF, PACK], BF16, tag=tag)
-            interleave(nc.scalar.copy, x_bf[a, h][:], picked[a][:, :, h * HALF : (h + 1) * HALF])
+        def x_round(copy, a, dst, j0, j1):
+            interleave(copy, dst, picked[a][:, :, j0:j1])
 
-        def x_quantize(a, h, tag=None):
-            x_codes[a, h] = sb(f"x_codes{a}{h}", [P, HALF], U32, tag=tag)
-            cols = slice(h * HALF, (h + 1) * HALF)
-            quantize(x_codes[a, h][:], x_sc[:, a, cols], x_bf[a, h][:].rearrange("p c t -> p (c t)"))
+        def x_quantize(codes, a, j0, j1, rounded):
+            quantize(codes, x_sc[:, a, j0:j1], rounded.rearrange("p c t -> p (c t)"))
 
         def x_words(a, j):
             return x_codes[a, j // HALF][:, j % HALF : j % HALF + QUARTER].bitcast(FP8X4)
 
-        d_codes = [sb(f"d_codes{a}", [P, R], U32) for a in range(PASSES)]
+        d_codes = {}
         d_sc = sb("d_sc", [P, PASSES, R], U8)
         d_bf = [sb(f"d_bf{a}", [P, PACK, P, PACK], BF16) for a in range(PASSES)]
 
-        def down_round(a):
-            split = DOWN_ON_VECTOR[a]
-            for copy, m0, m1 in [(nc.scalar.copy, split, P), (nc.vector.tensor_copy, 0, split)]:
-                copy(
-                    d_bf[a][:, :, m0:m1, :].rearrange("p t m j -> p m j t"),
-                    down_raw[a][:, :, PACK * m0 : PACK * m1].rearrange("p j (m t) -> p m j t", t=PACK),
-                )
+        def down_round(copy, c, t0, t1, m0, m1):
+            a, first, last = DOWN_PIECES[c]
+            copy(
+                d_bf[a][:, t0:t1, first + m0 : first + m1, :].rearrange("p t m j -> p m j t"),
+                down_raw[c][:].rearrange("p j (m t) -> p m j t", t=PACK)[:, m0:m1, :, t0:t1],
+            )
 
         def down_quantize(a, t0, t1):
             m = slice(t0 * P, t1 * P)
@@ -165,18 +169,22 @@ def tile_list_hboth_l_gelu_kernel(
         u_codes = sb("u_codes", [P, M], U32)
         u_sc = sb("u_sc", [P, M], U8)
 
-        def up_chunk(copy, c):
-            cols = slice(c * UP_CHUNK, (c + 1) * UP_CHUNK)
-            rounded = sb(f"u_bf{c}", [P, UP_CHUNK, PACK], BF16)
-            interleave(copy, rounded[:], up_raw[c][:])
+        def up_chunk(c, on_vector=0, tag=None):
+            n0, width = UP_CHUNKS[c]
+            cols = slice(n0, n0 + width)
+            rounded = sb(f"u_bf{c}", [P, width, PACK], BF16, tag=tag)
+            if on_vector < width:
+                interleave(nc.scalar.copy, rounded[:, on_vector:width, :], up_raw[c][:, :, on_vector:width])
+            if on_vector:
+                interleave(nc.vector.tensor_copy, rounded[:, 0:on_vector, :], up_raw[c][:, :, 0:on_vector])
             quantize(u_codes[:, cols], u_sc[:, cols], rounded[:].rearrange("p n t -> p (n t)"))
 
         h_codes = sb("h_codes", [P, S], U32)
         h_sc = sb("h_sc", [P, S], U8)
 
-        def h_pass(acc, q, a):
+        def h_pass(acc, q, a, order=(0, 1, 2, 3)):
             cols = slice(q * QUARTER, (q + 1) * QUARTER)
-            for t in range(PACK):
+            for t in order:
                 m = slice(t * P, (t + 1) * P)
                 nc.tensor.matmul_mx(
                     out=acc[:, m],
@@ -184,8 +192,8 @@ def tile_list_hboth_l_gelu_kernel(
                     lhsT_scale=d_sc[:, a, m],
                     rhs=x_words(a, cols.start),
                     rhs_scale=x_sc[:, a, cols],
-                    start=(a == 0 and t == 0),
-                    stop=(a == PASSES - 1 and t == PACK - 1),
+                    start=(a == 0 and t == order[0]),
+                    stop=(a == PASSES - 1 and t == order[-1]),
                 )
 
         def h_round(dst, acc):
@@ -196,7 +204,7 @@ def tile_list_hboth_l_gelu_kernel(
 
         def y_tile(n, j0, j1, bank_tag, act_tag=None):
             acc = bank(bank_tag)
-            c = 0 if n * P < UP_CHUNK else 1
+            c = 0 if n * P < W4_SPLIT else 1
             first = n * P - W4_CHUNKS[c][0]
             rows = slice(n * P, (n + 1) * P)
             for a in range(PASSES):
@@ -204,7 +212,7 @@ def tile_list_hboth_l_gelu_kernel(
                     nc.tensor.matmul_mx(
                         out=acc[:, j - j0 : j - j0 + QUARTER],
                         lhsT=w4_codes[c][:, a, 2 * first : 2 * (first + P)].bitcast(FP4X4),
-                        lhsT_scale=w4_sc[:, a, rows],
+                        lhsT_scale=w4_sc[c][:, a, first : first + P],
                         rhs=x_words(a, j),
                         rhs_scale=x_sc[:, a, j : j + QUARTER],
                         start=(a == 0 and j == j0),
@@ -221,61 +229,96 @@ def tile_list_hboth_l_gelu_kernel(
             )
             act = sb(f"act{n}_{j0}", [P, j1 - j0], F32, tag=act_tag)
             nc.scalar.activation(act[:], acc[:, 0 : j1 - j0], GELU, bias=bias[:, n : n + 1])
-            h = j0 // HALF
             window = outs[n][:].indirect(place[:, j0 // GROUP : j1 // GROUP])
-            nc.vector.tensor_tensor(window, act[:], wgo_sb[h][:, j0 - h * HALF : j1 - h * HALF], MULT)
+            nc.vector.tensor_tensor(window, act[:], wgo_sb[:, j0:j1], MULT)
             return act
 
         for i in range(PACK):
             gather(0, i)
-        x_round(0, 0)
-        x_round(0, 1)
-        for i in range(PACK - 1):
-            gather(1, i)
-        gather(1, PACK - 1, 0, HALF)
-        gather(1, PACK - 1, HALF, S)
-        x_round(1, 0)
-        x_quantize(0, 0, tag="plane13")
-        x_quantize(1, 0)
-        down_round(0)
+        x_bf[0] = sb("x_bf0", [P, S, PACK], BF16)
+        x_round(nc.scalar.copy, 0, x_bf[0][:], 0, S)
+        parked = picked[1][:, 2, HALF:S]
+        nc.scalar.copy(parked, wgt_sb[:, 0:HALF])
+        gather(1, 0)
+        gather(1, 1)
+        gather(1, 2, 0, HALF)
+        gather(1, 3, 0, HALF, weights=parked)
+        gather(1, 3, HALF, S)
+        gather(1, 2, HALF, S)
+        x_first = sb("x_first", [P, HALF, PACK], BF16)
+        x_round(nc.scalar.copy, 1, x_first[:], 0, HALF)
+        x_codes0 = sb("x_codes0", [P, S], U32, tag="plane12")
+        x_codes[0, 0], x_codes[0, 1] = x_codes0[:, 0:HALF], x_codes0[:, HALF:S]
+        x_quantize(x_codes0[:], 0, 0, S, x_bf[0][:])
+        spare = bank("b")
+        for w in range(3):
+            nc.tensor.matmul_mx(
+                out=spare[:],
+                lhsT=x_codes0[:, 0:P].bitcast(FP8X4),
+                lhsT_scale=x_sc[:, 0, 0:P],
+                rhs=x_codes0[:].bitcast(FP8X4),
+                rhs_scale=x_sc[:, 0, :],
+                start=True,
+                stop=True,
+            )
+        down_round(nc.scalar.copy, 0, 0, PACK, FIRST_ON_VECTOR, P)
+        down_round(nc.vector.tensor_copy, 0, 0, PACK, 0, FIRST_ON_VECTOR)
+        d_codes[0] = sb("d_codes0", [P, R], U32)
+        x_codes[1, 0] = sb("x_codes10", [P, HALF], U32)[:]
+        x_quantize(x_codes[1, 0], 1, 0, HALF, x_first[:])
         down_quantize(0, 0, PACK)
         h_acc = [bank("a"), bank("b")]
         h_pass(h_acc[0], 0, 0)
         h_pass(h_acc[1], 1, 0)
-        down_round(1)
-        for t in range(PACK):
-            down_quantize(1, t, t + 1)
+        down_round(nc.scalar.copy, 1, 0, PACK, SECOND_ON_VECTOR, P // 2)
+        down_round(nc.vector.tensor_copy, 1, 0, PACK, 0, SECOND_ON_VECTOR)
+        down_round(nc.scalar.copy, 2, 2, PACK, LAST_ON_VECTOR, P // 2)
+        down_round(nc.vector.tensor_copy, 2, 0, 2, 0, P // 2)
+        down_round(nc.vector.tensor_copy, 2, 2, PACK, 0, LAST_ON_VECTOR)
+        d_codes[1] = sb("d_codes1", [P, R], U32)
+        down_quantize(1, 0, 2)
+        down_quantize(1, 2, PACK)
         h_pass(h_acc[0], 0, 1)
-        h_pass(h_acc[1], 1, 1)
-        up_chunk(nc.vector.tensor_copy, 0)
-        x_round(1, 1, tag="down_raw1")
-        x_quantize(0, 1, tag="d_bf1")
+        h_pass(h_acc[1], 1, 1, order=(2, 3, 0, 1))
+        x_second = sb("x_second", [P, HALF, PACK], BF16, tag="down_raw2")
+        x_round(nc.scalar.copy, 1, x_second[:, 0:QUARTER, :], HALF, HALF + QUARTER)
+        x_round(nc.vector.tensor_copy, 1, x_second[:, QUARTER:HALF, :], HALF + QUARTER, S)
+        up_chunk(0, on_vector=2 * P)
         h_first = [sb(f"h_bf{v}", [P, QUARTER, PACK], BF16)[:] for v in range(2)]
         h_round(h_first[0], h_acc[0])
         h_round(h_first[1], h_acc[1])
         h_quantize(0, QUARTER, h_first[0])
         h_quantize(QUARTER, HALF, h_first[1])
-        x_quantize(1, 1)
+        x_codes[1, 1] = sb("x_codes11", [P, HALF], U32)[:]
+        x_quantize(x_codes[1, 1], 1, HALF, S, x_second[:])
+        up_chunk(1, on_vector=2 * P, tag="h_bf0")
         first_act = y_tile(0, 0, QUARTER, "ring")
         y_tile(1, 0, QUARTER, "ring")
         y_tile(0, QUARTER, HALF, "a")
-        up_chunk(nc.scalar.copy, 1)
-        y_tile(1, QUARTER, HALF, "b", act_tag="up_raw1")
-        y_tile(2, 0, HALF, "ring")
-        up_chunk(nc.scalar.copy, 2)
-        y_tile(3, 0, HALF, "ring", act_tag="up_raw2")
-        h_second = sb("h_second", [P, HALF, PACK], BF16, tag="up_raw2")
+        y_tile(1, QUARTER, HALF, "b")
+        h_second = sb("h_second", [P, HALF, PACK], BF16)
         for q, tag in [(2, "a"), (3, "b")]:
             acc = bank(tag)
             h_pass(acc, q, 0)
             h_pass(acc, q, 1)
             h_round(h_second[:, (q - 2) * QUARTER : (q - 1) * QUARTER, :], acc)
-        y_tile(4, 0, HALF, "ring")
         h_quantize(HALF, S, h_second[:])
-        up_chunk(nc.scalar.copy, 3)
-        y_tile(5, 0, HALF, "ring", act_tag="up_raw3")
-        y_tile(6, 0, HALF, "ring")
-        y_tile(7, 0, HALF, "ring")
-        for n in range(ROW_TILES):
-            y_tile(n, HALF, S, "ring")
+
+        def store(n):
             nc.sync.dma_start(out[n * P : (n + 1) * P, :], outs[n][:])
+
+        y_tile(2, 0, HALF, "ring")
+        y_tile(3, 0, HALF, "ring")
+        y_tile(0, HALF, S, "ring", act_tag="act2_0")
+        store(0)
+        up_chunk(2)
+        y_tile(1, HALF, S, "ring", act_tag="up_raw2")
+        store(1)
+        y_tile(2, HALF, S, "ring", act_tag="act3_0")
+        store(2)
+        up_chunk(3)
+        y_tile(3, HALF, S, "ring", act_tag="up_raw3")
+        store(3)
+        for n in range(4, ROW_TILES):
+            y_tile(n, 0, S, "ring")
+            store(n)

@@ -250,17 +250,6 @@ def tile_list_hboth_l_gelu_kernel(
         x_codes0 = sb("x_codes0", [P, S], U32, tag="plane12")
         x_codes[0, 0], x_codes[0, 1] = x_codes0[:, 0:HALF], x_codes0[:, HALF:S]
         x_quantize(x_codes0[:], 0, 0, S, x_bf[0][:])
-        spare = bank("b")
-        for w in range(3):
-            nc.tensor.matmul_mx(
-                out=spare[:],
-                lhsT=x_codes0[:, 0:P].bitcast(FP8X4),
-                lhsT_scale=x_sc[:, 0, 0:P],
-                rhs=x_codes0[:].bitcast(FP8X4),
-                rhs_scale=x_sc[:, 0, :],
-                start=True,
-                stop=True,
-            )
         down_round(nc.scalar.copy, 0, 0, PACK, FIRST_ON_VECTOR, P)
         down_round(nc.vector.tensor_copy, 0, 0, PACK, 0, FIRST_ON_VECTOR)
         d_codes[0] = sb("d_codes0", [P, R], U32)

@@ -18,6 +18,7 @@ MULT = mybir.AluOpType.mult
 GELU = mybir.ActivationFunctionType.Gelu_apprx_tanh
 
 P = 128
+EXTRA = 0
 PACK = 4
 K_PASS = P * PACK
 PASSES = K // K_PASS
@@ -25,14 +26,13 @@ HALF = S // 2
 QUARTER = S // 4
 GROUP = 16
 ROW_TILES = M // P
-RING_BANKS = 6
+RING_BANKS = 4
 UP_CHUNKS = [(0, 2 * P), (2 * P, 2 * P), (4 * P, 2 * P), (6 * P, 2 * P)]
-W4_SPLIT = 2 * P
-W4_CHUNKS = [(0, W4_SPLIT), (W4_SPLIT, M - W4_SPLIT)]
-FIRST_ON_VECTOR = 64
-DOWN_PIECES = [(0, 0, P), (1, 0, P // 2), (1, P // 2, P)]
-SECOND_ON_VECTOR = 24
-LAST_ON_VECTOR = 24
+W4_CHUNKS = [(0, 2 * P), (2 * P, 2 * P), (4 * P, 4 * P)]
+SC_WIDTH = M // 2
+FIRST_ON_VECTOR = 48
+DOWN_PIECES = [(0, 0, PACK), (1, 0, PACK)]
+LAST_ON_VECTOR = 32
 
 
 def tile_list_hboth_l_gelu_kernel(
@@ -54,10 +54,12 @@ def tile_list_hboth_l_gelu_kernel(
         wgt_sb = sb("wgt_sb", [P, S], F32)
         wgo_sb = sb("wgo_sb", [P, S], F32)
         planes = [[sb(f"plane{a}{i}", [P, T], F32) for i in range(PACK)] for a in range(PASSES)]
-        down_raw = [sb(f"down_raw{c}", [P, PACK, PACK * (m1 - m0)], F32) for c, (a, m0, m1) in enumerate(DOWN_PIECES)]
-        up_raw = [sb(f"up_raw{c}", [P, PACK, width], F32) for c, (n0, width) in enumerate(UP_CHUNKS)]
-        w4_codes = [sb(f"w4_codes{c}", [P, PASSES, 2 * width], U8) for c, (n0, width) in enumerate(W4_CHUNKS)]
-        w4_sc = [sb(f"w4_sc{c}", [P, PASSES, width], U8) for c, (n0, width) in enumerate(W4_CHUNKS)]
+        down_raw = [sb(f"down_raw{c}", [P, j1 - j0, R], F32) for c, (a, j0, j1) in enumerate(DOWN_PIECES)]
+        up_wide = [sb(f"up_raw{c}", [P, PACK, width + EXTRA], F32) for c, (n0, width) in enumerate(UP_CHUNKS)]
+        up_at = [EXTRA if c else 0 for c in range(4)]
+        up_raw = [up_wide[c][:, :, up_at[c] : up_at[c] + width] for c, (n0, width) in enumerate(UP_CHUNKS)]
+        w4_codes = [sb(f"w4_codes{c}", [P, PASSES, 2 * width + (0 if c == 2 else 8 * EXTRA)], U8) for c, (n0, width) in enumerate(W4_CHUNKS)]
+        w4_sc = [sb(f"w4_sc{h}", [P, PASSES, SC_WIDTH], U8) for h in range(2)]
         b_rows = sb("b_rows", [P, P], F32)
         bias = sb("bias", [P, ROW_TILES], F32)
         ident = sb("ident", [P, P], F32)
@@ -65,7 +67,6 @@ def tile_list_hboth_l_gelu_kernel(
         outs = [sb(f"out{n}", [P, T], F32) for n in range(ROW_TILES)]
 
         nc.gpsimd.memset(b_rows[:], 0.0)
-        nc.scalar.dma_start(b_rows[0:ROW_TILES, :], b.rearrange("(c p) -> c p", p=P))
         make_identity(nc, ident[:])
         nc.scalar.activation(table_load[:, 0:1], ident[:, 0:1], GELU)
         for scales in w4_sc:
@@ -78,21 +79,23 @@ def tile_list_hboth_l_gelu_kernel(
             nc.sync.dma_start(planes[a][i][:], rows[:, i, :])
 
         def load_down(c):
-            a, m0, m1 = DOWN_PIECES[c]
+            a, j0, j1 = DOWN_PIECES[c]
             rows = down[a * K_PASS : (a + 1) * K_PASS, :].rearrange("(p j) r -> p j r", j=PACK)
-            nc.sync.dma_start(down_raw[c][:], rows[:, :, PACK * m0 : PACK * m1])
+            nc.sync.dma_start(down_raw[c][:], rows[:, j0:j1, :])
 
         def load_up(c):
             rows = up.rearrange("(p j) n -> p j n", j=PACK)
             n0, width = UP_CHUNKS[c]
-            nc.sync.dma_start(up_raw[c][:], rows[:, :, n0 : n0 + width])
+            nc.sync.dma_start(up_wide[c][:], rows[:, :, n0 - up_at[c] : n0 - up_at[c] + width + EXTRA])
+
+        def load_scales(h):
+            for r in range(4):
+                rows = w4_scales.rearrange("a (q r) n -> r q a n", r=4)[r][:, :, h * SC_WIDTH : (h + 1) * SC_WIDTH]
+                nc.sync.dma_start(w4_sc[h][r:P:32, :, :].bitcast(I32), rows.bitcast(I32))
 
         def load_w4(c):
             n0, width = W4_CHUNKS[c]
-            for r in range(4):
-                rows = w4_scales.rearrange("a (q r) n -> r q a n", r=4)[r][:, :, n0 : n0 + width]
-                nc.sync.dma_start(w4_sc[c][r:P:32, :, :].bitcast(I32), rows.bitcast(I32))
-            src = w4_words[:, :, 2 * n0 : 2 * (n0 + width)].rearrange("a p n -> p a n")
+            src = w4_words[:, :, 2 * n0 : 2 * (n0 + width) + (0 if c == 2 else 8 * EXTRA)].rearrange("a p n -> p a n")
             nc.sync.dma_start(w4_codes[c][:].bitcast(I32), src.bitcast(I32))
 
         def load_wgo(h):
@@ -100,6 +103,7 @@ def tile_list_hboth_l_gelu_kernel(
 
         nc.sync.dma_start(pick[:], offs)
         nc.sync.dma_start(wgt_sb[:], wgt)
+        nc.sync.dma_start(b_rows[0:ROW_TILES, :], b.rearrange("(c p) -> c p", p=P))
         for i in range(PACK):
             load_plane(0, i)
         load_plane(1, 0)
@@ -108,15 +112,17 @@ def tile_list_hboth_l_gelu_kernel(
         load_plane(1, 3)
         load_down(0)
         load_down(1)
-        load_down(2)
         load_up(0)
-        load_up(1)
+        load_scales(0)
         load_w4(0)
         nc.sync.dma_start(place[:], offs2)
         load_wgo(0)
+        load_up(1)
         load_w4(1)
         load_wgo(1)
         load_up(2)
+        load_scales(1)
+        load_w4(2)
         load_up(3)
 
         turned = bank("a")
@@ -133,32 +139,38 @@ def tile_list_hboth_l_gelu_kernel(
             nc.vector.quantize_mx(out=codes.bitcast(FP8X4), scales=scales, in_=rounded)
 
         picked = [sb(f"picked{a}", [P, PACK, S], F32) for a in range(PASSES)]
-        x_sc = sb("x_sc", [P, PASSES, S], U8)
+        x_sc = sb("x_sc", [P, 2, PASSES, HALF], U8)
+        x_bf = sb("x_bf", [P, 2, PASSES, HALF, PACK], BF16)
         x_codes = {}
-
-        x_bf = {}
 
         def gather(a, i, j0=0, j1=S, weights=None):
             window = planes[a][i][:].indirect(pick[:, j0 // GROUP : j1 // GROUP])
             nc.vector.tensor_tensor(picked[a][:, i, j0:j1], window, wgt_sb[:, j0:j1] if weights is None else weights, MULT)
 
-        def x_round(copy, a, dst, j0, j1):
-            interleave(copy, dst, picked[a][:, :, j0:j1])
-
-        def x_quantize(codes, a, j0, j1, rounded):
-            quantize(codes, x_sc[:, a, j0:j1], rounded.rearrange("p c t -> p (c t)"))
+        def x_round(a, h0, h1, i0, i1):
+            nc.scalar.copy(
+                x_bf[:, h0:h1, a, :, i0:i1].rearrange("p h (c e) t -> p h c t e", e=4),
+                picked[a][:, i0:i1, h0 * HALF : h1 * HALF].rearrange("p t (h c e) -> p h c t e", c=HALF // 4, e=4),
+            )
 
         def x_words(a, j):
             return x_codes[a, j // HALF][:, j % HALF : j % HALF + QUARTER].bitcast(FP8X4)
+
+        def x_scales(a, j):
+            return x_sc[:, j // HALF, a, j % HALF : j % HALF + QUARTER]
+
+        def x_quantize_first(a, tag):
+            x_codes[a, 0] = sb(f"x_codes{a}", [P, HALF], U32, tag=tag)[:]
+            quantize(x_codes[a, 0], x_sc[:, 0, a, :], x_bf[:, 0, a].rearrange("p c t -> p (c t)"))
 
         d_codes = {}
         d_sc = sb("d_sc", [P, PASSES, R], U8)
         d_bf = [sb(f"d_bf{a}", [P, PACK, P, PACK], BF16) for a in range(PASSES)]
 
         def down_round(copy, c, t0, t1, m0, m1):
-            a, first, last = DOWN_PIECES[c]
+            a, j0, j1 = DOWN_PIECES[c]
             copy(
-                d_bf[a][:, t0:t1, first + m0 : first + m1, :].rearrange("p t m j -> p m j t"),
+                d_bf[a][:, t0:t1, m0:m1, j0:j1].rearrange("p t m j -> p m j t"),
                 down_raw[c][:].rearrange("p j (m t) -> p m j t", t=PACK)[:, m0:m1, :, t0:t1],
             )
 
@@ -191,7 +203,7 @@ def tile_list_hboth_l_gelu_kernel(
                     lhsT=d_codes[a][:, m].bitcast(FP8X4),
                     lhsT_scale=d_sc[:, a, m],
                     rhs=x_words(a, cols.start),
-                    rhs_scale=x_sc[:, a, cols],
+                    rhs_scale=x_scales(a, cols.start),
                     start=(a == 0 and t == order[0]),
                     stop=(a == PASSES - 1 and t == order[-1]),
                 )
@@ -202,9 +214,10 @@ def tile_list_hboth_l_gelu_kernel(
         def h_quantize(j0, j1, rounded):
             quantize(h_codes[:, j0:j1], h_sc[:, j0:j1], rounded.rearrange("p n t -> p (n t)"))
 
-        def y_tile(n, j0, j1, bank_tag, act_tag=None):
+        def y_tile(n, j0, j1, bank_tag, act_tag=None, act=None):
             acc = bank(bank_tag)
-            c = 0 if n * P < W4_SPLIT else 1
+            c = min(n // 2, 2)
+            at = n * P % SC_WIDTH
             first = n * P - W4_CHUNKS[c][0]
             rows = slice(n * P, (n + 1) * P)
             for a in range(PASSES):
@@ -212,9 +225,9 @@ def tile_list_hboth_l_gelu_kernel(
                     nc.tensor.matmul_mx(
                         out=acc[:, j - j0 : j - j0 + QUARTER],
                         lhsT=w4_codes[c][:, a, 2 * first : 2 * (first + P)].bitcast(FP4X4),
-                        lhsT_scale=w4_sc[c][:, a, first : first + P],
+                        lhsT_scale=w4_sc[n * P // SC_WIDTH][:, a, at : at + P],
                         rhs=x_words(a, j),
-                        rhs_scale=x_sc[:, a, j : j + QUARTER],
+                        rhs_scale=x_scales(a, j),
                         start=(a == 0 and j == j0),
                         stop=False,
                     )
@@ -227,76 +240,73 @@ def tile_list_hboth_l_gelu_kernel(
                 start=False,
                 stop=True,
             )
-            act = sb(f"act{n}_{j0}", [P, j1 - j0], F32, tag=act_tag)
-            nc.scalar.activation(act[:], acc[:, 0 : j1 - j0], GELU, bias=bias[:, n : n + 1])
+            if act is None:
+                act = sb(f"act{n}_{j0}", [P, j1 - j0], F32, tag=act_tag)[:]
+            nc.scalar.activation(act, acc[:, 0 : j1 - j0], GELU, bias=bias[:, n : n + 1])
             window = outs[n][:].indirect(place[:, j0 // GROUP : j1 // GROUP])
-            nc.vector.tensor_tensor(window, act[:], wgo_sb[:, j0:j1], MULT)
+            nc.vector.tensor_tensor(window, act, wgo_sb[:, j0:j1], MULT)
             return act
 
         for i in range(PACK):
             gather(0, i)
-        x_bf[0] = sb("x_bf0", [P, S, PACK], BF16)
-        x_round(nc.scalar.copy, 0, x_bf[0][:], 0, S)
-        parked = picked[1][:, 2, HALF:S]
-        nc.scalar.copy(parked, wgt_sb[:, 0:HALF])
-        gather(1, 0)
-        gather(1, 1)
-        gather(1, 2, 0, HALF)
-        gather(1, 3, 0, HALF, weights=parked)
-        gather(1, 3, HALF, S)
-        gather(1, 2, HALF, S)
-        x_first = sb("x_first", [P, HALF, PACK], BF16)
-        x_round(nc.scalar.copy, 1, x_first[:], 0, HALF)
-        x_codes0 = sb("x_codes0", [P, S], U32, tag="plane12")
-        x_codes[0, 0], x_codes[0, 1] = x_codes0[:, 0:HALF], x_codes0[:, HALF:S]
-        x_quantize(x_codes0[:], 0, 0, S, x_bf[0][:])
-        down_round(nc.scalar.copy, 0, 0, PACK, FIRST_ON_VECTOR, P)
-        down_round(nc.vector.tensor_copy, 0, 0, PACK, 0, FIRST_ON_VECTOR)
+        x_round(0, 0, 2, 0, PACK)
+        for i in range(PACK - 1):
+            gather(1, i)
+        gather(1, PACK - 1, 0, HALF)
+        gather(1, PACK - 1, HALF, S)
+        x_round(1, 0, 1, 0, 2)
+        x_round(1, 0, 1, 2, PACK)
+        x_round(1, 1, 2, 0, PACK)
+        x_quantize_first(0, "plane13")
+        x_quantize_first(1, None)
+        down_round(nc.scalar.copy, 0, 2, PACK, FIRST_ON_VECTOR, P)
+        down_round(nc.vector.tensor_copy, 0, 0, 2, 0, P)
+        down_round(nc.vector.tensor_copy, 0, 2, PACK, 0, FIRST_ON_VECTOR)
         d_codes[0] = sb("d_codes0", [P, R], U32)
-        x_codes[1, 0] = sb("x_codes10", [P, HALF], U32)[:]
-        x_quantize(x_codes[1, 0], 1, 0, HALF, x_first[:])
-        down_quantize(0, 0, PACK)
+        down_quantize(0, 0, 2)
+        down_quantize(0, 2, PACK)
         h_acc = [bank("a"), bank("b")]
         h_pass(h_acc[0], 0, 0)
         h_pass(h_acc[1], 1, 0)
-        down_round(nc.scalar.copy, 1, 0, PACK, SECOND_ON_VECTOR, P // 2)
-        down_round(nc.vector.tensor_copy, 1, 0, PACK, 0, SECOND_ON_VECTOR)
-        down_round(nc.scalar.copy, 2, 2, PACK, LAST_ON_VECTOR, P // 2)
-        down_round(nc.vector.tensor_copy, 2, 0, 2, 0, P // 2)
-        down_round(nc.vector.tensor_copy, 2, 2, PACK, 0, LAST_ON_VECTOR)
+        down_round(nc.scalar.copy, 1, 2, PACK, LAST_ON_VECTOR, P)
+        down_round(nc.vector.tensor_copy, 1, 0, 2, 0, P)
+        down_round(nc.vector.tensor_copy, 1, 2, PACK, 0, LAST_ON_VECTOR)
         d_codes[1] = sb("d_codes1", [P, R], U32)
         down_quantize(1, 0, 2)
         down_quantize(1, 2, PACK)
         h_pass(h_acc[0], 0, 1)
         h_pass(h_acc[1], 1, 1, order=(2, 3, 0, 1))
-        x_second = sb("x_second", [P, HALF, PACK], BF16, tag="down_raw2")
-        x_round(nc.scalar.copy, 1, x_second[:, 0:QUARTER, :], HALF, HALF + QUARTER)
-        x_round(nc.vector.tensor_copy, 1, x_second[:, QUARTER:HALF, :], HALF + QUARTER, S)
-        up_chunk(0, on_vector=2 * P)
+        up_chunk(0, on_vector=P + 32)
         h_first = [sb(f"h_bf{v}", [P, QUARTER, PACK], BF16)[:] for v in range(2)]
         h_round(h_first[0], h_acc[0])
         h_round(h_first[1], h_acc[1])
         h_quantize(0, QUARTER, h_first[0])
+        x_second = sb("x_second", [P, PASSES, HALF], U32, tag="h_bf0")
+        x_codes[0, 1], x_codes[1, 1] = x_second[:, 0, :], x_second[:, 1, :]
+        quantize(
+            x_second[:].rearrange("p a c -> p (a c)"),
+            x_sc[:, 1].rearrange("p a c -> p (a c)"),
+            x_bf[:, 1].rearrange("p a c t -> p (a c t)"),
+        )
         h_quantize(QUARTER, HALF, h_first[1])
-        x_codes[1, 1] = sb("x_codes11", [P, HALF], U32)[:]
-        x_quantize(x_codes[1, 1], 1, HALF, S, x_second[:])
-        up_chunk(1, on_vector=2 * P, tag="h_bf0")
-        first_act = y_tile(0, 0, QUARTER, "ring")
-        y_tile(1, 0, QUARTER, "ring")
+        first_act = y_tile(0, 0, QUARTER, "c")
+        y_tile(1, 0, QUARTER, "d")
         y_tile(0, QUARTER, HALF, "a")
-        y_tile(1, QUARTER, HALF, "b")
-        h_second = sb("h_second", [P, HALF, PACK], BF16)
-        for q, tag in [(2, "a"), (3, "b")]:
+        up_chunk(1)
+        behind_up = sb("behind_up", [P, QUARTER + S], F32, tag="up_raw1")
+        y_tile(1, QUARTER, HALF, "b", act=behind_up[:, 0:QUARTER])
+        h_second = behind_up[:, QUARTER : QUARTER + S].bitcast(BF16).rearrange("p (n t) -> p n t", t=PACK)
+        for q, tag in [(2, "c"), (3, "d")]:
             acc = bank(tag)
             h_pass(acc, q, 0)
             h_pass(acc, q, 1)
             h_round(h_second[:, (q - 2) * QUARTER : (q - 1) * QUARTER, :], acc)
-        h_quantize(HALF, S, h_second[:])
+        h_quantize(HALF, S, h_second)
 
         def store(n):
             nc.sync.dma_start(out[n * P : (n + 1) * P, :], outs[n][:])
 
-        y_tile(2, 0, HALF, "ring")
+        act2 = y_tile(2, 0, HALF, "ring")
         y_tile(3, 0, HALF, "ring")
         y_tile(0, HALF, S, "ring", act_tag="act2_0")
         store(0)

@@ -25,14 +25,17 @@ PASSES = K // K_PASS
 HALF = S // 2
 QUARTER = S // 4
 GROUP = 16
+BLOCK = 32
+SMALL = 40
 ROW_TILES = M // P
-RING_BANKS = 4
+RING_BANKS = 6
 UP_CHUNKS = [(0, 2 * P), (2 * P, 2 * P), (4 * P, 2 * P), (6 * P, 2 * P)]
-W4_CHUNKS = [(0, 2 * P), (2 * P, 2 * P), (4 * P, 4 * P)]
-SC_WIDTH = M // 2
-FIRST_ON_VECTOR = 48
-DOWN_PIECES = [(0, 0, PACK), (1, 0, PACK)]
-LAST_ON_VECTOR = 32
+W4_SPLIT = 2 * P
+W4_CHUNKS = [(0, W4_SPLIT), (W4_SPLIT, M - W4_SPLIT)]
+FIRST_ON_VECTOR = 24
+DOWN_PIECES = [(0, 0, P), (1, 0, P // 2), (1, P // 2, P)]
+SECOND_ON_VECTOR = 16
+LAST_ON_VECTOR = 24
 
 
 def tile_list_hboth_l_gelu_kernel(
@@ -52,23 +55,27 @@ def tile_list_hboth_l_gelu_kernel(
         pick = keep.tile([P, S // GROUP], U16, name="pick")
         place = keep.tile([P, S // GROUP], U16, name="place")
         wgt_sb = sb("wgt_sb", [P, S], F32)
+        wgt_rows = sb("wgt_rows", [P, BLOCK], F32)
+        wgt_turned = sb("wgt_turned", [P, BLOCK], F32)
+        wgt_spread = sb("wgt_spread", [P, S], F32)
+        wgo_turned = sb("wgo_turned", [P, S], F32)
         wgo_sb = sb("wgo_sb", [P, S], F32)
         planes = [[sb(f"plane{a}{i}", [P, T], F32) for i in range(PACK)] for a in range(PASSES)]
-        down_raw = [sb(f"down_raw{c}", [P, j1 - j0, R], F32) for c, (a, j0, j1) in enumerate(DOWN_PIECES)]
+        down_wide = [sb(f"down_raw{c}", [P, PACK, PACK * (m1 - m0) + (EXTRA if c else 0)], F32) for c, (a, m0, m1) in enumerate(DOWN_PIECES)]
+        down_raw = [down_wide[0][:], down_wide[1][:, :, 0 : 2 * P], down_wide[2][:, :, EXTRA : EXTRA + 2 * P]]
         up_wide = [sb(f"up_raw{c}", [P, PACK, width + EXTRA], F32) for c, (n0, width) in enumerate(UP_CHUNKS)]
         up_at = [EXTRA if c else 0 for c in range(4)]
         up_raw = [up_wide[c][:, :, up_at[c] : up_at[c] + width] for c, (n0, width) in enumerate(UP_CHUNKS)]
-        w4_codes = [sb(f"w4_codes{c}", [P, PASSES, 2 * width + (0 if c == 2 else 8 * EXTRA)], U8) for c, (n0, width) in enumerate(W4_CHUNKS)]
-        w4_sc = [sb(f"w4_sc{h}", [P, PASSES, SC_WIDTH], U8) for h in range(2)]
+        w4_codes = [sb(f"w4_codes{c}", [P, PASSES, 2 * width + (0 if c else 8 * EXTRA)], U8) for c, (n0, width) in enumerate(W4_CHUNKS)]
+        w4_sc = [sb(f"w4_sc{c}", [P, PASSES, width], U8) for c, (n0, width) in enumerate(W4_CHUNKS)]
         b_rows = sb("b_rows", [P, P], F32)
         bias = sb("bias", [P, ROW_TILES], F32)
         ident = sb("ident", [P, P], F32)
-        table_load = sb("table_load", [P, 8], F32)
         outs = [sb(f"out{n}", [P, T], F32) for n in range(ROW_TILES)]
 
-        nc.gpsimd.memset(b_rows[:], 0.0)
+        nc.gpsimd.memset(b_rows[0 : P - SMALL, :], 0.0)
         make_identity(nc, ident[:])
-        nc.scalar.activation(table_load[:, 0:1], ident[:, 0:1], GELU)
+        nc.scalar.activation(bias[0:64, 0:1], b_rows[0:64, 0:1], GELU)
         for scales in w4_sc:
             nc.gpsimd.memset(scales[:].rearrange("p a n -> p (a n)").bitcast(U32), 0)
         for n in range(ROW_TILES):
@@ -79,32 +86,29 @@ def tile_list_hboth_l_gelu_kernel(
             nc.sync.dma_start(planes[a][i][:], rows[:, i, :])
 
         def load_down(c):
-            a, j0, j1 = DOWN_PIECES[c]
+            a, m0, m1 = DOWN_PIECES[c]
             rows = down[a * K_PASS : (a + 1) * K_PASS, :].rearrange("(p j) r -> p j r", j=PACK)
-            nc.sync.dma_start(down_raw[c][:], rows[:, j0:j1, :])
+            nc.sync.dma_start(down_wide[c][:], rows[:, :, PACK * m0 - (EXTRA if c == 2 else 0) : PACK * m1 + (EXTRA if c == 1 else 0)])
 
         def load_up(c):
             rows = up.rearrange("(p j) n -> p j n", j=PACK)
             n0, width = UP_CHUNKS[c]
             nc.sync.dma_start(up_wide[c][:], rows[:, :, n0 - up_at[c] : n0 - up_at[c] + width + EXTRA])
 
-        def load_scales(h):
-            for r in range(4):
-                rows = w4_scales.rearrange("a (q r) n -> r q a n", r=4)[r][:, :, h * SC_WIDTH : (h + 1) * SC_WIDTH]
-                nc.sync.dma_start(w4_sc[h][r:P:32, :, :].bitcast(I32), rows.bitcast(I32))
-
         def load_w4(c):
             n0, width = W4_CHUNKS[c]
-            src = w4_words[:, :, 2 * n0 : 2 * (n0 + width) + (0 if c == 2 else 8 * EXTRA)].rearrange("a p n -> p a n")
+            for r in range(4):
+                rows = w4_scales.rearrange("a (q r) n -> r q a n", r=4)[r][:, :, n0 : n0 + width]
+                nc.sync.dma_start(w4_sc[c][r:P:32, :, :].bitcast(I32), rows.bitcast(I32))
+            src = w4_words[:, :, 2 * n0 : 2 * (n0 + width) + (0 if c else 8 * EXTRA)].rearrange("a p n -> p a n")
             nc.sync.dma_start(w4_codes[c][:].bitcast(I32), src.bitcast(I32))
 
-        def load_wgo(h):
-            nc.sync.dma_start(wgo_sb[:, h * HALF : (h + 1) * HALF], wgo[:, h * HALF : (h + 1) * HALF])
-
+        nc.sync.dma_start(wgt_rows[:], wgt.rearrange("(g d) (c k) -> d g c k", d=GROUP, k=BLOCK)[0])
         nc.sync.dma_start(pick[:], offs)
-        nc.sync.dma_start(wgt_sb[:], wgt)
-        nc.sync.dma_start(b_rows[0:ROW_TILES, :], b.rearrange("(c p) -> c p", p=P))
-        for i in range(PACK):
+        load_plane(0, 0)
+        nc.sync.dma_start(b_rows[P - ROW_TILES : P, :], b.rearrange("(c p) -> c p", p=P))
+        nc.sync.dma_start(b_rows[P - SMALL : P - ROW_TILES, :], wgo.rearrange("(g d) (c n) -> d g c n", d=GROUP, n=P)[0])
+        for i in range(1, PACK):
             load_plane(0, i)
         load_plane(1, 0)
         load_plane(1, 1)
@@ -112,22 +116,36 @@ def tile_list_hboth_l_gelu_kernel(
         load_plane(1, 3)
         load_down(0)
         load_down(1)
+        load_down(2)
         load_up(0)
-        load_scales(0)
+        load_up(1)
         load_w4(0)
         nc.sync.dma_start(place[:], offs2)
-        load_wgo(0)
-        load_up(1)
         load_w4(1)
-        load_wgo(1)
         load_up(2)
-        load_scales(1)
-        load_w4(2)
         load_up(3)
+
+        nc.vector.transpose(wgt_turned[:], wgt_rows[:])
+        for h in range(2):
+            source = wgt_turned[:].rearrange("p (e c) -> p c e", e=2)[:, 8 * h : 8 * h + 8, :]
+            source = source.unsqueeze(3).to_broadcast([P, 8, 2, GROUP])
+            spread = wgt_spread[:, h * HALF : (h + 1) * HALF].rearrange("p (c e d) -> p c e d", e=2, d=GROUP)
+            nc.vector.tensor_tensor(spread, source, source, mybir.AluOpType.max)
+        for h in range(2):
+            cols = slice(h * HALF, (h + 1) * HALF)
+            nc.vector.transpose(wgt_sb[:, cols], wgt_spread[:, cols])
 
         turned = bank("a")
         nc.tensor.transpose(turned[:, 0:P], b_rows[:], ident[:])
-        nc.scalar.copy(bias[:], turned[:, 0:ROW_TILES])
+        nc.scalar.copy(bias[:], turned[:, P - ROW_TILES : P])
+        nc.scalar.copy(
+            wgo_turned[:].rearrange("p (c g d) -> p c g d", c=4, d=GROUP),
+            turned[:, P - SMALL : P - ROW_TILES].rearrange("p (g c) -> p c g", c=4).unsqueeze(3).to_broadcast([P, 4, 8, GROUP]),
+        )
+        back = bank("b")
+        for c in range(4):
+            nc.tensor.transpose(back[:, c * P : (c + 1) * P], wgo_turned[:, c * P : (c + 1) * P], ident[:])
+        nc.scalar.copy(wgo_sb[:], back[:])
 
         def interleave(copy, dst, src):
             copy(
@@ -139,8 +157,8 @@ def tile_list_hboth_l_gelu_kernel(
             nc.vector.quantize_mx(out=codes.bitcast(FP8X4), scales=scales, in_=rounded)
 
         picked = [sb(f"picked{a}", [P, PACK, S], F32) for a in range(PASSES)]
-        x_sc = sb("x_sc", [P, 2, PASSES, HALF], U8)
-        x_bf = sb("x_bf", [P, 2, PASSES, HALF, PACK], BF16)
+        x_sc = sb("x_sc", [P, PASSES, 2, HALF], U8)
+        x_bf = sb("x_bf", [P, PASSES, 2, HALF, PACK], BF16)
         x_codes = {}
 
         def gather(a, i, j0=0, j1=S, weights=None):
@@ -149,7 +167,7 @@ def tile_list_hboth_l_gelu_kernel(
 
         def x_round(a, h0, h1, i0, i1):
             nc.scalar.copy(
-                x_bf[:, h0:h1, a, :, i0:i1].rearrange("p h (c e) t -> p h c t e", e=4),
+                x_bf[:, a, h0:h1, :, i0:i1].rearrange("p h (c e) t -> p h c t e", e=4),
                 picked[a][:, i0:i1, h0 * HALF : h1 * HALF].rearrange("p t (h c e) -> p h c t e", c=HALF // 4, e=4),
             )
 
@@ -157,21 +175,27 @@ def tile_list_hboth_l_gelu_kernel(
             return x_codes[a, j // HALF][:, j % HALF : j % HALF + QUARTER].bitcast(FP8X4)
 
         def x_scales(a, j):
-            return x_sc[:, j // HALF, a, j % HALF : j % HALF + QUARTER]
+            return x_sc[:, a, j // HALF, j % HALF : j % HALF + QUARTER]
 
-        def x_quantize_first(a, tag):
-            x_codes[a, 0] = sb(f"x_codes{a}", [P, HALF], U32, tag=tag)[:]
-            quantize(x_codes[a, 0], x_sc[:, 0, a, :], x_bf[:, 0, a].rearrange("p c t -> p (c t)"))
+        def x_quantize(a, h0, h1, tag):
+            codes = sb(f"x_codes{a}{h0}", [P, h1 - h0, HALF], U32, tag=tag)
+            for h in range(h0, h1):
+                x_codes[a, h] = codes[:, h - h0, :]
+            quantize(
+                codes[:].rearrange("p h c -> p (h c)"),
+                x_sc[:, a, h0:h1].rearrange("p h c -> p (h c)"),
+                x_bf[:, a, h0:h1].rearrange("p h c t -> p (h c t)"),
+            )
 
         d_codes = {}
         d_sc = sb("d_sc", [P, PASSES, R], U8)
         d_bf = [sb(f"d_bf{a}", [P, PACK, P, PACK], BF16) for a in range(PASSES)]
 
         def down_round(copy, c, t0, t1, m0, m1):
-            a, j0, j1 = DOWN_PIECES[c]
+            a, first, last = DOWN_PIECES[c]
             copy(
-                d_bf[a][:, t0:t1, m0:m1, j0:j1].rearrange("p t m j -> p m j t"),
-                down_raw[c][:].rearrange("p j (m t) -> p m j t", t=PACK)[:, m0:m1, :, t0:t1],
+                d_bf[a][:, t0:t1, first + m0 : first + m1, :].rearrange("p t m j -> p m j t"),
+                down_raw[c].rearrange("p j (m t) -> p m j t", t=PACK)[:, m0:m1, :, t0:t1],
             )
 
         def down_quantize(a, t0, t1):
@@ -216,8 +240,7 @@ def tile_list_hboth_l_gelu_kernel(
 
         def y_tile(n, j0, j1, bank_tag, act_tag=None, act=None):
             acc = bank(bank_tag)
-            c = min(n // 2, 2)
-            at = n * P % SC_WIDTH
+            c = 0 if n * P < W4_SPLIT else 1
             first = n * P - W4_CHUNKS[c][0]
             rows = slice(n * P, (n + 1) * P)
             for a in range(PASSES):
@@ -225,7 +248,7 @@ def tile_list_hboth_l_gelu_kernel(
                     nc.tensor.matmul_mx(
                         out=acc[:, j - j0 : j - j0 + QUARTER],
                         lhsT=w4_codes[c][:, a, 2 * first : 2 * (first + P)].bitcast(FP4X4),
-                        lhsT_scale=w4_sc[n * P // SC_WIDTH][:, a, at : at + P],
+                        lhsT_scale=w4_sc[c][:, a, first : first + P],
                         rhs=x_words(a, j),
                         rhs_scale=x_scales(a, j),
                         start=(a == 0 and j == j0),
@@ -247,7 +270,9 @@ def tile_list_hboth_l_gelu_kernel(
             nc.vector.tensor_tensor(window, act, wgo_sb[:, j0:j1], MULT)
             return act
 
-        for i in range(PACK):
+        gather(0, 0, 0, HALF)
+        gather(0, 0, HALF, S)
+        for i in range(1, PACK):
             gather(0, i)
         x_round(0, 0, 2, 0, PACK)
         for i in range(PACK - 1):
@@ -256,9 +281,8 @@ def tile_list_hboth_l_gelu_kernel(
         gather(1, PACK - 1, HALF, S)
         x_round(1, 0, 1, 0, 2)
         x_round(1, 0, 1, 2, PACK)
-        x_round(1, 1, 2, 0, PACK)
-        x_quantize_first(0, "plane13")
-        x_quantize_first(1, None)
+        x_quantize(0, 0, 2, "plane13")
+        x_quantize(1, 0, 1, None)
         down_round(nc.scalar.copy, 0, 2, PACK, FIRST_ON_VECTOR, P)
         down_round(nc.vector.tensor_copy, 0, 0, 2, 0, P)
         down_round(nc.vector.tensor_copy, 0, 2, PACK, 0, FIRST_ON_VECTOR)
@@ -268,35 +292,33 @@ def tile_list_hboth_l_gelu_kernel(
         h_acc = [bank("a"), bank("b")]
         h_pass(h_acc[0], 0, 0)
         h_pass(h_acc[1], 1, 0)
-        down_round(nc.scalar.copy, 1, 2, PACK, LAST_ON_VECTOR, P)
-        down_round(nc.vector.tensor_copy, 1, 0, 2, 0, P)
-        down_round(nc.vector.tensor_copy, 1, 2, PACK, 0, LAST_ON_VECTOR)
+        down_round(nc.scalar.copy, 1, 0, PACK, SECOND_ON_VECTOR, P // 2)
+        down_round(nc.vector.tensor_copy, 1, 0, PACK, 0, SECOND_ON_VECTOR)
+        down_round(nc.scalar.copy, 2, 2, PACK, LAST_ON_VECTOR, P // 2)
+        down_round(nc.vector.tensor_copy, 2, 0, 2, 0, P // 2)
+        down_round(nc.vector.tensor_copy, 2, 2, PACK, 0, LAST_ON_VECTOR)
         d_codes[1] = sb("d_codes1", [P, R], U32)
         down_quantize(1, 0, 2)
         down_quantize(1, 2, PACK)
         h_pass(h_acc[0], 0, 1)
         h_pass(h_acc[1], 1, 1, order=(2, 3, 0, 1))
-        up_chunk(0, on_vector=P + 32)
+        x_second = sb("x_second", [P, HALF, PACK], BF16, tag="down_raw2")
+        interleave(nc.scalar.copy, x_second[:], picked[1][:, :, HALF:S])
+        up_chunk(0, on_vector=2 * P)
         h_first = [sb(f"h_bf{v}", [P, QUARTER, PACK], BF16)[:] for v in range(2)]
         h_round(h_first[0], h_acc[0])
         h_round(h_first[1], h_acc[1])
         h_quantize(0, QUARTER, h_first[0])
-        x_second = sb("x_second", [P, PASSES, HALF], U32, tag="h_bf0")
-        x_codes[0, 1], x_codes[1, 1] = x_second[:, 0, :], x_second[:, 1, :]
-        quantize(
-            x_second[:].rearrange("p a c -> p (a c)"),
-            x_sc[:, 1].rearrange("p a c -> p (a c)"),
-            x_bf[:, 1].rearrange("p a c t -> p (a c t)"),
-        )
         h_quantize(QUARTER, HALF, h_first[1])
-        first_act = y_tile(0, 0, QUARTER, "c")
-        y_tile(1, 0, QUARTER, "d")
+        x_codes[1, 1] = sb("x_codes11", [P, HALF], U32)[:]
+        quantize(x_codes[1, 1], x_sc[:, 1, 1, :], x_second[:].rearrange("p c t -> p (c t)"))
+        up_chunk(1, on_vector=2 * P, tag="h_bf0")
+        first_act = y_tile(0, 0, QUARTER, "ring")
+        y_tile(1, 0, QUARTER, "ring")
         y_tile(0, QUARTER, HALF, "a")
-        up_chunk(1)
-        behind_up = sb("behind_up", [P, QUARTER + S], F32, tag="up_raw1")
-        y_tile(1, QUARTER, HALF, "b", act=behind_up[:, 0:QUARTER])
-        h_second = behind_up[:, QUARTER : QUARTER + S].bitcast(BF16).rearrange("p (n t) -> p n t", t=PACK)
-        for q, tag in [(2, "c"), (3, "d")]:
+        y_tile(1, QUARTER, HALF, "b")
+        h_second = sb("h_second", [P, HALF, PACK], BF16)[:]
+        for q, tag in [(2, "a"), (3, "b")]:
             acc = bank(tag)
             h_pass(acc, q, 0)
             h_pass(acc, q, 1)
@@ -306,7 +328,7 @@ def tile_list_hboth_l_gelu_kernel(
         def store(n):
             nc.sync.dma_start(out[n * P : (n + 1) * P, :], outs[n][:])
 
-        act2 = y_tile(2, 0, HALF, "ring")
+        y_tile(2, 0, HALF, "ring")
         y_tile(3, 0, HALF, "ring")
         y_tile(0, HALF, S, "ring", act_tag="act2_0")
         store(0)

@@ -95,11 +95,14 @@ def tile_list_hboth_l_gelu_kernel(
             n0, width = UP_CHUNKS[c]
             nc.sync.dma_start(up_wide[c][:], rows[:, :, n0 - up_at[c] : n0 - up_at[c] + width + EXTRA])
 
-        def load_w4(c):
+        def load_scales(c):
             n0, width = W4_CHUNKS[c]
             for r in range(4):
                 rows = w4_scales.rearrange("a (q r) n -> r q a n", r=4)[r][:, :, n0 : n0 + width]
                 nc.sync.dma_start(w4_sc[c][r:P:32, :, :].bitcast(I32), rows.bitcast(I32))
+
+        def load_w4(c):
+            n0, width = W4_CHUNKS[c]
             src = w4_words[:, :, 2 * n0 : 2 * (n0 + width) + (0 if c else 8 * EXTRA)].rearrange("a p n -> p a n")
             nc.sync.dma_start(w4_codes[c][:].bitcast(I32), src.bitcast(I32))
 
@@ -110,6 +113,7 @@ def tile_list_hboth_l_gelu_kernel(
         nc.sync.dma_start(b_rows[P - SMALL : P - ROW_TILES, :], wgo.rearrange("(g d) (c n) -> d g c n", d=GROUP, n=P)[0])
         for i in range(1, PACK):
             load_plane(0, i)
+        load_scales(0)
         load_plane(1, 0)
         load_plane(1, 1)
         load_plane(1, 2)
@@ -121,6 +125,7 @@ def tile_list_hboth_l_gelu_kernel(
         load_up(1)
         load_w4(0)
         nc.sync.dma_start(place[:], offs2)
+        load_scales(1)
         load_w4(1)
         load_up(2)
         load_up(3)

@@ -18,7 +18,6 @@ MULT = mybir.AluOpType.mult
 GELU = mybir.ActivationFunctionType.Gelu_apprx_tanh
 
 P = 128
-EXTRA = 0
 PACK = 4
 K_PASS = P * PACK
 PASSES = K // K_PASS
@@ -35,7 +34,8 @@ W4_CHUNKS = [(0, W4_SPLIT), (W4_SPLIT, M - W4_SPLIT)]
 FIRST_ON_VECTOR = 24
 DOWN_PIECES = [(0, 0, P), (1, 0, P // 2), (1, P // 2, P)]
 SECOND_ON_VECTOR = 16
-LAST_ON_VECTOR = 24
+LAST_ON_VECTOR = 44
+X_SECOND_AT = 3 * HALF + PACK * LAST_ON_VECTOR - S
 
 
 def tile_list_hboth_l_gelu_kernel(
@@ -61,12 +61,11 @@ def tile_list_hboth_l_gelu_kernel(
         wgo_turned = sb("wgo_turned", [P, S], F32)
         wgo_sb = sb("wgo_sb", [P, S], F32)
         planes = [[sb(f"plane{a}{i}", [P, T], F32) for i in range(PACK)] for a in range(PASSES)]
-        down_wide = [sb(f"down_raw{c}", [P, PACK, PACK * (m1 - m0) + (EXTRA if c else 0)], F32) for c, (a, m0, m1) in enumerate(DOWN_PIECES)]
-        down_raw = [down_wide[0][:], down_wide[1][:, :, 0 : 2 * P], down_wide[2][:, :, EXTRA : EXTRA + 2 * P]]
-        up_wide = [sb(f"up_raw{c}", [P, PACK, width + EXTRA], F32) for c, (n0, width) in enumerate(UP_CHUNKS)]
-        up_at = [EXTRA if c else 0 for c in range(4)]
-        up_raw = [up_wide[c][:, :, up_at[c] : up_at[c] + width] for c, (n0, width) in enumerate(UP_CHUNKS)]
-        w4_codes = [sb(f"w4_codes{c}", [P, PASSES, 2 * width + (0 if c else 8 * EXTRA)], U8) for c, (n0, width) in enumerate(W4_CHUNKS)]
+        down_raw = [sb(f"down_raw{c}", [P, PACK, PACK * (m1 - m0)], F32)[:] for c, (a, m0, m1) in enumerate(DOWN_PIECES[:2])]
+        last_piece = sb("last_piece", [P, 2 * S + X_SECOND_AT], F32)
+        down_raw.append(last_piece[:, 0 : 2 * S].rearrange("p (j r) -> p j r", j=PACK))
+        up_raw = [sb(f"up_raw{c}", [P, PACK, width], F32)[:] for c, (n0, width) in enumerate(UP_CHUNKS)]
+        w4_codes = [sb(f"w4_codes{c}", [P, PASSES, 2 * width], U8) for c, (n0, width) in enumerate(W4_CHUNKS)]
         w4_sc = [sb(f"w4_sc{c}", [P, PASSES, width], U8) for c, (n0, width) in enumerate(W4_CHUNKS)]
         b_rows = sb("b_rows", [P, P], F32)
         bias = sb("bias", [P, ROW_TILES], F32)
@@ -88,12 +87,12 @@ def tile_list_hboth_l_gelu_kernel(
         def load_down(c):
             a, m0, m1 = DOWN_PIECES[c]
             rows = down[a * K_PASS : (a + 1) * K_PASS, :].rearrange("(p j) r -> p j r", j=PACK)
-            nc.sync.dma_start(down_wide[c][:], rows[:, :, PACK * m0 - (EXTRA if c == 2 else 0) : PACK * m1 + (EXTRA if c == 1 else 0)])
+            nc.sync.dma_start(down_raw[c], rows[:, :, PACK * m0 : PACK * m1])
 
         def load_up(c):
             rows = up.rearrange("(p j) n -> p j n", j=PACK)
             n0, width = UP_CHUNKS[c]
-            nc.sync.dma_start(up_wide[c][:], rows[:, :, n0 - up_at[c] : n0 - up_at[c] + width + EXTRA])
+            nc.sync.dma_start(up_raw[c], rows[:, :, n0 : n0 + width])
 
         def load_scales(c):
             n0, width = W4_CHUNKS[c]
@@ -103,7 +102,7 @@ def tile_list_hboth_l_gelu_kernel(
 
         def load_w4(c):
             n0, width = W4_CHUNKS[c]
-            src = w4_words[:, :, 2 * n0 : 2 * (n0 + width) + (0 if c else 8 * EXTRA)].rearrange("a p n -> p a n")
+            src = w4_words[:, :, 2 * n0 : 2 * (n0 + width)].rearrange("a p n -> p a n")
             nc.sync.dma_start(w4_codes[c][:].bitcast(I32), src.bitcast(I32))
 
         nc.sync.dma_start(wgt_rows[:], wgt.rearrange("(g d) (c k) -> d g c k", d=GROUP, k=BLOCK)[0])
@@ -166,9 +165,9 @@ def tile_list_hboth_l_gelu_kernel(
         x_bf = sb("x_bf", [P, PASSES, 2, HALF, PACK], BF16)
         x_codes = {}
 
-        def gather(a, i, j0=0, j1=S, weights=None):
+        def gather(a, i, j0=0, j1=S):
             window = planes[a][i][:].indirect(pick[:, j0 // GROUP : j1 // GROUP])
-            nc.vector.tensor_tensor(picked[a][:, i, j0:j1], window, wgt_sb[:, j0:j1] if weights is None else weights, MULT)
+            nc.vector.tensor_tensor(picked[a][:, i, j0:j1], window, wgt_sb[:, j0:j1], MULT)
 
         def x_round(a, h0, h1, i0, i1):
             nc.scalar.copy(
@@ -243,7 +242,7 @@ def tile_list_hboth_l_gelu_kernel(
         def h_quantize(j0, j1, rounded):
             quantize(h_codes[:, j0:j1], h_sc[:, j0:j1], rounded.rearrange("p n t -> p (n t)"))
 
-        def y_tile(n, j0, j1, bank_tag, act_tag=None, act=None):
+        def y_tile(n, j0, j1, bank_tag, act_tag=None):
             acc = bank(bank_tag)
             c = 0 if n * P < W4_SPLIT else 1
             first = n * P - W4_CHUNKS[c][0]
@@ -268,12 +267,10 @@ def tile_list_hboth_l_gelu_kernel(
                 start=False,
                 stop=True,
             )
-            if act is None:
-                act = sb(f"act{n}_{j0}", [P, j1 - j0], F32, tag=act_tag)[:]
+            act = sb(f"act{n}_{j0}", [P, j1 - j0], F32, tag=act_tag)[:]
             nc.scalar.activation(act, acc[:, 0 : j1 - j0], GELU, bias=bias[:, n : n + 1])
             window = outs[n][:].indirect(place[:, j0 // GROUP : j1 // GROUP])
             nc.vector.tensor_tensor(window, act, wgo_sb[:, j0:j1], MULT)
-            return act
 
         gather(0, 0, 0, HALF)
         gather(0, 0, HALF, S)
@@ -286,7 +283,7 @@ def tile_list_hboth_l_gelu_kernel(
         gather(1, PACK - 1, HALF, S)
         x_round(1, 0, 1, 0, 2)
         x_round(1, 0, 1, 2, PACK)
-        x_quantize(0, 0, 2, "plane13")
+        x_quantize(0, 0, 1, "plane13")
         x_quantize(1, 0, 1, None)
         down_round(nc.scalar.copy, 0, 2, PACK, FIRST_ON_VECTOR, P)
         down_round(nc.vector.tensor_copy, 0, 0, 2, 0, P)
@@ -299,26 +296,27 @@ def tile_list_hboth_l_gelu_kernel(
         h_pass(h_acc[1], 1, 0)
         down_round(nc.scalar.copy, 1, 0, PACK, SECOND_ON_VECTOR, P // 2)
         down_round(nc.vector.tensor_copy, 1, 0, PACK, 0, SECOND_ON_VECTOR)
-        down_round(nc.scalar.copy, 2, 2, PACK, LAST_ON_VECTOR, P // 2)
-        down_round(nc.vector.tensor_copy, 2, 0, 2, 0, P // 2)
+        down_round(nc.scalar.copy, 2, 0, PACK, LAST_ON_VECTOR, P // 2)
+        down_round(nc.vector.tensor_copy, 2, 0, 2, 0, LAST_ON_VECTOR)
         down_round(nc.vector.tensor_copy, 2, 2, PACK, 0, LAST_ON_VECTOR)
         d_codes[1] = sb("d_codes1", [P, R], U32)
         down_quantize(1, 0, 2)
         down_quantize(1, 2, PACK)
+        x_quantize(0, 1, 2, "d_bf1")
         h_pass(h_acc[0], 0, 1)
         h_pass(h_acc[1], 1, 1, order=(2, 3, 0, 1))
-        x_second = sb("x_second", [P, HALF, PACK], BF16, tag="down_raw2")
-        interleave(nc.scalar.copy, x_second[:], picked[1][:, :, HALF:S])
-        up_chunk(0, on_vector=2 * P)
+        x_second = last_piece[:, S + X_SECOND_AT : 2 * S + X_SECOND_AT].bitcast(BF16).rearrange("p (c t) -> p c t", t=PACK)
+        interleave(nc.scalar.copy, x_second, picked[1][:, :, HALF:S])
+        up_chunk(0, on_vector=160)
         h_first = [sb(f"h_bf{v}", [P, QUARTER, PACK], BF16)[:] for v in range(2)]
         h_round(h_first[0], h_acc[0])
         h_round(h_first[1], h_acc[1])
         h_quantize(0, QUARTER, h_first[0])
         h_quantize(QUARTER, HALF, h_first[1])
         x_codes[1, 1] = sb("x_codes11", [P, HALF], U32)[:]
-        quantize(x_codes[1, 1], x_sc[:, 1, 1, :], x_second[:].rearrange("p c t -> p (c t)"))
-        up_chunk(1, on_vector=2 * P, tag="h_bf0")
-        first_act = y_tile(0, 0, QUARTER, "ring")
+        quantize(x_codes[1, 1], x_sc[:, 1, 1, :], x_second.rearrange("p c t -> p (c t)"))
+        up_chunk(1, on_vector=160, tag="h_bf0")
+        y_tile(0, 0, QUARTER, "ring")
         y_tile(1, 0, QUARTER, "ring")
         y_tile(0, QUARTER, HALF, "a")
         y_tile(1, QUARTER, HALF, "b")

@@ -35,6 +35,7 @@ FIRST_ON_VECTOR = 24
 DOWN_PIECES = [(0, 0, P), (1, 0, P // 2), (1, P // 2, P)]
 SECOND_ON_VECTOR = 16
 LAST_ON_VECTOR = 44
+UP_ON_SCALAR = 96
 X_SECOND_AT = 3 * HALF + PACK * LAST_ON_VECTOR - S
 
 
@@ -64,7 +65,8 @@ def tile_list_hboth_l_gelu_kernel(
         down_raw = [sb(f"down_raw{c}", [P, PACK, PACK * (m1 - m0)], F32)[:] for c, (a, m0, m1) in enumerate(DOWN_PIECES[:2])]
         last_piece = sb("last_piece", [P, 2 * S + X_SECOND_AT], F32)
         down_raw.append(last_piece[:, 0 : 2 * S].rearrange("p (j r) -> p j r", j=PACK))
-        up_raw = [sb(f"up_raw{c}", [P, PACK, width], F32)[:] for c, (n0, width) in enumerate(UP_CHUNKS)]
+        up_rows = [sb(f"up_raw{c}", [P, PACK * width + (QUARTER - UP_ON_SCALAR if c == 1 else 0)], F32) for c, (n0, width) in enumerate(UP_CHUNKS)]
+        up_raw = [rows[:, 0 : 2 * S].rearrange("p (j n) -> p j n", j=PACK) for rows in up_rows]
         w4_codes = [sb(f"w4_codes{c}", [P, PASSES, 2 * width], U8) for c, (n0, width) in enumerate(W4_CHUNKS)]
         w4_sc = [sb(f"w4_sc{c}", [P, PASSES, width], U8) for c, (n0, width) in enumerate(W4_CHUNKS)]
         b_rows = sb("b_rows", [P, P], F32)
@@ -106,8 +108,8 @@ def tile_list_hboth_l_gelu_kernel(
             nc.sync.dma_start(w4_codes[c][:].bitcast(I32), src.bitcast(I32))
 
         nc.sync.dma_start(wgt_rows[:], wgt.rearrange("(g d) (c k) -> d g c k", d=GROUP, k=BLOCK)[0])
-        nc.sync.dma_start(pick[:], offs)
         load_plane(0, 0)
+        nc.sync.dma_start(pick[:], offs)
         nc.sync.dma_start(b_rows[P - ROW_TILES : P, :], b.rearrange("(c p) -> c p", p=P))
         nc.sync.dma_start(b_rows[P - SMALL : P - ROW_TILES, :], wgo.rearrange("(g d) (c n) -> d g c n", d=GROUP, n=P)[0])
         for i in range(1, PACK):
@@ -121,8 +123,8 @@ def tile_list_hboth_l_gelu_kernel(
         load_down(1)
         load_down(2)
         load_up(0)
-        load_up(1)
         load_w4(0)
+        load_up(1)
         nc.sync.dma_start(place[:], offs2)
         load_scales(1)
         load_w4(1)
@@ -242,7 +244,7 @@ def tile_list_hboth_l_gelu_kernel(
         def h_quantize(j0, j1, rounded):
             quantize(h_codes[:, j0:j1], h_sc[:, j0:j1], rounded.rearrange("p n t -> p (n t)"))
 
-        def y_tile(n, j0, j1, bank_tag, act_tag=None):
+        def y_tile(n, j0, j1, bank_tag, act_tag=None, act=None):
             acc = bank(bank_tag)
             c = 0 if n * P < W4_SPLIT else 1
             first = n * P - W4_CHUNKS[c][0]
@@ -267,7 +269,8 @@ def tile_list_hboth_l_gelu_kernel(
                 start=False,
                 stop=True,
             )
-            act = sb(f"act{n}_{j0}", [P, j1 - j0], F32, tag=act_tag)[:]
+            if act is None:
+                act = sb(f"act{n}_{j0}", [P, j1 - j0], F32, tag=act_tag)[:]
             nc.scalar.activation(act, acc[:, 0 : j1 - j0], GELU, bias=bias[:, n : n + 1])
             window = outs[n][:].indirect(place[:, j0 // GROUP : j1 // GROUP])
             nc.vector.tensor_tensor(window, act, wgo_sb[:, j0:j1], MULT)
@@ -307,7 +310,7 @@ def tile_list_hboth_l_gelu_kernel(
         h_pass(h_acc[1], 1, 1, order=(2, 3, 0, 1))
         x_second = last_piece[:, S + X_SECOND_AT : 2 * S + X_SECOND_AT].bitcast(BF16).rearrange("p (c t) -> p c t", t=PACK)
         interleave(nc.scalar.copy, x_second, picked[1][:, :, HALF:S])
-        up_chunk(0, on_vector=160)
+        up_chunk(0, on_vector=2 * P - UP_ON_SCALAR)
         h_first = [sb(f"h_bf{v}", [P, QUARTER, PACK], BF16)[:] for v in range(2)]
         h_round(h_first[0], h_acc[0])
         h_round(h_first[1], h_acc[1])
@@ -315,8 +318,8 @@ def tile_list_hboth_l_gelu_kernel(
         h_quantize(QUARTER, HALF, h_first[1])
         x_codes[1, 1] = sb("x_codes11", [P, HALF], U32)[:]
         quantize(x_codes[1, 1], x_sc[:, 1, 1, :], x_second.rearrange("p c t -> p (c t)"))
-        up_chunk(1, on_vector=160, tag="h_bf0")
-        y_tile(0, 0, QUARTER, "ring")
+        up_chunk(1, on_vector=2 * P - UP_ON_SCALAR, tag="h_bf0")
+        y_tile(0, 0, QUARTER, "ring", act=up_rows[1][:, 2 * S - UP_ON_SCALAR : 2 * S - UP_ON_SCALAR + QUARTER])
         y_tile(1, 0, QUARTER, "ring")
         y_tile(0, QUARTER, HALF, "a")
         y_tile(1, QUARTER, HALF, "b")

@@ -31,11 +31,11 @@ RING_BANKS = 6
 UP_CHUNKS = [(0, 2 * P), (2 * P, 2 * P), (4 * P, 2 * P), (6 * P, 2 * P)]
 W4_SPLIT = 2 * P
 W4_CHUNKS = [(0, W4_SPLIT), (W4_SPLIT, M - W4_SPLIT)]
-FIRST_ON_VECTOR = 24
 DOWN_PIECES = [(0, 0, P), (1, 0, P // 2), (1, P // 2, P)]
-SECOND_ON_VECTOR = 16
+SECOND_ON_VECTOR = 8
 LAST_ON_VECTOR = 44
-UP_ON_SCALAR = 96
+UP_ON_SCALAR = 64
+FIRST_UP_ON_SCALAR = 80
 X_SECOND_AT = 3 * HALF + PACK * LAST_ON_VECTOR - S
 
 
@@ -55,7 +55,8 @@ def tile_list_hboth_l_gelu_kernel(
 
         pick = keep.tile([P, S // GROUP], U16, name="pick")
         place = keep.tile([P, S // GROUP], U16, name="place")
-        wgt_sb = sb("wgt_sb", [P, S], F32)
+        second_rows = sb("second_rows", [P, PACK * (S + HALF)], F32)
+        wgt_sb = second_rows[:, 2 * (S + HALF) + HALF : 3 * (S + HALF)]
         wgt_rows = sb("wgt_rows", [P, BLOCK], F32)
         wgt_turned = sb("wgt_turned", [P, BLOCK], F32)
         wgt_spread = sb("wgt_spread", [P, S], F32)
@@ -162,7 +163,7 @@ def tile_list_hboth_l_gelu_kernel(
         def quantize(codes, scales, rounded):
             nc.vector.quantize_mx(out=codes.bitcast(FP8X4), scales=scales, in_=rounded)
 
-        picked = [sb(f"picked{a}", [P, PACK, S], F32) for a in range(PASSES)]
+        picked = [sb("picked0", [P, PACK, S], F32)[:], second_rows[:].rearrange("p (i j) -> p i j", i=PACK)[:, :, 0:S]]
         x_sc = sb("x_sc", [P, PASSES, 2, HALF], U8)
         x_bf = sb("x_bf", [P, PASSES, 2, HALF, PACK], BF16)
         x_codes = {}
@@ -280,17 +281,16 @@ def tile_list_hboth_l_gelu_kernel(
         for i in range(1, PACK):
             gather(0, i)
         x_round(0, 0, 2, 0, PACK)
-        for i in range(PACK - 1):
+        for i in range(2):
             gather(1, i)
-        gather(1, PACK - 1, 0, HALF)
-        gather(1, PACK - 1, HALF, S)
-        x_round(1, 0, 1, 0, 2)
-        x_round(1, 0, 1, 2, PACK)
+        for j0 in (0, HALF):
+            for i in range(2, PACK):
+                gather(1, i, j0, j0 + HALF)
+        x_round(1, 0, 1, 0, PACK)
         x_quantize(0, 0, 1, "plane13")
         x_quantize(1, 0, 1, None)
-        down_round(nc.scalar.copy, 0, 2, PACK, FIRST_ON_VECTOR, P)
+        down_round(nc.scalar.copy, 0, 2, PACK, 0, P)
         down_round(nc.vector.tensor_copy, 0, 0, 2, 0, P)
-        down_round(nc.vector.tensor_copy, 0, 2, PACK, 0, FIRST_ON_VECTOR)
         d_codes[0] = sb("d_codes0", [P, R], U32)
         down_quantize(0, 0, 2)
         down_quantize(0, 2, PACK)
@@ -310,17 +310,17 @@ def tile_list_hboth_l_gelu_kernel(
         h_pass(h_acc[1], 1, 1, order=(2, 3, 0, 1))
         x_second = last_piece[:, S + X_SECOND_AT : 2 * S + X_SECOND_AT].bitcast(BF16).rearrange("p (c t) -> p c t", t=PACK)
         interleave(nc.scalar.copy, x_second, picked[1][:, :, HALF:S])
-        up_chunk(0, on_vector=2 * P - UP_ON_SCALAR)
+        up_chunk(0, on_vector=2 * P - FIRST_UP_ON_SCALAR)
+        x_codes[1, 1] = sb("x_codes11", [P, HALF], U32)[:]
+        quantize(x_codes[1, 1], x_sc[:, 1, 1, :], x_second.rearrange("p c t -> p (c t)"))
         h_first = [sb(f"h_bf{v}", [P, QUARTER, PACK], BF16)[:] for v in range(2)]
         h_round(h_first[0], h_acc[0])
         h_round(h_first[1], h_acc[1])
         h_quantize(0, QUARTER, h_first[0])
         h_quantize(QUARTER, HALF, h_first[1])
-        x_codes[1, 1] = sb("x_codes11", [P, HALF], U32)[:]
-        quantize(x_codes[1, 1], x_sc[:, 1, 1, :], x_second.rearrange("p c t -> p (c t)"))
-        up_chunk(1, on_vector=2 * P - UP_ON_SCALAR, tag="h_bf0")
-        y_tile(0, 0, QUARTER, "ring", act=up_rows[1][:, 2 * S - UP_ON_SCALAR : 2 * S - UP_ON_SCALAR + QUARTER])
-        y_tile(1, 0, QUARTER, "ring")
+        up_chunk(1, on_vector=2 * P - UP_ON_SCALAR, tag="u_bf0")
+        y_tile(0, 0, QUARTER, "ring")
+        y_tile(1, 0, QUARTER, "ring", act=up_rows[1][:, 2 * S - UP_ON_SCALAR : 2 * S - UP_ON_SCALAR + QUARTER])
         y_tile(0, QUARTER, HALF, "a")
         y_tile(1, QUARTER, HALF, "b")
         h_second = sb("h_second", [P, HALF, PACK], BF16)[:]

from contextlib import ExitStack

import concourse.mybir as mybir
from concourse.masks import make_identity

K, M, T, S, R = 1024, 1024, 1024, 512, 512
FLOPS = 2 * S * (K * R + K * M + R * M)

F32 = mybir.dt.float32
BF16 = mybir.dt.bfloat16
I32 = mybir.dt.int32
U32 = mybir.dt.uint32
U16 = mybir.dt.uint16
U8 = mybir.dt.uint8
FP8X4 = mybir.dt.float8_e4m3fn_x4
FP4X4 = mybir.dt.float4_e2m1fn_x4
MULT = mybir.AluOpType.mult
GELU = mybir.ActivationFunctionType.Gelu_apprx_tanh

P = 128
PACK = 4
K_PASS = P * PACK
PASSES = K // K_PASS
HALF = S // 2
QUARTER = S // 4
GROUP = 16
BLOCK = 32
SMALL = 40
ROW_TILES = M // P
RING_BANKS = 6
UP_CHUNKS = [(0, 2 * P), (2 * P, 2 * P), (4 * P, 2 * P), (6 * P, 2 * P)]
W4_SPLIT = 2 * P
W4_CHUNKS = [(0, W4_SPLIT), (W4_SPLIT, M - W4_SPLIT)]
DOWN_PIECES = [(0, 0, P), (1, 0, P // 2), (1, P // 2, P)]
SECOND_ON_VECTOR = 8
LAST_ON_VECTOR = 44
UP_ON_SCALAR = 64
FIRST_UP_ON_SCALAR = 80
X_SECOND_AT = 3 * HALF + PACK * LAST_ON_VECTOR - S


def tile_list_hboth_l_gelu_kernel(
    tc, xT, w4_words, w4_scales, down, up, wgt, b, wgo, offs, offs2, out
):
    nc = tc.nc
    with ExitStack() as ctx:
        keep = ctx.enter_context(tc.tile_pool(name="keep", bufs=1))
        psum = ctx.enter_context(tc.psum_pool(name="psum", bufs=1))

        def sb(name, shape, dtype, tag=None):
            return keep.tile(shape, dtype, name=name, tag=tag or name, align_bytes=64)

        def bank(tag):
            return psum.tile([P, S], F32, name=tag, tag=tag, bufs=RING_BANKS if tag == "ring" else 1)

        pick = keep.tile([P, S // GROUP], U16, name="pick")
        place = keep.tile([P, S // GROUP], U16, name="place")
        second_rows = sb("second_rows", [P, PACK * (S + HALF)], F32)
        wgt_sb = second_rows[:, 2 * (S + HALF) + HALF : 3 * (S + HALF)]
        wgt_rows = sb("wgt_rows", [P, BLOCK], F32)
        wgt_turned = sb("wgt_turned", [P, BLOCK], F32)
        wgt_spread = sb("wgt_spread", [P, S], F32)
        wgo_turned = sb("wgo_turned", [P, S], F32)
        wgo_sb = sb("wgo_sb", [P, S], F32)
        planes = [[sb(f"plane{a}{i}", [P, T], F32) for i in range(PACK)] for a in range(PASSES)]
        down_raw = [sb(f"down_raw{c}", [P, PACK, PACK * (m1 - m0)], F32)[:] for c, (a, m0, m1) in enumerate(DOWN_PIECES[:2])]
        last_piece = sb("last_piece", [P, 2 * S + X_SECOND_AT], F32)
        down_raw.append(last_piece[:, 0 : 2 * S].rearrange("p (j r) -> p j r", j=PACK))
        up_rows = [sb(f"up_raw{c}", [P, PACK * width + (QUARTER - UP_ON_SCALAR if c == 1 else 0)], F32) for c, (n0, width) in enumerate(UP_CHUNKS)]
        up_raw = [rows[:, 0 : 2 * S].rearrange("p (j n) -> p j n", j=PACK) for rows in up_rows]
        w4_codes = [sb(f"w4_codes{c}", [P, PASSES, 2 * width], U8) for c, (n0, width) in enumerate(W4_CHUNKS)]
        w4_sc = [sb(f"w4_sc{c}", [P, PASSES, width], U8) for c, (n0, width) in enumerate(W4_CHUNKS)]
        b_rows = sb("b_rows", [P, P], F32)
        bias = sb("bias", [P, ROW_TILES], F32)
        ident = sb("ident", [P, P], F32)
        outs = [sb(f"out{n}", [P, T], F32) for n in range(ROW_TILES)]

        nc.gpsimd.memset(b_rows[0 : P - SMALL, :], 0.0)
        make_identity(nc, ident[:])
        nc.scalar.activation(bias[0:64, 0:1], b_rows[0:64, 0:1], GELU)
        for scales in w4_sc:
            nc.gpsimd.memset(scales[:].rearrange("p a n -> p (a n)").bitcast(U32), 0)
        for n in range(ROW_TILES):
            nc.gpsimd.memset(outs[n][:].bitcast(I32), 0)

        def load_plane(a, i):
            rows = xT[a * K_PASS : (a + 1) * K_PASS, :].rearrange("(p i) t -> p i t", i=PACK)
            nc.sync.dma_start(planes[a][i][:], rows[:, i, :])

        def load_down(c):
            a, m0, m1 = DOWN_PIECES[c]
            rows = down[a * K_PASS : (a + 1) * K_PASS, :].rearrange("(p j) r -> p j r", j=PACK)
            nc.sync.dma_start(down_raw[c], rows[:, :, PACK * m0 : PACK * m1])

        def load_up(c):
            rows = up.rearrange("(p j) n -> p j n", j=PACK)
            n0, width = UP_CHUNKS[c]
            nc.sync.dma_start(up_raw[c], rows[:, :, n0 : n0 + width])

        def load_scales(c):
            n0, width = W4_CHUNKS[c]
            for r in range(4):
                rows = w4_scales.rearrange("a (q r) n -> r q a n", r=4)[r][:, :, n0 : n0 + width]
                nc.sync.dma_start(w4_sc[c][r:P:32, :, :].bitcast(I32), rows.bitcast(I32))

        def load_w4(c):
            n0, width = W4_CHUNKS[c]
            src = w4_words[:, :, 2 * n0 : 2 * (n0 + width)].rearrange("a p n -> p a n")
            nc.sync.dma_start(w4_codes[c][:].bitcast(I32), src.bitcast(I32))

        nc.sync.dma_start(wgt_rows[:], wgt.rearrange("(g d) (c k) -> d g c k", d=GROUP, k=BLOCK)[0])
        load_plane(0, 0)
        nc.sync.dma_start(pick[:], offs)
        nc.sync.dma_start(b_rows[P - ROW_TILES : P, :], b.rearrange("(c p) -> c p", p=P))
        nc.sync.dma_start(b_rows[P - SMALL : P - ROW_TILES, :], wgo.rearrange("(g d) (c n) -> d g c n", d=GROUP, n=P)[0])
        for i in range(1, PACK):
            load_plane(0, i)
        load_scales(0)
        load_plane(1, 0)
        load_plane(1, 1)
        load_plane(1, 2)
        load_plane(1, 3)
        load_down(0)
        load_down(1)
        load_down(2)
        load_up(0)
        load_w4(0)
        load_up(1)
        nc.sync.dma_start(place[:], offs2)
        load_scales(1)
        load_w4(1)
        load_up(2)
        load_up(3)

        nc.vector.transpose(wgt_turned[:], wgt_rows[:])
        for h in range(2):
            source = wgt_turned[:].rearrange("p (e c) -> p c e", e=2)[:, 8 * h : 8 * h + 8, :]
            source = source.unsqueeze(3).to_broadcast([P, 8, 2, GROUP])
            spread = wgt_spread[:, h * HALF : (h + 1) * HALF].rearrange("p (c e d) -> p c e d", e=2, d=GROUP)
            nc.vector.tensor_tensor(spread, source, source, mybir.AluOpType.max)
        for h in range(2):
            cols = slice(h * HALF, (h + 1) * HALF)
            nc.vector.transpose(wgt_sb[:, cols], wgt_spread[:, cols])

        turned = bank("a")
        nc.tensor.transpose(turned[:, 0:P], b_rows[:], ident[:])
        nc.scalar.copy(bias[:], turned[:, P - ROW_TILES : P])
        nc.scalar.copy(
            wgo_turned[:].rearrange("p (c g d) -> p c g d", c=4, d=GROUP),
            turned[:, P - SMALL : P - ROW_TILES].rearrange("p (g c) -> p c g", c=4).unsqueeze(3).to_broadcast([P, 4, 8, GROUP]),
        )
        back = bank("b")
        for c in range(4):
            nc.tensor.transpose(back[:, c * P : (c + 1) * P], wgo_turned[:, c * P : (c + 1) * P], ident[:])
        nc.scalar.copy(wgo_sb[:], back[:])

        def interleave(copy, dst, src):
            copy(
                dst.rearrange("p (c e) t -> p c t e", e=4),
                src.rearrange("p t (c e) -> p c t e", e=4),
            )

        def quantize(codes, scales, rounded):
            nc.vector.quantize_mx(out=codes.bitcast(FP8X4), scales=scales, in_=rounded)

        picked = [sb("picked0", [P, PACK, S], F32)[:], second_rows[:].rearrange("p (i j) -> p i j", i=PACK)[:, :, 0:S]]
        x_sc = sb("x_sc", [P, PASSES, 2, HALF], U8)
        x_bf = sb("x_bf", [P, PASSES, 2, HALF, PACK], BF16)
        x_codes = {}

        def gather(a, i, j0=0, j1=S):
            window = planes[a][i][:].indirect(pick[:, j0 // GROUP : j1 // GROUP])
            nc.vector.tensor_tensor(picked[a][:, i, j0:j1], window, wgt_sb[:, j0:j1], MULT)

        def x_round(a, h0, h1, i0, i1):
            nc.scalar.copy(
                x_bf[:, a, h0:h1, :, i0:i1].rearrange("p h (c e) t -> p h c t e", e=4),
                picked[a][:, i0:i1, h0 * HALF : h1 * HALF].rearrange("p t (h c e) -> p h c t e", c=HALF // 4, e=4),
            )

        def x_words(a, j):
            return x_codes[a, j // HALF][:, j % HALF : j % HALF + QUARTER].bitcast(FP8X4)

        def x_scales(a, j):
            return x_sc[:, a, j // HALF, j % HALF : j % HALF + QUARTER]

        def x_quantize(a, h0, h1, tag):
            codes = sb(f"x_codes{a}{h0}", [P, h1 - h0, HALF], U32, tag=tag)
            for h in range(h0, h1):
                x_codes[a, h] = codes[:, h - h0, :]
            quantize(
                codes[:].rearrange("p h c -> p (h c)"),
                x_sc[:, a, h0:h1].rearrange("p h c -> p (h c)"),
                x_bf[:, a, h0:h1].rearrange("p h c t -> p (h c t)"),
            )

        d_codes = {}
        d_sc = sb("d_sc", [P, PASSES, R], U8)
        d_bf = [sb(f"d_bf{a}", [P, PACK, P, PACK], BF16) for a in range(PASSES)]

        def down_round(copy, c, t0, t1, m0, m1):
            a, first, last = DOWN_PIECES[c]
            copy(
                d_bf[a][:, t0:t1, first + m0 : first + m1, :].rearrange("p t m j -> p m j t"),
                down_raw[c].rearrange("p j (m t) -> p m j t", t=PACK)[:, m0:m1, :, t0:t1],
            )

        def down_quantize(a, t0, t1):
            m = slice(t0 * P, t1 * P)
            quantize(d_codes[a][:, m], d_sc[:, a, m], d_bf[a][:, t0:t1].rearrange("p t m j -> p (t m j)"))

        u_codes = sb("u_codes", [P, M], U32)
        u_sc = sb("u_sc", [P, M], U8)

        def up_chunk(c, on_vector=0, tag=None):
            n0, width = UP_CHUNKS[c]
            cols = slice(n0, n0 + width)
            rounded = sb(f"u_bf{c}", [P, width, PACK], BF16, tag=tag)
            if on_vector < width:
                interleave(nc.scalar.copy, rounded[:, on_vector:width, :], up_raw[c][:, :, on_vector:width])
            if on_vector:
                interleave(nc.vector.tensor_copy, rounded[:, 0:on_vector, :], up_raw[c][:, :, 0:on_vector])
            quantize(u_codes[:, cols], u_sc[:, cols], rounded[:].rearrange("p n t -> p (n t)"))

        h_codes = sb("h_codes", [P, S], U32)
        h_sc = sb("h_sc", [P, S], U8)

        def h_pass(acc, q, a, order=(0, 1, 2, 3)):
            cols = slice(q * QUARTER, (q + 1) * QUARTER)
            for t in order:
                m = slice(t * P, (t + 1) * P)
                nc.tensor.matmul_mx(
                    out=acc[:, m],
                    lhsT=d_codes[a][:, m].bitcast(FP8X4),
                    lhsT_scale=d_sc[:, a, m],
                    rhs=x_words(a, cols.start),
                    rhs_scale=x_scales(a, cols.start),
                    start=(a == 0 and t == order[0]),
                    stop=(a == PASSES - 1 and t == order[-1]),
                )

        def h_round(dst, acc):
            nc.scalar.copy(dst, acc[:].rearrange("p (t n) -> p n t", t=PACK))

        def h_quantize(j0, j1, rounded):
            quantize(h_codes[:, j0:j1], h_sc[:, j0:j1], rounded.rearrange("p n t -> p (n t)"))

        def y_tile(n, j0, j1, bank_tag, act_tag=None, act=None):
            acc = bank(bank_tag)
            c = 0 if n * P < W4_SPLIT else 1
            first = n * P - W4_CHUNKS[c][0]
            rows = slice(n * P, (n + 1) * P)
            for a in range(PASSES):
                for j in range(j0, j1, QUARTER):
                    nc.tensor.matmul_mx(
                        out=acc[:, j - j0 : j - j0 + QUARTER],
                        lhsT=w4_codes[c][:, a, 2 * first : 2 * (first + P)].bitcast(FP4X4),
                        lhsT_scale=w4_sc[c][:, a, first : first + P],
                        rhs=x_words(a, j),
                        rhs_scale=x_scales(a, j),
                        start=(a == 0 and j == j0),
                        stop=False,
                    )
            nc.tensor.matmul_mx(
                out=acc[:, 0 : j1 - j0],
                lhsT=u_codes[:, rows].bitcast(FP8X4),
                lhsT_scale=u_sc[:, rows],
                rhs=h_codes[:, j0:j1].bitcast(FP8X4),
                rhs_scale=h_sc[:, j0:j1],
                start=False,
                stop=True,
            )
            if act is None:
                act = sb(f"act{n}_{j0}", [P, j1 - j0], F32, tag=act_tag)[:]
            nc.scalar.activation(act, acc[:, 0 : j1 - j0], GELU, bias=bias[:, n : n + 1])
            window = outs[n][:].indirect(place[:, j0 // GROUP : j1 // GROUP])
            nc.vector.tensor_tensor(window, act, wgo_sb[:, j0:j1], MULT)

        gather(0, 0, 0, HALF)
        gather(0, 0, HALF, S)
        for i in range(1, PACK):
            gather(0, i)
        x_round(0, 0, 2, 0, PACK)
        for i in range(2):
            gather(1, i)
        for j0 in (0, HALF):
            for i in range(2, PACK):
                gather(1, i, j0, j0 + HALF)
        x_round(1, 0, 1, 0, PACK)
        x_quantize(0, 0, 1, "plane13")
        x_quantize(1, 0, 1, None)
        down_round(nc.scalar.copy, 0, 2, PACK, 0, P)
        down_round(nc.vector.tensor_copy, 0, 0, 2, 0, P)
        d_codes[0] = sb("d_codes0", [P, R], U32)
        down_quantize(0, 0, 2)
        down_quantize(0, 2, PACK)
        h_acc = [bank("a"), bank("b")]
        h_pass(h_acc[0], 0, 0)
        h_pass(h_acc[1], 1, 0)
        down_round(nc.scalar.copy, 1, 0, PACK, SECOND_ON_VECTOR, P // 2)
        down_round(nc.vector.tensor_copy, 1, 0, PACK, 0, SECOND_ON_VECTOR)
        down_round(nc.scalar.copy, 2, 0, PACK, LAST_ON_VECTOR, P // 2)
        down_round(nc.vector.tensor_copy, 2, 0, 2, 0, LAST_ON_VECTOR)
        down_round(nc.vector.tensor_copy, 2, 2, PACK, 0, LAST_ON_VECTOR)
        d_codes[1] = sb("d_codes1", [P, R], U32)
        down_quantize(1, 0, 2)
        down_quantize(1, 2, PACK)
        x_quantize(0, 1, 2, "d_bf1")
        h_pass(h_acc[0], 0, 1)
        h_pass(h_acc[1], 1, 1, order=(2, 3, 0, 1))
        x_second = last_piece[:, S + X_SECOND_AT : 2 * S + X_SECOND_AT].bitcast(BF16).rearrange("p (c t) -> p c t", t=PACK)
        interleave(nc.scalar.copy, x_second, picked[1][:, :, HALF:S])
        up_chunk(0, on_vector=2 * P - FIRST_UP_ON_SCALAR)
        x_codes[1, 1] = sb("x_codes11", [P, HALF], U32)[:]
        quantize(x_codes[1, 1], x_sc[:, 1, 1, :], x_second.rearrange("p c t -> p (c t)"))
        h_first = [sb(f"h_bf{v}", [P, QUARTER, PACK], BF16)[:] for v in range(2)]
        h_round(h_first[0], h_acc[0])
        h_round(h_first[1], h_acc[1])
        h_quantize(0, QUARTER, h_first[0])
        h_quantize(QUARTER, HALF, h_first[1])
        up_chunk(1, on_vector=2 * P - UP_ON_SCALAR, tag="u_bf0")
        y_tile(0, 0, QUARTER, "ring")
        y_tile(1, 0, QUARTER, "ring", act=up_rows[1][:, 2 * S - UP_ON_SCALAR : 2 * S - UP_ON_SCALAR + QUARTER])
        y_tile(0, QUARTER, HALF, "a")
        y_tile(1, QUARTER, HALF, "b")
        h_second = sb("h_second", [P, HALF, PACK], BF16)[:]
        for q, tag in [(2, "a"), (3, "b")]:
            acc = bank(tag)
            h_pass(acc, q, 0)
            h_pass(acc, q, 1)
            h_round(h_second[:, (q - 2) * QUARTER : (q - 1) * QUARTER, :], acc)
        h_quantize(HALF, S, h_second)

        def store(n):
            nc.sync.dma_start(out[n * P : (n + 1) * P, :], outs[n][:])

        y_tile(2, 0, HALF, "ring")
        y_tile(3, 0, HALF, "ring")
        y_tile(0, HALF, S, "ring", act_tag="act2_0")
        store(0)
        up_chunk(2)
        y_tile(1, HALF, S, "ring", act_tag="up_raw2")
        store(1)
        y_tile(2, HALF, S, "ring", act_tag="act3_0")
        store(2)
        up_chunk(3)
        y_tile(3, HALF, S, "ring", act_tag="up_raw3")
        store(3)
        for n in range(4, ROW_TILES):
            y_tile(n, 0, S, "ring")
            store(n)
